import numpy as np
import ml_dtypes


def mxq(x, axis, fmt="e4m3"):
    dtype, down = {"e4m3": (ml_dtypes.float8_e4m3fn, 7), "e5m2": (ml_dtypes.float8_e5m2, 14)}[fmt]
    v = np.moveaxis(np.asarray(x, np.float32).astype(ml_dtypes.bfloat16).astype(np.float64), axis, -1)
    blocks = v.reshape(v.shape[:-1] + (-1, 32))
    amax = np.abs(blocks).max(-1, keepdims=True)
    byte = np.maximum(np.where(amax > 0, np.frexp(amax)[1] - 1 + 127, 0) - down, 1)
    scale = np.exp2(byte - 127.0)
    codes = (blocks / scale).astype(np.float32).astype(dtype).astype(np.float64)
    return np.moveaxis((codes * scale).reshape(v.shape), -1, axis)


WIDE = False


def mx_kscale(k):
    if not WIDE:
        return np.ones(k)
    levels = np.array([10, -10, 5, -5, 0])
    if k % 512:
        return np.exp2(np.random.permutation(np.resize(levels, k // 32))).repeat(32)
    a = np.empty((k // 512, 16))
    for p in range(k // 512):
        a[p, :8] = np.random.permutation(np.resize(levels, 8))
        for g in range(8):
            far = levels[np.abs(levels - a[p, g]) >= 10]
            a[p, g + 8] = far[np.random.randint(len(far))]
    return np.exp2(a.ravel()).repeat(32)


def f64(x):
    return np.asarray(x).astype(np.float64)


def striped(idx):
    return np.tile(idx.reshape(-1, 16).T, (8, 1)).astype(np.uint16)


def unstriped(offs):
    return offs[:16].T.reshape(-1).astype(np.int64)


E2M1 = np.array([0.0, 0.5, 1.0, 1.5, 2.0, 3.0, 4.0, 6.0, -0.0, -0.5, -1.0, -1.5, -2.0, -3.0, -4.0, -6.0])


def pack_weight(w, fmt):
    k, n = w.shape
    w = f64(np.asarray(w, np.float32).astype(ml_dtypes.bfloat16)).reshape(k // 32, 32, n)
    amax = np.abs(w).max(1)
    if fmt == "e4m3":
        byte = np.frexp(amax)[1] - 1 + 127 - 7
    else:
        mant, ex = np.frexp(amax / 6.0)
        byte = np.where(mant > 0.5, ex, ex - 1) + 127
    byte = np.clip(np.where(amax > 0, byte, 1), 1, 254)
    scaled = (w * np.exp2(127.0 - byte)[:, None, :]).reshape(k, n).astype(np.float32)
    by_word = np.ascontiguousarray(scaled.reshape(k // 512, 128, 4, n).transpose(0, 1, 3, 2))
    if fmt == "e4m3":
        words = by_word.astype(ml_dtypes.float8_e4m3fn).view(np.uint8)
    else:
        c = by_word.astype(ml_dtypes.float4_e2m1fn).view(np.uint8) & 0xF
        words = (c[..., 0::2] | (c[..., 1::2] << 4)).reshape(k // 512, 128, 2 * n)
    return np.ascontiguousarray(words), np.ascontiguousarray(byte.astype(np.uint8).reshape(k // 512, 16, n))


def unpack_weight(words, scales, fmt):
    g, _, n = scales.shape
    words = np.ascontiguousarray(words).reshape(g, 128, n, -1)
    if fmt == "e4m3":
        vals = words.view(ml_dtypes.float8_e4m3fn).astype(np.float64)
    else:
        nib = np.empty((g, 128, n, 4), np.uint8)
        nib[..., 0::2] = words & 0xF
        nib[..., 1::2] = words >> 4
        vals = E2M1[nib]
    vals = vals * np.repeat(np.exp2(scales.astype(np.float64) - 127.0), 8, axis=1)[..., None]
    return vals.transpose(0, 1, 3, 2).reshape(g * 512, n)


K, T, E, C, N, TOP = 512, 512, 12, 128, 512, 3


def by_expert(wq, xq):
    return np.concatenate([wq[e].T @ xq[:, e * C:(e + 1) * C] for e in range(E)], axis=1)


def setup_inputs():
    n = np.random.standard_normal
    v = mx_kscale(N)
    deal = np.repeat(np.arange(E), C).reshape(TOP, T)[:, np.random.permutation(T)]
    deal = np.take_along_axis(deal, np.argsort(np.random.rand(TOP, T), axis=0), axis=0)
    for _ in range(8):
        s_, t_ = np.random.permutation(T).reshape(2, -1); r = np.random.randint(TOP, size=T // 2); x, y = deal[r, s_].copy(), deal[r, t_].copy()
        ok = ~((deal[:, s_] == y).any(0) | (deal[:, t_] == x).any(0)); deal[r[ok], s_[ok]] = y[ok]; deal[r[ok], t_[ok]] = x[ok]
    order = np.argsort(deal.reshape(-1) + 0.5 * np.random.rand(TOP * T))
    slot_token = order % T; pos = np.empty(TOP * T, np.int64); pos[order] = np.arange(TOP * T); pos = pos.reshape(TOP, T)
    g = np.random.uniform(0.5, 1.5, (TOP, T)); g = g / g.sum(0)
    w_slot = np.empty(E * C)
    for r in range(TOP): w_slot[pos[r]] = g[r]
    dq = pack_weight(n((N, T)) * v[:, None], "e4m3")
    dk = pack_weight(n((N, T)) * v[:, None], "e4m3")
    dv = pack_weight(n((N, T)) * v[:, None], "e4m3")
    wk = [pack_weight(m, "e2m1") for m in n((E, N, K)) / np.sqrt(N) / v[None, :, None]]
    wv = [pack_weight(m, "e4m3") for m in n((E, N, K)) / np.sqrt(N) / v[None, :, None]]
    return {
        "dq_words": dq[0],
        "dq_scales": dq[1],
        "dk_words": dk[0],
        "dk_scales": dk[1],
        "dv_words": dv[0],
        "dv_scales": dv[1],
        "wq": (n((E, N, K)) / np.sqrt(N) / v[None, :, None]).astype(np.float32),
        "wk_words": np.stack([m[0] for m in wk]),
        "wk_scales": np.stack([m[1] for m in wk]),
        "wv_words": np.stack([m[0] for m in wv]),
        "wv_scales": np.stack([m[1] for m in wv]),
        "gate": (np.tile(w_slot, (128, 1))).astype(np.float32),
        "offs": striped(slot_token),
        "pos1": striped(pos[0]),
        "pos2": striped(pos[1]),
        "pos3": striped(pos[2]),
    }


def reference(dq_words, dq_scales, dk_words, dk_scales, dv_words, dv_scales, wq, wk_words, wk_scales, wv_words, wv_scales, gate, offs, pos1, pos2, pos3):
    wqq = mxq(f64(wq), 1, "e4m3")
    wk = np.stack([unpack_weight(wk_words[e], wk_scales[e], "e2m1") for e in range(E)])
    wv = np.stack([unpack_weight(wv_words[e], wv_scales[e], "e4m3") for e in range(E)])
    idx = unstriped(offs)
    gq, gk, gv = [unpack_weight(w, s, "e4m3")[:, idx] for w, s in ((dq_words, dq_scales), (dk_words, dk_scales), (dv_words, dv_scales))]
    dx = f64(gate[:1]) * (by_expert(wqq, gq) + by_expert(wk, gk) + by_expert(wv, gv))
    out = dx[:, unstriped(pos1)] + dx[:, unstriped(pos2)] + dx[:, unstriped(pos3)]
    return out

@@ -1,0 +1,197 @@
+from contextlib import ExitStack
+
+import concourse.mybir as mybir
+
+F32 = mybir.dt.float32
+BF16 = mybir.dt.bfloat16
+I32 = mybir.dt.int32
+U32 = mybir.dt.uint32
+U16 = mybir.dt.uint16
+U8 = mybir.dt.uint8
+FP8X4 = mybir.dt.float8_e4m3fn_x4
+FP4X4 = mybir.dt.float4_e2m1fn_x4
+MULT = mybir.AluOpType.mult
+ADD = mybir.AluOpType.add
+
+P = 128
+T = 512
+E = 12
+C = 128
+S = E * C
+K = 512
+HALF = 256
+GATHER = 384
+CHUNK = 4
+FLOPS = 2 * 3 * 512 * K * S
+
+
+def tile_moe_qkb_kernel(
+    tc, dq_words, dq_scales, dk_words, dk_scales, dv_words, dv_scales, wq, wk_words, wk_scales,
+    wv_words, wv_scales, gate, offs, pos1, pos2, pos3, out,
+):
+    nc = tc.nc
+    with ExitStack() as ctx:
+        keep = ctx.enter_context(tc.tile_pool(name="keep", bufs=1))
+        ring = ctx.enter_context(tc.tile_pool(name="ring", bufs=1))
+        psum = ctx.enter_context(tc.psum_pool(name="psum", bufs=8))
+
+        offs_sb = keep.tile([P, S // 16], U16, name="offs_sb")
+        pos_sb = [keep.tile([P, T // 16], U16, name="pos_sb%d" % i) for i in range(3)]
+        d_words = [keep.tile([P, T], I32, name="d_words%d" % i, align_bytes=64) for i in range(3)]
+        d_scales = [keep.tile([P, T], U8, name="d_scales%d" % i, align_bytes=64) for i in range(3)]
+        g_words = [keep.tile([P, S], U32, name="g_words%d" % i, align_bytes=64) for i in range(3)]
+        g_scales = [keep.tile([P, S], U8, name="g_scales%d" % i, align_bytes=64) for i in range(3)]
+        k_codes = [keep.tile([P, CHUNK * 2 * K], U8, name="k_codes%d" % i, align_bytes=64) for i in range(E // CHUNK)]
+        v_codes = [keep.tile([P, CHUNK * 4 * K], U8, name="v_codes%d" % i, align_bytes=64) for i in range(E // CHUNK)]
+        k_plane = keep.tile([P, E * K], U8, name="k_plane", align_bytes=64)
+        v_plane = keep.tile([P, E * K], U8, name="v_plane", align_bytes=64)
+        gate_sb = keep.tile([P, S], F32, name="gate_sb")
+        dx = [keep.tile([P, S], F32, name="dx%d" % b) for b in range(K // P)]
+
+        for i in range(3):
+            nc.vector.memset(d_scales[i][:].bitcast(I32), 0)
+        nc.vector.memset(k_plane[:].bitcast(I32), 0)
+        nc.vector.memset(v_plane[:].bitcast(I32), 0)
+
+        def load_d_scales(i, r):
+            src = (dq_scales, dk_scales, dv_scales)[i]
+            nc.sync.dma_start(
+                out=d_scales[i][r:P:32, :].bitcast(I32),
+                in_=src.rearrange("s (q r) t -> r (s q) t", r=4)[r].bitcast(I32),
+            )
+
+        def load_w_scales(plane, src, r):
+            nc.sync.dma_start(
+                out=plane[r:P:32, :].bitcast(I32).rearrange("q (e c) -> q e c", e=E),
+                in_=src.rearrange("e s (q r) c -> r q (e s) c", r=4)[r].bitcast(I32),
+            )
+
+        def load_k(g):
+            nc.sync.dma_start(
+                out=k_codes[g][:].bitcast(I32).rearrange("p (e c) -> p e c", e=CHUNK),
+                in_=wk_words[g * CHUNK:(g + 1) * CHUNK].rearrange("e s p c -> p (e s) c").bitcast(I32),
+            )
+
+        def load_v(g):
+            nc.sync.dma_start(
+                out=v_codes[g][:].bitcast(I32).rearrange("p (e c) -> p e c", e=CHUNK),
+                in_=wv_words[g * CHUNK:(g + 1) * CHUNK].rearrange("e s p c d -> p (e s) (c d)").bitcast(I32),
+            )
+
+        raw = {}
+
+        def load_q(h, e):
+            raw[h, e] = ring.tile([P, 4, HALF], F32, name="raw", tag="raw", bufs=12)
+            nc.sync.dma_start(
+                out=raw[h, e][:],
+                in_=wq[e].rearrange("(p j) c -> p j c", j=4)[:, :, h * HALF:(h + 1) * HALF],
+            )
+
+        grouped = {}
+
+        def cast_q(h, e):
+            grouped[h, e] = ring.tile([P, HALF, 4], BF16, name="grouped", tag="grouped", bufs=16, align_bytes=64)
+            nc.scalar.copy(
+                out=grouped[h, e][:].rearrange("p (c i) j -> p c j i", i=4),
+                in_=raw[h, e][:].rearrange("p j (c i) -> p c j i", i=4),
+            )
+
+        q_codes = {}
+        q_plane = {}
+
+        def quantize_q(h, e):
+            q_codes[h, e] = ring.tile([P, HALF], U32, name="q_codes", tag="q_codes", bufs=12, align_bytes=64)
+            q_plane[h, e] = ring.tile([P, HALF], U8, name="q_plane", tag="q_plane", bufs=12, align_bytes=64)
+            nc.vector.quantize_mx(
+                out=q_codes[h, e][:].bitcast(FP8X4),
+                scales=q_plane[h, e][:],
+                in_=grouped[h, e][:].rearrange("p c j -> p (c j)"),
+            )
+
+        def gather_words(i, u):
+            nc.vector.tensor_copy(
+                g_words[i][:, u * GATHER:(u + 1) * GATHER],
+                d_words[i][:].bitcast(U32).indirect(offs_sb[:, u * GATHER // 16:(u + 1) * GATHER // 16]),
+            )
+
+        def gather_scales(i, u):
+            nc.vector.tensor_copy(
+                g_scales[i][:, u * GATHER:(u + 1) * GATHER],
+                d_scales[i][:].indirect(offs_sb[:, u * GATHER // 16:(u + 1) * GATHER // 16]),
+            )
+
+        def multiply(acc, b, e):
+            slots = slice(e * C, (e + 1) * C)
+            g, u = divmod(e, CHUNK)
+            col = u * K + b * P
+            w_cols = slice(e * K + b * P, e * K + (b + 1) * P)
+            h, bh = divmod(b, 2)
+            q_cols = slice(bh * P, (bh + 1) * P)
+            nc.tensor.matmul_mx(
+                out=acc, lhsT=k_codes[g][:, 2 * col:2 * (col + P)].bitcast(FP4X4), lhsT_scale=k_plane[:, w_cols],
+                rhs=g_words[1][:, slots].bitcast(FP8X4), rhs_scale=g_scales[1][:, slots], start=True, stop=False,
+            )
+            nc.tensor.matmul_mx(
+                out=acc, lhsT=v_codes[g][:, 4 * col:4 * (col + P)].bitcast(FP8X4), lhsT_scale=v_plane[:, w_cols],
+                rhs=g_words[2][:, slots].bitcast(FP8X4), rhs_scale=g_scales[2][:, slots], start=False, stop=False,
+            )
+            nc.tensor.matmul_mx(
+                out=acc, lhsT=q_codes[h, e][:, q_cols].bitcast(FP8X4), lhsT_scale=q_plane[h, e][:, q_cols],
+                rhs=g_words[0][:, slots].bitcast(FP8X4), rhs_scale=g_scales[0][:, slots], start=False, stop=True,
+            )
+
+        def combine(b, queue, stores):
+            sums = [ring.tile([P, T], F32, name="sums", tag="sums", bufs=6) for step in range(3)]
+            for step in range(3):
+                for th in range(2):
+                    picked = dx[b][:].indirect(pos_sb[step][:, th * 16:(th + 1) * 16])
+                    cols = slice(th * (T // 2), (th + 1) * (T // 2))
+                    if step == 0:
+                        nc.vector.tensor_copy(sums[0][:, cols], picked)
+                    else:
+                        nc.vector.tensor_tensor(sums[step][:, cols], picked, sums[step - 1][:, cols], ADD)
+            for piece in range(stores):
+                cols = slice(piece * (T // stores), (piece + 1) * (T // stores))
+                queue.dma_start(out=out[b * P:(b + 1) * P, cols], in_=sums[2][:, cols])
+
+        nc.sync.dma_start(offs_sb[:], offs)
+        for i, src in enumerate((dq_words, dk_words, dv_words)):
+            nc.sync.dma_start(out=d_words[i][:], in_=src[0].rearrange("p t d -> p (t d)").bitcast(I32))
+        small = [lambda i=i, r=r: load_d_scales(i, r) for i in range(3) for r in range(4)]
+        small += [lambda r=r: load_w_scales(k_plane, wk_scales, r) for r in range(4)]
+        small += [lambda r=r: load_w_scales(v_plane, wv_scales, r) for r in range(4)]
+        small += [lambda i=i, src=src: nc.sync.dma_start(pos_sb[i][:], src) for i, src in enumerate((pos1, pos2, pos3))]
+        for e in range(E):
+            load_q(0, e)
+            for issue in small[2 * e:2 * e + 2]:
+                issue()
+            if e % CHUNK == 1:
+                load_v(e // CHUNK)
+            if e % CHUNK == 2:
+                load_k(e // CHUNK)
+            if e == 7:
+                nc.sync.dma_start(out=gate_sb[:], in_=gate)
+
+        for i in range(3):
+            for u in range(S // GATHER):
+                gather_words(i, u)
+        for u in range(S // GATHER):
+            for i in range(3):
+                gather_scales(i, u)
+
+        for h in range(2):
+            groups = ((0, 4), (4, 8), (8, 12)) if h == 0 else ((0, 4), (4, 8), (8, 11), (11, 12))
+            for first, last in groups:
+                banks = [psum.tile([P, CHUNK * C], F32, name="bank", tag="bank") for bh in range(2)]
+                for e in range(first, last):
+                    if h == 1:
+                        load_q(h, e)
+                    cast_q(h, e)
+                    quantize_q(h, e)
+                    for bh in range(2):
+                        multiply(banks[bh][:, (e - first) * C:(e - first + 1) * C], 2 * h + bh, e)
+                cols = slice(first * C, last * C)
+                for bh in range(2):
+                    nc.vector.tensor_tensor(dx[2 * h + bh][:, cols], banks[bh][:, 0:(last - first) * C], gate_sb[:, cols], MULT)
+            for bh in range(2):
+                combine(2 * h + bh, nc.gpsimd if h == 0 else nc.sync, 1 + h * bh)

@@ -1,6 +1,7 @@
 from contextlib import ExitStack
 
 import concourse.mybir as mybir
+from concourse.masks import make_identity
 
 F32 = mybir.dt.float32
 BF16 = mybir.dt.bfloat16
@@ -10,8 +11,8 @@ U16 = mybir.dt.uint16
 U8 = mybir.dt.uint8
 FP8X4 = mybir.dt.float8_e4m3fn_x4
 FP4X4 = mybir.dt.float4_e2m1fn_x4
-MULT = mybir.AluOpType.mult
 ADD = mybir.AluOpType.add
+COPY = mybir.ActivationFunctionType.Copy
 
 P = 128
 T = 512
@@ -19,9 +20,10 @@ E = 12
 C = 128
 S = E * C
 K = 512
-HALF = 256
+BLOCKS = K // P
 GATHER = 384
-CHUNK = 4
+GROUPS = ((0, 4), (4, 8), (8, 10), (10, 12))
+SHARED_FROM = 8
 FLOPS = 2 * 3 * 512 * K * S
 
 
@@ -33,7 +35,7 @@ def tile_moe_qkb_kernel(
     with ExitStack() as ctx:
         keep = ctx.enter_context(tc.tile_pool(name="keep", bufs=1))
         ring = ctx.enter_context(tc.tile_pool(name="ring", bufs=1))
-        psum = ctx.enter_context(tc.psum_pool(name="psum", bufs=8))
+        psum = ctx.enter_context(tc.psum_pool(name="psum", bufs=4))
 
         offs_sb = keep.tile([P, S // 16], U16, name="offs_sb")
         pos_sb = [keep.tile([P, T // 16], U16, name="pos_sb%d" % i) for i in range(3)]
@@ -41,72 +43,96 @@ def tile_moe_qkb_kernel(
         d_scales = [keep.tile([P, T], U8, name="d_scales%d" % i, align_bytes=64) for i in range(3)]
         g_words = [keep.tile([P, S], U32, name="g_words%d" % i, align_bytes=64) for i in range(3)]
         g_scales = [keep.tile([P, S], U8, name="g_scales%d" % i, align_bytes=64) for i in range(3)]
-        k_codes = [keep.tile([P, CHUNK * 2 * K], U8, name="k_codes%d" % i, align_bytes=64) for i in range(E // CHUNK)]
-        v_codes = [keep.tile([P, CHUNK * 4 * K], U8, name="v_codes%d" % i, align_bytes=64) for i in range(E // CHUNK)]
         k_plane = keep.tile([P, E * K], U8, name="k_plane", align_bytes=64)
-        v_plane = keep.tile([P, E * K], U8, name="v_plane", align_bytes=64)
-        gate_sb = keep.tile([P, S], F32, name="gate_sb")
-        dx = [keep.tile([P, S], F32, name="dx%d" % b) for b in range(K // P)]
+        v_plane = keep.tile([P, E // 4 * K], U8, name="v_plane", align_bytes=64)
+        gate_rows = keep.tile([P, C], F32, name="gate_rows")
+        gate_cols = keep.tile([P, E], F32, name="gate_cols")
+        identity = keep.tile([P, P], F32, name="identity")
+        dx = [keep.tile([P, S], F32, name="dx%d" % b) for b in range(BLOCKS)]
 
         for i in range(3):
             nc.vector.memset(d_scales[i][:].bitcast(I32), 0)
-        nc.vector.memset(k_plane[:].bitcast(I32), 0)
         nc.vector.memset(v_plane[:].bitcast(I32), 0)
+        nc.vector.memset(k_plane[:].bitcast(I32), 0)
+        nc.gpsimd.memset(gate_rows[:], 0.0)
+        make_identity(nc, identity[:])
 
-        def load_d_scales(i, r):
+        nc.scalar.dma_start(out=gate_rows[0:E, :], in_=gate[0].rearrange("(e u) -> e u", u=C))
+        gate_bank = psum.tile([P, K], F32, name="gate_bank", tag="by_channel")
+        nc.tensor.transpose(gate_bank[:, 0:P], gate_rows[:], identity[:])
+        nc.scalar.activation(gate_cols[:], gate_bank[:, 0:E], COPY)
+
+        def load_d_words(i):
+            src = (dq_words, dk_words, dv_words)[i]
+            nc.sync.dma_start(out=d_words[i][:], in_=src[0].rearrange("p t d -> p (t d)").bitcast(I32))
+
+        def load_d_scales(i):
             src = (dq_scales, dk_scales, dv_scales)[i]
-            nc.sync.dma_start(
-                out=d_scales[i][r:P:32, :].bitcast(I32),
-                in_=src.rearrange("s (q r) t -> r (s q) t", r=4)[r].bitcast(I32),
-            )
+            for r in range(4):
+                nc.sync.dma_start(
+                    out=d_scales[i][r:P:32, :].bitcast(I32),
+                    in_=src.rearrange("s (q r) t -> r (s q) t", r=4)[r].bitcast(I32),
+                )
 
-        def load_w_scales(plane, src, r):
-            nc.sync.dma_start(
-                out=plane[r:P:32, :].bitcast(I32).rearrange("q (e c) -> q e c", e=E),
-                in_=src.rearrange("e s (q r) c -> r q (e s) c", r=4)[r].bitcast(I32),
-            )
+        def load_k_scales():
+            for r in range(4):
+                nc.sync.dma_start(
+                    out=k_plane[r:P:32, :].bitcast(I32).rearrange("q (e c) -> q e c", e=E),
+                    in_=wk_scales.rearrange("e s (q r) c -> r q (e s) c", r=4)[r].bitcast(I32),
+                )
 
-        def load_k(g):
-            nc.sync.dma_start(
-                out=k_codes[g][:].bitcast(I32).rearrange("p (e c) -> p e c", e=CHUNK),
-                in_=wk_words[g * CHUNK:(g + 1) * CHUNK].rearrange("e s p c -> p (e s) c").bitcast(I32),
-            )
+        def load_v_scales(four):
+            for q in range(4):
+                nc.sync.dma_start(
+                    out=v_plane[32 * q:32 * q + 16, four * K:(four + 1) * K].bitcast(I32),
+                    in_=wv_scales[4 * four:4 * four + 4, 0, 4 * q:4 * q + 4, :].bitcast(I32),
+                )
 
-        def load_v(g):
+        def load_pos():
+            for i, src in enumerate((pos1, pos2, pos3)):
+                nc.sync.dma_start(pos_sb[i][:], src)
+
+        k_codes = {}
+        v_codes = {}
+
+        def load_kv(b, first, last):
+            n = last - first
+            k_codes[b, first] = keep.tile([P, n * 2 * P], U8, name="k_codes%d_%d" % (b, first), align_bytes=64)
+            v_codes[b, first] = keep.tile([P, n * 4 * P], U8, name="v_codes%d_%d" % (b, first), align_bytes=64)
             nc.sync.dma_start(
-                out=v_codes[g][:].bitcast(I32).rearrange("p (e c) -> p e c", e=CHUNK),
-                in_=wv_words[g * CHUNK:(g + 1) * CHUNK].rearrange("e s p c d -> p (e s) (c d)").bitcast(I32),
+                out=k_codes[b, first][:].bitcast(I32).rearrange("p (e c) -> p e c", e=n),
+                in_=wk_words[first:last].rearrange("e s p c -> p (e s) c")[:, :, b * 2 * P:(b + 1) * 2 * P].bitcast(I32),
+            )
+            nc.sync.dma_start(
+                out=v_codes[b, first][:].bitcast(I32).rearrange("p (e c) -> p e c", e=n),
+                in_=wv_words[first:last].rearrange("e s p c d -> p (e s) (c d)")[:, :, b * 4 * P:(b + 1) * 4 * P].bitcast(I32),
             )
 
         raw = {}
 
-        def load_q(h, e):
-            raw[h, e] = ring.tile([P, 4, HALF], F32, name="raw", tag="raw", bufs=12)
-            nc.sync.dma_start(
-                out=raw[h, e][:],
-                in_=wq[e].rearrange("(p j) c -> p j c", j=4)[:, :, h * HALF:(h + 1) * HALF],
-            )
-
-        grouped = {}
-
-        def cast_q(h, e):
-            grouped[h, e] = ring.tile([P, HALF, 4], BF16, name="grouped", tag="grouped", bufs=16, align_bytes=64)
-            nc.scalar.copy(
-                out=grouped[h, e][:].rearrange("p (c i) j -> p c j i", i=4),
-                in_=raw[h, e][:].rearrange("p j (c i) -> p c j i", i=4),
-            )
+        def load_q(e):
+            raw[e] = ring.tile([P, 4, K], F32, name="raw", tag="raw", bufs=6)
+            nc.sync.dma_start(out=raw[e][:], in_=wq[e].rearrange("(p j) c -> p j c", j=4))
 
         q_codes = {}
         q_plane = {}
 
-        def quantize_q(h, e):
-            q_codes[h, e] = ring.tile([P, HALF], U32, name="q_codes", tag="q_codes", bufs=12, align_bytes=64)
-            q_plane[h, e] = ring.tile([P, HALF], U8, name="q_plane", tag="q_plane", bufs=12, align_bytes=64)
-            nc.vector.quantize_mx(
-                out=q_codes[h, e][:].bitcast(FP8X4),
-                scales=q_plane[h, e][:],
-                in_=grouped[h, e][:].rearrange("p c j -> p (c j)"),
+        def quantize_q(e, first, last, copy):
+            width = (last - first) * P
+            grouped = ring.tile([P, width, 4], BF16, name="grouped", tag="grouped", bufs=7, align_bytes=64)
+            copy(
+                grouped[:].rearrange("p (c i) j -> p c j i", i=4),
+                raw[e][:, :, first * P:last * P].rearrange("p j (c i) -> p c j i", i=4),
             )
+            codes = keep.tile([P, width], U32, name="q_codes%d_%d" % (e, first), align_bytes=64)
+            plane = keep.tile([P, width], U8, name="q_plane%d_%d" % (e, first), align_bytes=64)
+            nc.vector.quantize_mx(
+                out=codes[:].bitcast(FP8X4), scales=plane[:], in_=grouped[:].rearrange("p c j -> p (c j)"),
+            )
+            for b in range(first, last):
+                cols = slice((b - first) * P, (b - first + 1) * P)
+                q_codes[e, b] = codes[:, cols]
+                q_plane[e, b] = plane[:, cols]
 
         def gather_words(i, u):
             nc.vector.tensor_copy(
@@ -120,28 +146,42 @@ def tile_moe_qkb_kernel(
                 d_scales[i][:].indirect(offs_sb[:, u * GATHER // 16:(u + 1) * GATHER // 16]),
             )
 
-        def multiply(acc, b, e):
+        def multiply(acc, b, first, e):
             slots = slice(e * C, (e + 1) * C)
-            g, u = divmod(e, CHUNK)
-            col = u * K + b * P
-            w_cols = slice(e * K + b * P, e * K + (b + 1) * P)
-            h, bh = divmod(b, 2)
-            q_cols = slice(bh * P, (bh + 1) * P)
+            col = (e - first) * P
+            four, j = divmod(e, 4)
             nc.tensor.matmul_mx(
-                out=acc, lhsT=k_codes[g][:, 2 * col:2 * (col + P)].bitcast(FP4X4), lhsT_scale=k_plane[:, w_cols],
-                rhs=g_words[1][:, slots].bitcast(FP8X4), rhs_scale=g_scales[1][:, slots], start=True, stop=False,
+                out=acc, lhsT=g_words[1][:, slots].bitcast(FP8X4), lhsT_scale=g_scales[1][:, slots],
+                rhs=k_codes[b, first][:, 2 * col:2 * (col + P)].bitcast(FP4X4),
+                rhs_scale=k_plane[:, e * K + b * P:e * K + (b + 1) * P], start=True, stop=False,
             )
             nc.tensor.matmul_mx(
-                out=acc, lhsT=v_codes[g][:, 4 * col:4 * (col + P)].bitcast(FP8X4), lhsT_scale=v_plane[:, w_cols],
-                rhs=g_words[2][:, slots].bitcast(FP8X4), rhs_scale=g_scales[2][:, slots], start=False, stop=False,
+                out=acc, lhsT=g_words[2][:, slots].bitcast(FP8X4), lhsT_scale=g_scales[2][:, slots],
+                rhs=v_codes[b, first][:, 4 * col:4 * (col + P)].bitcast(FP8X4),
+                rhs_scale=v_plane[4 * j:P, four * K + b * P:four * K + (b + 1) * P], start=False, stop=False,
             )
             nc.tensor.matmul_mx(
-                out=acc, lhsT=q_codes[h, e][:, q_cols].bitcast(FP8X4), lhsT_scale=q_plane[h, e][:, q_cols],
-                rhs=g_words[0][:, slots].bitcast(FP8X4), rhs_scale=g_scales[0][:, slots], start=False, stop=True,
+                out=acc, lhsT=g_words[0][:, slots].bitcast(FP8X4), lhsT_scale=g_scales[0][:, slots],
+                rhs=q_codes[e, b].bitcast(FP8X4), rhs_scale=q_plane[e, b], start=False, stop=True,
             )
 
-        def combine(b, queue, stores):
-            sums = [ring.tile([P, T], F32, name="sums", tag="sums", bufs=6) for step in range(3)]
+        def slots_of(b, first, last):
+            by_slot = psum.tile([P, K], F32, name="by_slot", tag="by_slot")
+            for e in range(first, last):
+                multiply(by_slot[:, (e - first) * P:(e - first + 1) * P], b, first, e)
+            gated = ring.tile([P, K], F32, name="gated", tag="gated", bufs=4)
+            for e in range(first, last):
+                cols = slice((e - first) * P, (e - first + 1) * P)
+                nc.scalar.activation(gated[:, cols], by_slot[:, cols], COPY, scale=gate_cols[:, e:e + 1])
+            by_channel = psum.tile([P, K], F32, name="by_channel", tag="by_channel")
+            for e in range(first, last):
+                cols = slice((e - first) * P, (e - first + 1) * P)
+                nc.tensor.transpose(by_channel[:, cols], gated[:, cols], identity[:])
+            nc.scalar.copy(dx[b][:, first * C:last * C], by_channel[:, 0:(last - first) * C])
+
+        def combine(b, stores):
+            sums = [ring.tile([P, T], F32, name="sums", tag="sums", bufs=6) for step in range(2)]
+            sums.append(ring.tile([P, T], F32, name="result", tag="result", bufs=4))
             for step in range(3):
                 for th in range(2):
                     picked = dx[b][:].indirect(pos_sb[step][:, th * 16:(th + 1) * 16])
@@ -152,25 +192,36 @@ def tile_moe_qkb_kernel(
                         nc.vector.tensor_tensor(sums[step][:, cols], picked, sums[step - 1][:, cols], ADD)
             for piece in range(stores):
                 cols = slice(piece * (T // stores), (piece + 1) * (T // stores))
-                queue.dma_start(out=out[b * P:(b + 1) * P, cols], in_=sums[2][:, cols])
+                nc.sync.dma_start(out=out[b * P:(b + 1) * P, cols], in_=sums[2][:, cols])
 
         nc.sync.dma_start(offs_sb[:], offs)
-        for i, src in enumerate((dq_words, dk_words, dv_words)):
-            nc.sync.dma_start(out=d_words[i][:], in_=src[0].rearrange("p t d -> p (t d)").bitcast(I32))
-        small = [lambda i=i, r=r: load_d_scales(i, r) for i in range(3) for r in range(4)]
-        small += [lambda r=r: load_w_scales(k_plane, wk_scales, r) for r in range(4)]
-        small += [lambda r=r: load_w_scales(v_plane, wv_scales, r) for r in range(4)]
-        small += [lambda i=i, src=src: nc.sync.dma_start(pos_sb[i][:], src) for i, src in enumerate((pos1, pos2, pos3))]
-        for e in range(E):
-            load_q(0, e)
-            for issue in small[2 * e:2 * e + 2]:
-                issue()
-            if e % CHUNK == 1:
-                load_v(e // CHUNK)
-            if e % CHUNK == 2:
-                load_k(e // CHUNK)
-            if e == 7:
-                nc.sync.dma_start(out=gate_sb[:], in_=gate)
+        load_d_words(0)
+        load_q(0)
+        load_d_words(1)
+        load_d_scales(0)
+        load_q(1)
+        load_d_words(2)
+        load_d_scales(1)
+        load_q(2)
+        load_d_scales(2)
+        load_q(3)
+        load_k_scales()
+        for four in range(3):
+            load_q(4 + four)
+            load_v_scales(four)
+        load_q(7)
+        load_kv(0, *GROUPS[0])
+        load_q(8)
+        load_pos()
+        load_kv(0, *GROUPS[1])
+        load_q(9)
+        load_q(10)
+        load_kv(0, *GROUPS[2])
+        load_q(11)
+        load_kv(0, *GROUPS[3])
+        for b in range(1, BLOCKS):
+            for first, last in GROUPS:
+                load_kv(b, first, last)
 
         for i in range(3):
             for u in range(S // GATHER):
@@ -179,19 +230,16 @@ def tile_moe_qkb_kernel(
             for i in range(3):
                 gather_scales(i, u)
 
-        for h in range(2):
-            groups = ((0, 4), (4, 8), (8, 12)) if h == 0 else ((0, 4), (4, 8), (8, 11), (11, 12))
-            for first, last in groups:
-                banks = [psum.tile([P, CHUNK * C], F32, name="bank", tag="bank") for bh in range(2)]
-                for e in range(first, last):
-                    if h == 1:
-                        load_q(h, e)
-                    cast_q(h, e)
-                    quantize_q(h, e)
-                    for bh in range(2):
-                        multiply(banks[bh][:, (e - first) * C:(e - first + 1) * C], 2 * h + bh, e)
-                cols = slice(first * C, last * C)
-                for bh in range(2):
-                    nc.vector.tensor_tensor(dx[2 * h + bh][:, cols], banks[bh][:, 0:(last - first) * C], gate_sb[:, cols], MULT)
-            for bh in range(2):
-                combine(2 * h + bh, nc.gpsimd if h == 0 else nc.sync, 1 + h * bh)
+        for first, last in GROUPS:
+            for e in range(first, last):
+                if e < SHARED_FROM:
+                    quantize_q(e, 0, BLOCKS, nc.scalar.copy)
+                else:
+                    quantize_q(e, 0, 2, nc.vector.tensor_copy)
+                    quantize_q(e, 2, BLOCKS, nc.scalar.copy)
+            slots_of(0, first, last)
+        combine(0, 1)
+        for b in range(1, BLOCKS):
+            for first, last in GROUPS:
+                slots_of(b, first, last)
+            combine(b, 2 if b == BLOCKS - 1 else 1)

@@ -22,8 +22,10 @@ S = E * C
 K = 512
 BLOCKS = K // P
 GATHER = 384
-GROUPS = ((0, 4), (4, 8), (8, 10), (10, 12))
-SHARED_FROM = 8
+EARLY = 3
+FIRST_GROUPS = ((3, 7), (7, 11), (11, 12))
+LATER_GROUPS = ((3, 7), (7, 10), (10, 12))
+VECTOR_FROM = 10
 FLOPS = 2 * 3 * 512 * K * S
 
 
@@ -50,12 +52,22 @@ def tile_moe_qkb_kernel(
         identity = keep.tile([P, P], F32, name="identity")
         dx = [keep.tile([P, S], F32, name="dx%d" % b) for b in range(BLOCKS)]
 
+        make_identity(nc, identity[:])
         for i in range(3):
-            nc.vector.memset(d_scales[i][:].bitcast(I32), 0)
+            nc.gpsimd.memset(d_scales[i][:].bitcast(I32), 0)
         nc.vector.memset(v_plane[:].bitcast(I32), 0)
         nc.vector.memset(k_plane[:].bitcast(I32), 0)
-        nc.gpsimd.memset(gate_rows[:], 0.0)
-        make_identity(nc, identity[:])
+        nc.vector.memset(gate_rows[:], 0.0)
+
+        def load_d_scales(queue, i, r):
+            queue.dma_start(
+                out=d_scales[i][r:P:32, :].bitcast(I32),
+                in_=(dq_scales, dk_scales, dv_scales)[i].rearrange("s (q r) t -> r (s q) t", r=4)[r].bitcast(I32),
+            )
+
+        for i in (1, 2):
+            for r in range(4):
+                load_d_scales(nc.gpsimd, i, r)
 
         nc.scalar.dma_start(out=gate_rows[0:E, :], in_=gate[0].rearrange("(e u) -> e u", u=C))
         gate_bank = psum.tile([P, K], F32, name="gate_bank", tag="by_channel")
@@ -66,47 +78,49 @@ def tile_moe_qkb_kernel(
             src = (dq_words, dk_words, dv_words)[i]
             nc.sync.dma_start(out=d_words[i][:], in_=src[0].rearrange("p t d -> p (t d)").bitcast(I32))
 
-        def load_d_scales(i):
-            src = (dq_scales, dk_scales, dv_scales)[i]
-            for r in range(4):
-                nc.sync.dma_start(
-                    out=d_scales[i][r:P:32, :].bitcast(I32),
-                    in_=src.rearrange("s (q r) t -> r (s q) t", r=4)[r].bitcast(I32),
-                )
+        def load_k_scales(r):
+            nc.sync.dma_start(
+                out=k_plane[r:P:32, :].bitcast(I32).rearrange("q (e c) -> q e c", e=E),
+                in_=wk_scales.rearrange("e s (q r) c -> r q (e s) c", r=4)[r].bitcast(I32),
+            )
 
-        def load_k_scales():
-            for r in range(4):
-                nc.sync.dma_start(
-                    out=k_plane[r:P:32, :].bitcast(I32).rearrange("q (e c) -> q e c", e=E),
-                    in_=wk_scales.rearrange("e s (q r) c -> r q (e s) c", r=4)[r].bitcast(I32),
-                )
+        def load_v_scales(four, q):
+            nc.sync.dma_start(
+                out=v_plane[32 * q:32 * q + 16, four * K:(four + 1) * K].bitcast(I32),
+                in_=wv_scales[4 * four:4 * four + 4, 0, 4 * q:4 * q + 4, :].bitcast(I32),
+            )
 
-        def load_v_scales(four):
-            for q in range(4):
-                nc.sync.dma_start(
-                    out=v_plane[32 * q:32 * q + 16, four * K:(four + 1) * K].bitcast(I32),
-                    in_=wv_scales[4 * four:4 * four + 4, 0, 4 * q:4 * q + 4, :].bitcast(I32),
-                )
-
-        def load_pos():
-            for i, src in enumerate((pos1, pos2, pos3)):
-                nc.sync.dma_start(pos_sb[i][:], src)
+        def load_small(which, *where):
+            if which == "d":
+                load_d_scales(nc.sync, 0, *where)
+            elif which == "k":
+                load_k_scales(*where)
+            elif which == "v":
+                load_v_scales(*where)
+            else:
+                nc.sync.dma_start(pos_sb[where[0]][:], (pos1, pos2, pos3)[where[0]])
 
         k_codes = {}
         v_codes = {}
 
-        def load_kv(b, first, last):
+        def load_kv(first, last, b0, b1):
             n = last - first
-            k_codes[b, first] = keep.tile([P, n * 2 * P], U8, name="k_codes%d_%d" % (b, first), align_bytes=64)
-            v_codes[b, first] = keep.tile([P, n * 4 * P], U8, name="v_codes%d_%d" % (b, first), align_bytes=64)
+            width = (b1 - b0) * P
+            k_tile = keep.tile([P, n * width * 2], U8, name="k_codes%d_%d" % (first, b0), align_bytes=64)
+            v_tile = keep.tile([P, n * width * 4], U8, name="v_codes%d_%d" % (first, b0), align_bytes=64)
             nc.sync.dma_start(
-                out=k_codes[b, first][:].bitcast(I32).rearrange("p (e c) -> p e c", e=n),
-                in_=wk_words[first:last].rearrange("e s p c -> p (e s) c")[:, :, b * 2 * P:(b + 1) * 2 * P].bitcast(I32),
+                out=k_tile[:].bitcast(I32).rearrange("p (e c) -> p e c", e=n),
+                in_=wk_words[first:last].rearrange("e s p c -> p (e s) c")[:, :, b0 * 2 * P:b1 * 2 * P].bitcast(I32),
             )
             nc.sync.dma_start(
-                out=v_codes[b, first][:].bitcast(I32).rearrange("p (e c) -> p e c", e=n),
-                in_=wv_words[first:last].rearrange("e s p c d -> p (e s) (c d)")[:, :, b * 4 * P:(b + 1) * 4 * P].bitcast(I32),
+                out=v_tile[:].bitcast(I32).rearrange("p (e c) -> p e c", e=n),
+                in_=wv_words[first:last].rearrange("e s p c d -> p (e s) (c d)")[:, :, b0 * 4 * P:b1 * 4 * P].bitcast(I32),
             )
+            for e in range(first, last):
+                for b in range(b0, b1):
+                    col = (e - first) * width + (b - b0) * P
+                    k_codes[e, b] = k_tile[:, 2 * col:2 * (col + P)]
+                    v_codes[e, b] = v_tile[:, 4 * col:4 * (col + P)]
 
         raw = {}
 
@@ -114,16 +128,19 @@ def tile_moe_qkb_kernel(
             raw[e] = ring.tile([P, 4, K], F32, name="raw", tag="raw", bufs=6)
             nc.sync.dma_start(out=raw[e][:], in_=wq[e].rearrange("(p j) c -> p j c", j=4))
 
+        def cast_on_scalar(grouped, rows):
+            nc.scalar.copy(grouped.rearrange("p (c i) j -> p c j i", i=4), rows.rearrange("p j (c i) -> p c j i", i=4))
+
+        def cast_on_vector(grouped, rows):
+            nc.vector.tensor_copy(grouped.rearrange("p (c i) j -> p c j i", i=4), rows.rearrange("p j (c i) -> p c j i", i=4))
+
         q_codes = {}
         q_plane = {}
 
         def quantize_q(e, first, last, copy):
             width = (last - first) * P
             grouped = ring.tile([P, width, 4], BF16, name="grouped", tag="grouped", bufs=7, align_bytes=64)
-            copy(
-                grouped[:].rearrange("p (c i) j -> p c j i", i=4),
-                raw[e][:, :, first * P:last * P].rearrange("p j (c i) -> p c j i", i=4),
-            )
+            copy(grouped[:], raw[e][:, :, first * P:last * P])
             codes = keep.tile([P, width], U32, name="q_codes%d_%d" % (e, first), align_bytes=64)
             plane = keep.tile([P, width], U8, name="q_plane%d_%d" % (e, first), align_bytes=64)
             nc.vector.quantize_mx(
@@ -146,18 +163,17 @@ def tile_moe_qkb_kernel(
                 d_scales[i][:].indirect(offs_sb[:, u * GATHER // 16:(u + 1) * GATHER // 16]),
             )
 
-        def multiply(acc, b, first, e):
+        def multiply(acc, b, e):
             slots = slice(e * C, (e + 1) * C)
-            col = (e - first) * P
             four, j = divmod(e, 4)
             nc.tensor.matmul_mx(
                 out=acc, lhsT=g_words[1][:, slots].bitcast(FP8X4), lhsT_scale=g_scales[1][:, slots],
-                rhs=k_codes[b, first][:, 2 * col:2 * (col + P)].bitcast(FP4X4),
+                rhs=k_codes[e, b].bitcast(FP4X4),
                 rhs_scale=k_plane[:, e * K + b * P:e * K + (b + 1) * P], start=True, stop=False,
             )
             nc.tensor.matmul_mx(
                 out=acc, lhsT=g_words[2][:, slots].bitcast(FP8X4), lhsT_scale=g_scales[2][:, slots],
-                rhs=v_codes[b, first][:, 4 * col:4 * (col + P)].bitcast(FP8X4),
+                rhs=v_codes[e, b].bitcast(FP8X4),
                 rhs_scale=v_plane[4 * j:P, four * K + b * P:four * K + (b + 1) * P], start=False, stop=False,
             )
             nc.tensor.matmul_mx(
@@ -168,7 +184,7 @@ def tile_moe_qkb_kernel(
         def slots_of(b, first, last):
             by_slot = psum.tile([P, K], F32, name="by_slot", tag="by_slot")
             for e in range(first, last):
-                multiply(by_slot[:, (e - first) * P:(e - first + 1) * P], b, first, e)
+                multiply(by_slot[:, (e - first) * P:(e - first + 1) * P], b, e)
             gated = ring.tile([P, K], F32, name="gated", tag="gated", bufs=4)
             for e in range(first, last):
                 cols = slice((e - first) * P, (e - first + 1) * P)
@@ -180,7 +196,7 @@ def tile_moe_qkb_kernel(
             nc.scalar.copy(dx[b][:, first * C:last * C], by_channel[:, 0:(last - first) * C])
 
         def combine(b, stores):
-            sums = [ring.tile([P, T], F32, name="sums", tag="sums", bufs=6) for step in range(2)]
+            sums = [ring.tile([P, T], F32, name="sums", tag="sums", bufs=4) for step in range(2)]
             sums.append(ring.tile([P, T], F32, name="result", tag="result", bufs=4))
             for step in range(3):
                 for th in range(2):
@@ -194,52 +210,47 @@ def tile_moe_qkb_kernel(
                 cols = slice(piece * (T // stores), (piece + 1) * (T // stores))
                 nc.sync.dma_start(out=out[b * P:(b + 1) * P, cols], in_=sums[2][:, cols])
 
+        small = [("d", r) for r in range(4)]
+        small += [("k", r) for r in range(4)]
+        small += [("v", four, q) for four in range(E // 4) for q in range(4)]
+        small += [("pos", i) for i in range(2)]
+        kv_after = {7: (0, EARLY, 0, BLOCKS), 8: FIRST_GROUPS[0] + (0, 1), 9: (FIRST_GROUPS[1][0], E, 0, 1)}
         nc.sync.dma_start(offs_sb[:], offs)
-        load_d_words(0)
-        load_q(0)
-        load_d_words(1)
-        load_d_scales(0)
-        load_q(1)
-        load_d_words(2)
-        load_d_scales(1)
-        load_q(2)
-        load_d_scales(2)
-        load_q(3)
-        load_k_scales()
-        for four in range(3):
-            load_q(4 + four)
-            load_v_scales(four)
-        load_q(7)
-        load_kv(0, *GROUPS[0])
-        load_q(8)
-        load_pos()
-        load_kv(0, *GROUPS[1])
-        load_q(9)
-        load_q(10)
-        load_kv(0, *GROUPS[2])
-        load_q(11)
-        load_kv(0, *GROUPS[3])
+        for e in range(E):
+            if e < 3:
+                load_d_words(e)
+            load_q(e)
+            for item in small[2 * e:2 * e + 2]:
+                load_small(*item)
+            if e in kv_after:
+                load_kv(*kv_after[e])
+            if e == 9:
+                load_small("pos", 2)
         for b in range(1, BLOCKS):
-            for first, last in GROUPS:
-                load_kv(b, first, last)
+            for first, last in LATER_GROUPS:
+                load_kv(first, last, b, b + 1)
 
         for i in range(3):
             for u in range(S // GATHER):
                 gather_words(i, u)
-        for u in range(S // GATHER):
-            for i in range(3):
+        for i in range(3):
+            for u in range(S // GATHER):
                 gather_scales(i, u)
 
-        for first, last in GROUPS:
+        for e in range(EARLY):
+            quantize_q(e, 0, BLOCKS, cast_on_scalar)
+        for b in range(BLOCKS):
+            slots_of(b, 0, EARLY)
+        for first, last in FIRST_GROUPS[:-1]:
             for e in range(first, last):
-                if e < SHARED_FROM:
-                    quantize_q(e, 0, BLOCKS, nc.scalar.copy)
-                else:
-                    quantize_q(e, 0, 2, nc.vector.tensor_copy)
-                    quantize_q(e, 2, BLOCKS, nc.scalar.copy)
+                quantize_q(e, 0, BLOCKS, cast_on_scalar if e < VECTOR_FROM else cast_on_vector)
             slots_of(0, first, last)
+        quantize_q(E - 1, 0, 1, cast_on_vector)
+        slots_of(0, *FIRST_GROUPS[-1])
+        quantize_q(E - 1, 1, 2, cast_on_vector)
+        quantize_q(E - 1, 2, BLOCKS, cast_on_vector)
         combine(0, 1)
         for b in range(1, BLOCKS):
-            for first, last in GROUPS:
+            for first, last in LATER_GROUPS:
                 slots_of(b, first, last)
             combine(b, 2 if b == BLOCKS - 1 else 1)

@@ -20,12 +20,15 @@ E = 12
 C = 128
 S = E * C
 K = 512
-BLOCKS = K // P
-GATHER = 384
-EARLY = 3
-FIRST_GROUPS = ((3, 7), (7, 11), (11, 12))
-LATER_GROUPS = ((3, 7), (7, 10), (10, 12))
-VECTOR_FROM = 10
+BANDS = K // P
+TRIO = 3
+EARLY = 6
+GATHER = EARLY * C
+WINDOW = 2 * T
+STAGE_BYTES = 4 * K * 2
+PIECE_BYTES = 4 * P * 2
+LAG = 4
+V_ROW = 4
 FLOPS = 2 * 3 * 512 * K * S
 
 
@@ -36,97 +39,77 @@ def tile_moe_qkb_kernel(
     nc = tc.nc
     with ExitStack() as ctx:
         keep = ctx.enter_context(tc.tile_pool(name="keep", bufs=1))
+        shared = ctx.enter_context(tc.tile_pool(name="shared", bufs=1))
+        landing = ctx.enter_context(tc.tile_pool(name="landing", bufs=1))
         ring = ctx.enter_context(tc.tile_pool(name="ring", bufs=1))
         psum = ctx.enter_context(tc.psum_pool(name="psum", bufs=4))
 
         offs_sb = keep.tile([P, S // 16], U16, name="offs_sb")
         pos_sb = [keep.tile([P, T // 16], U16, name="pos_sb%d" % i) for i in range(3)]
-        d_words = [keep.tile([P, T], I32, name="d_words%d" % i, align_bytes=64) for i in range(3)]
-        d_scales = [keep.tile([P, T], U8, name="d_scales%d" % i, align_bytes=64) for i in range(3)]
-        g_words = [keep.tile([P, S], U32, name="g_words%d" % i, align_bytes=64) for i in range(3)]
-        g_scales = [keep.tile([P, S], U8, name="g_scales%d" % i, align_bytes=64) for i in range(3)]
-        k_plane = keep.tile([P, E * K], U8, name="k_plane", align_bytes=64)
-        v_plane = keep.tile([P, E // 4 * K], U8, name="v_plane", align_bytes=64)
+        d_words = [keep.tile([P, WINDOW], I32, name="d_words%d" % i, align_bytes=64) for i in range(3)]
+        d_scales = [keep.tile([P, WINDOW], U8, name="d_scales%d" % i, align_bytes=64) for i in range(3)]
+        kv_plane = keep.tile([P, E * K], U8, name="kv_plane", align_bytes=64)
         gate_rows = keep.tile([P, C], F32, name="gate_rows")
         gate_cols = keep.tile([P, E], F32, name="gate_cols")
         identity = keep.tile([P, P], F32, name="identity")
-        dx = [keep.tile([P, S], F32, name="dx%d" % b) for b in range(BLOCKS)]
+        dx = [keep.tile([P, S], F32, name="dx%d" % b) for b in range(BANDS)]
 
-        make_identity(nc, identity[:])
         for i in range(3):
-            nc.gpsimd.memset(d_scales[i][:].bitcast(I32), 0)
-        nc.vector.memset(v_plane[:].bitcast(I32), 0)
-        nc.vector.memset(k_plane[:].bitcast(I32), 0)
-        nc.vector.memset(gate_rows[:], 0.0)
+            nc.vector.memset(d_scales[i][:].bitcast(I32), 0)
+        for i in range(3):
+            nc.gpsimd.memset(d_words[i][:, T:WINDOW], 0)
+        nc.vector.memset(kv_plane[:].bitcast(I32), 0)
+        nc.gpsimd.memset(gate_rows[:], 0.0)
+        nc.gpsimd.dma_start(out=gate_rows[0:E, :], in_=gate[0].rearrange("(e u) -> e u", u=C))
+        make_identity(nc, identity[:])
 
-        def load_d_scales(queue, i, r):
-            queue.dma_start(
-                out=d_scales[i][r:P:32, :].bitcast(I32),
-                in_=(dq_scales, dk_scales, dv_scales)[i].rearrange("s (q r) t -> r (s q) t", r=4)[r].bitcast(I32),
-            )
-
-        for i in (1, 2):
+        def load_d_scales(i):
             for r in range(4):
-                load_d_scales(nc.gpsimd, i, r)
+                nc.sync.dma_start(
+                    out=d_scales[i][r:P:32, 0:T].bitcast(I32),
+                    in_=(dq_scales, dk_scales, dv_scales)[i].rearrange("s (q r) t -> r (s q) t", r=4)[r].bitcast(I32),
+                )
 
-        nc.scalar.dma_start(out=gate_rows[0:E, :], in_=gate[0].rearrange("(e u) -> e u", u=C))
         gate_bank = psum.tile([P, K], F32, name="gate_bank", tag="by_channel")
         nc.tensor.transpose(gate_bank[:, 0:P], gate_rows[:], identity[:])
         nc.scalar.activation(gate_cols[:], gate_bank[:, 0:E], COPY)
 
-        def load_d_words(i):
-            src = (dq_words, dk_words, dv_words)[i]
-            nc.sync.dma_start(out=d_words[i][:], in_=src[0].rearrange("p t d -> p (t d)").bitcast(I32))
-
-        def load_k_scales(r):
+        def load_plane(j):
+            which, r = divmod(j, 4)
             nc.sync.dma_start(
-                out=k_plane[r:P:32, :].bitcast(I32).rearrange("q (e c) -> q e c", e=E),
-                in_=wk_scales.rearrange("e s (q r) c -> r q (e s) c", r=4)[r].bitcast(I32),
+                out=kv_plane[which * V_ROW + r:P:32, :].bitcast(I32).rearrange("q (e c) -> q e c", e=E),
+                in_=(wk_scales, wv_scales)[which].rearrange("e s (q r) c -> r q (e s) c", r=4)[r].bitcast(I32),
             )
-
-        def load_v_scales(four, q):
-            nc.sync.dma_start(
-                out=v_plane[32 * q:32 * q + 16, four * K:(four + 1) * K].bitcast(I32),
-                in_=wv_scales[4 * four:4 * four + 4, 0, 4 * q:4 * q + 4, :].bitcast(I32),
-            )
-
-        def load_small(which, *where):
-            if which == "d":
-                load_d_scales(nc.sync, 0, *where)
-            elif which == "k":
-                load_k_scales(*where)
-            elif which == "v":
-                load_v_scales(*where)
-            else:
-                nc.sync.dma_start(pos_sb[where[0]][:], (pos1, pos2, pos3)[where[0]])
 
         k_codes = {}
         v_codes = {}
 
-        def load_kv(first, last, b0, b1):
+        def load_k(first, last):
             n = last - first
-            width = (b1 - b0) * P
-            k_tile = keep.tile([P, n * width * 2], U8, name="k_codes%d_%d" % (first, b0), align_bytes=64)
-            v_tile = keep.tile([P, n * width * 4], U8, name="v_codes%d_%d" % (first, b0), align_bytes=64)
+            k_tile = keep.tile([P, n * K * 2], U8, name="k_codes%d" % first, align_bytes=64)
             nc.sync.dma_start(
                 out=k_tile[:].bitcast(I32).rearrange("p (e c) -> p e c", e=n),
-                in_=wk_words[first:last].rearrange("e s p c -> p (e s) c")[:, :, b0 * 2 * P:b1 * 2 * P].bitcast(I32),
-            )
-            nc.sync.dma_start(
-                out=v_tile[:].bitcast(I32).rearrange("p (e c) -> p e c", e=n),
-                in_=wv_words[first:last].rearrange("e s p c d -> p (e s) (c d)")[:, :, b0 * 4 * P:b1 * 4 * P].bitcast(I32),
+                in_=wk_words.rearrange("e s p c -> p (e s) c").bitcast(I32)[:, first:last, :],
             )
             for e in range(first, last):
-                for b in range(b0, b1):
-                    col = (e - first) * width + (b - b0) * P
-                    k_codes[e, b] = k_tile[:, 2 * col:2 * (col + P)]
-                    v_codes[e, b] = v_tile[:, 4 * col:4 * (col + P)]
+                k_codes[e] = k_tile[:, (e - first) * 2 * K:(e - first + 1) * 2 * K]
+
+        def load_v(first, last, b0, b1):
+            n = last - first
+            width = (b1 - b0) * P
+            v_tile = keep.tile([P, n * width * 4], U8, name="v_codes%d_%d" % (first, b0), align_bytes=64)
+            nc.sync.dma_start(
+                out=v_tile[:].bitcast(I32).rearrange("p (e c) -> p e c", e=n),
+                in_=wv_words.rearrange("e s p c d -> p (e s) (c d)").bitcast(I32)[:, first:last, b0 * P:b1 * P],
+            )
+            for e in range(first, last):
+                v_codes[e, b0] = v_tile[:, (e - first) * 4 * width:(e - first + 1) * 4 * width]
 
         raw = {}
 
-        def load_q(e):
-            raw[e] = ring.tile([P, 4, K], F32, name="raw", tag="raw", bufs=6)
-            nc.sync.dma_start(out=raw[e][:], in_=wq[e].rearrange("(p j) c -> p j c", j=4))
+        def load_q(e, b0, b1, start):
+            raw[e, b0] = landing.tile([P, 4, (b1 - b0) * P], F32, name="raw%d_%d" % (e, b0), offset=start)
+            nc.sync.dma_start(out=raw[e, b0][:], in_=wq[e].rearrange("(p j) c -> p j c", j=4)[:, :, b0 * P:b1 * P])
 
         def cast_on_scalar(grouped, rows):
             nc.scalar.copy(grouped.rearrange("p (c i) j -> p c j i", i=4), rows.rearrange("p j (c i) -> p c j i", i=4))
@@ -137,120 +120,155 @@ def tile_moe_qkb_kernel(
         q_codes = {}
         q_plane = {}
 
-        def quantize_q(e, first, last, copy):
-            width = (last - first) * P
-            grouped = ring.tile([P, width, 4], BF16, name="grouped", tag="grouped", bufs=7, align_bytes=64)
-            copy(grouped[:], raw[e][:, :, first * P:last * P])
-            codes = keep.tile([P, width], U32, name="q_codes%d_%d" % (e, first), align_bytes=64)
-            plane = keep.tile([P, width], U8, name="q_plane%d_%d" % (e, first), align_bytes=64)
+        def quantize_q(first, last, b0, grouped, copy):
+            width = grouped.shape[1]
+            each = width // (last - first)
+            for e in range(first, last):
+                copy(grouped[:, (e - first) * each:(e - first + 1) * each, :], raw[e, b0][:])
+            tag = "whole" if each == K else "band"
+            codes = ring.tile([P, width], U32, name="q_codes", tag="q_codes_" + tag, bufs=6, align_bytes=64)
+            plane = ring.tile([P, width], U8, name="q_plane", tag="q_plane_" + tag, bufs=6, align_bytes=64)
             nc.vector.quantize_mx(
                 out=codes[:].bitcast(FP8X4), scales=plane[:], in_=grouped[:].rearrange("p c j -> p (c j)"),
             )
-            for b in range(first, last):
-                cols = slice((b - first) * P, (b - first + 1) * P)
-                q_codes[e, b] = codes[:, cols]
-                q_plane[e, b] = plane[:, cols]
+            for e in range(first, last):
+                q_codes[e, b0] = codes[:, (e - first) * each:(e - first + 1) * each]
+                q_plane[e, b0] = plane[:, (e - first) * each:(e - first + 1) * each]
 
-        def gather_words(i, u):
+        g_words = {}
+        g_scales = {}
+
+        def gather_words(i, u, pool, **where):
+            g_words[i, u] = pool.tile([P, GATHER], U32, name="g_words%d_%d" % (i, u), align_bytes=64, **where)
             nc.vector.tensor_copy(
-                g_words[i][:, u * GATHER:(u + 1) * GATHER],
+                g_words[i, u][:],
                 d_words[i][:].bitcast(U32).indirect(offs_sb[:, u * GATHER // 16:(u + 1) * GATHER // 16]),
             )
 
-        def gather_scales(i, u):
+        def gather_scales(i, u, pool, **where):
+            g_scales[i, u] = pool.tile([P, GATHER], U8, name="g_scales%d_%d" % (i, u), align_bytes=64, **where)
             nc.vector.tensor_copy(
-                g_scales[i][:, u * GATHER:(u + 1) * GATHER],
+                g_scales[i, u][:],
                 d_scales[i][:].indirect(offs_sb[:, u * GATHER // 16:(u + 1) * GATHER // 16]),
             )
 
-        def multiply(acc, b, e):
-            slots = slice(e * C, (e + 1) * C)
-            four, j = divmod(e, 4)
+        def multiply(acc, e, b0, b1):
+            u, place = divmod(e, EARLY)
+            slots = slice(place * C, (place + 1) * C)
+            cols = slice(e * K + b0 * P, e * K + b1 * P)
             nc.tensor.matmul_mx(
-                out=acc, lhsT=g_words[1][:, slots].bitcast(FP8X4), lhsT_scale=g_scales[1][:, slots],
-                rhs=k_codes[e, b].bitcast(FP4X4),
-                rhs_scale=k_plane[:, e * K + b * P:e * K + (b + 1) * P], start=True, stop=False,
+                out=acc, lhsT=g_words[1, u][:, slots].bitcast(FP8X4), lhsT_scale=g_scales[1, u][:, slots],
+                rhs=k_codes[e][:, 2 * b0 * P:2 * b1 * P].bitcast(FP4X4),
+                rhs_scale=kv_plane[:, cols], start=True, stop=False,
             )
             nc.tensor.matmul_mx(
-                out=acc, lhsT=g_words[2][:, slots].bitcast(FP8X4), lhsT_scale=g_scales[2][:, slots],
-                rhs=v_codes[e, b].bitcast(FP8X4),
-                rhs_scale=v_plane[4 * j:P, four * K + b * P:four * K + (b + 1) * P], start=False, stop=False,
+                out=acc, lhsT=g_words[2, u][:, slots].bitcast(FP8X4), lhsT_scale=g_scales[2, u][:, slots],
+                rhs=v_codes[e, b0].bitcast(FP8X4), rhs_scale=kv_plane[V_ROW:P, cols], start=False, stop=False,
             )
             nc.tensor.matmul_mx(
-                out=acc, lhsT=g_words[0][:, slots].bitcast(FP8X4), lhsT_scale=g_scales[0][:, slots],
-                rhs=q_codes[e, b].bitcast(FP8X4), rhs_scale=q_plane[e, b], start=False, stop=True,
+                out=acc, lhsT=g_words[0, u][:, slots].bitcast(FP8X4), lhsT_scale=g_scales[0, u][:, slots],
+                rhs=q_codes[e, b0].bitcast(FP8X4), rhs_scale=q_plane[e, b0], start=False, stop=True,
             )
 
-        def slots_of(b, first, last):
-            by_slot = psum.tile([P, K], F32, name="by_slot", tag="by_slot")
-            for e in range(first, last):
-                multiply(by_slot[:, (e - first) * P:(e - first + 1) * P], b, e)
-            gated = ring.tile([P, K], F32, name="gated", tag="gated", bufs=4)
-            for e in range(first, last):
-                cols = slice((e - first) * P, (e - first + 1) * P)
-                nc.scalar.activation(gated[:, cols], by_slot[:, cols], COPY, scale=gate_cols[:, e:e + 1])
+        gated = {}
+
+        def turn_back(b, first, last):
             by_channel = psum.tile([P, K], F32, name="by_channel", tag="by_channel")
             for e in range(first, last):
-                cols = slice((e - first) * P, (e - first + 1) * P)
-                nc.tensor.transpose(by_channel[:, cols], gated[:, cols], identity[:])
+                nc.tensor.transpose(by_channel[:, (e - first) * C:(e - first + 1) * C], gated[e, b], identity[:])
             nc.scalar.copy(dx[b][:, first * C:last * C], by_channel[:, 0:(last - first) * C])
 
-        def combine(b, stores):
-            sums = [ring.tile([P, T], F32, name="sums", tag="sums", bufs=4) for step in range(2)]
-            sums.append(ring.tile([P, T], F32, name="result", tag="result", bufs=4))
-            for step in range(3):
-                for th in range(2):
-                    picked = dx[b][:].indirect(pos_sb[step][:, th * 16:(th + 1) * 16])
-                    cols = slice(th * (T // 2), (th + 1) * (T // 2))
-                    if step == 0:
-                        nc.vector.tensor_copy(sums[0][:, cols], picked)
-                    else:
-                        nc.vector.tensor_tensor(sums[step][:, cols], picked, sums[step - 1][:, cols], ADD)
-            for piece in range(stores):
-                cols = slice(piece * (T // stores), (piece + 1) * (T // stores))
-                nc.sync.dma_start(out=out[b * P:(b + 1) * P, cols], in_=sums[2][:, cols])
+        def whole_expert(e):
+            by_slot = psum.tile([P, K], F32, name="by_slot", tag="by_slot")
+            multiply(by_slot[:], e, 0, BANDS)
+            rows = keep.tile([P, K], F32, name="gated%d" % e)
+            nc.scalar.activation(rows[:], by_slot[:], COPY, scale=gate_cols[:, e:e + 1])
+            for b in range(BANDS):
+                gated[e, b] = rows[:, b * P:(b + 1) * P]
 
-        small = [("d", r) for r in range(4)]
-        small += [("k", r) for r in range(4)]
-        small += [("v", four, q) for four in range(E // 4) for q in range(4)]
-        small += [("pos", i) for i in range(2)]
-        kv_after = {7: (0, EARLY, 0, BLOCKS), 8: FIRST_GROUPS[0] + (0, 1), 9: (FIRST_GROUPS[1][0], E, 0, 1)}
+        def band_of(b, first, last):
+            by_slot = psum.tile([P, K], F32, name="by_slot", tag="by_slot")
+            for e in range(first, last):
+                multiply(by_slot[:, (e - first) * P:(e - first + 1) * P], e, b, b + 1)
+            rows = ring.tile([P, 2 * P], F32, name="gated", tag="gated", bufs=3)
+            for e in range(first, last):
+                cols = slice((e - first) * P, (e - first + 1) * P)
+                nc.scalar.activation(rows[:, cols], by_slot[:, cols], COPY, scale=gate_cols[:, e:e + 1])
+                gated[e, b] = rows[:, cols]
+            turn_back(b, first, last)
+
+        sums = {}
+
+        def combine_step(b, step, part, parts, pool, **where):
+            width = T // parts
+            sums[step, part] = pool.tile([P, width], F32, name="sums%d_%d_%d" % (b, step, part), align_bytes=64, **where)
+            picked = dx[b][:].indirect(pos_sb[step][:, part * width // 16:(part + 1) * width // 16])
+            if step == 0:
+                nc.vector.tensor_copy(sums[step, part][:], picked)
+            else:
+                nc.vector.tensor_tensor(sums[step, part][:], picked, sums[step - 1, part][:], ADD)
+            if step == 2:
+                nc.sync.dma_start(out=out[b * P:(b + 1) * P, part * width:(part + 1) * width], in_=sums[step, part][:])
+
+        def load_d_words(i):
+            src = (dq_words, dk_words, dv_words)[i]
+            nc.sync.dma_start(out=d_words[i][:, 0:T], in_=src[0].rearrange("p t d -> p (t d)").bitcast(I32))
+
         nc.sync.dma_start(offs_sb[:], offs)
-        for e in range(E):
-            if e < 3:
-                load_d_words(e)
-            load_q(e)
-            for item in small[2 * e:2 * e + 2]:
-                load_small(*item)
-            if e in kv_after:
-                load_kv(*kv_after[e])
-            if e == 9:
-                load_small("pos", 2)
-        for b in range(1, BLOCKS):
-            for first, last in LATER_GROUPS:
-                load_kv(first, last, b, b + 1)
+        load_d_words(0)
+        load_d_scales(0)
+        load_q(0, 0, BANDS, 0)
+        load_d_words(1)
+        load_d_words(2)
+        load_d_scales(1)
+        load_q(1, 0, BANDS, 2 * STAGE_BYTES)
+        load_d_scales(2)
+        planes_after = {2: (0, 1), 3: (2, 3, 4, 5), 4: (6, 7)}
+        kv_after = {4: (0, 1), 5: (2, 3, 4, 5)}
+        for e in range(2, EARLY):
+            load_q(e, 0, BANDS, e * 2 * STAGE_BYTES)
+            for j in planes_after.get(e, ()):
+                load_plane(j)
+            for x in kv_after.get(e, ()):
+                load_k(x, x + 1)
+                load_v(x, x + 1, 0, BANDS)
+        load_k(EARLY, E)
+        for i in range(3):
+            nc.sync.dma_start(pos_sb[i][:], (pos1, pos2, pos3)[i])
+        piece = 0
+        for b in range(BANDS):
+            load_v(EARLY, E, b, b + 1)
+            for e in range(EARLY, E):
+                load_q(e, b, b + 1, piece * 2 * PIECE_BYTES)
+                piece = piece + 1
 
         for i in range(3):
-            for u in range(S // GATHER):
-                gather_words(i, u)
-        for i in range(3):
-            for u in range(S // GATHER):
-                gather_scales(i, u)
+            gather_words(i, 0, keep)
+            gather_scales(i, 0, keep)
 
         for e in range(EARLY):
-            quantize_q(e, 0, BLOCKS, cast_on_scalar)
-        for b in range(BLOCKS):
-            slots_of(b, 0, EARLY)
-        for first, last in FIRST_GROUPS[:-1]:
-            for e in range(first, last):
-                quantize_q(e, 0, BLOCKS, cast_on_scalar if e < VECTOR_FROM else cast_on_vector)
-            slots_of(0, first, last)
-        quantize_q(E - 1, 0, 1, cast_on_vector)
-        slots_of(0, *FIRST_GROUPS[-1])
-        quantize_q(E - 1, 1, 2, cast_on_vector)
-        quantize_q(E - 1, 2, BLOCKS, cast_on_vector)
-        combine(0, 1)
-        for b in range(1, BLOCKS):
-            for first, last in LATER_GROUPS:
-                slots_of(b, first, last)
-            combine(b, 2 if b == BLOCKS - 1 else 1)
+            grouped = shared.tile([P, K, 4], BF16, name="grouped%d" % e, align_bytes=64, offset=e * STAGE_BYTES)
+            quantize_q(e, e + 1, 0, grouped, cast_on_scalar)
+            if e % 2 == 1:
+                gather_words(e // 2, 1, shared, offset=e * STAGE_BYTES)
+                gather_scales(e // 2, 1, shared, offset=e * STAGE_BYTES + 4 * GATHER)
+            whole_expert(e)
+            if e == TRIO - 1:
+                for b in range(BANDS):
+                    turn_back(b, 0, TRIO)
+        duo = 0
+        for b in range(BANDS):
+            turn_back(b, TRIO, EARLY)
+            for first in range(EARLY, E, 2):
+                start = EARLY * STAGE_BYTES + duo * 2 * PIECE_BYTES
+                grouped = shared.tile([P, 2 * P, 4], BF16, name="duo%d" % duo, align_bytes=64, offset=start)
+                quantize_q(first, first + 2, b, grouped, cast_on_scalar)
+                if duo >= LAG:
+                    combine_step(*divmod(duo - LAG, 3), 0, 1, shared, offset=start)
+                duo = duo + 1
+                band_of(b, first, first + 2)
+        for m in range(3 * BANDS - LAG, 3 * BANDS - 3):
+            combine_step(*divmod(m, 3), 0, 1, keep)
+        for step in range(3):
+            for part in range(2):
+                combine_step(BANDS - 1, step, part, 2, keep)

@@ -21,13 +21,16 @@ C = 128
 S = E * C
 K = 512
 BANDS = K // P
-TRIO = 3
-EARLY = 6
-GATHER = EARLY * C
-WINDOW = 2 * T
+QUAD = 4
+EARLY = 9
+GATHER = QUAD * C
+WINDOW = T + T // 2
+RAW_BYTES = 4 * K * 4
+LATE = E - EARLY
+VECTOR_FROM = 7
+GATED_HOME = 4
 STAGE_BYTES = 4 * K * 2
 PIECE_BYTES = 4 * P * 2
-LAG = 4
 V_ROW = 4
 FLOPS = 2 * 3 * 512 * K * S
 
@@ -94,10 +97,10 @@ def tile_moe_qkb_kernel(
             for e in range(first, last):
                 k_codes[e] = k_tile[:, (e - first) * 2 * K:(e - first + 1) * 2 * K]
 
-        def load_v(first, last, b0, b1):
+        def load_v(first, last, b0, b1, pool, **where):
             n = last - first
             width = (b1 - b0) * P
-            v_tile = keep.tile([P, n * width * 4], U8, name="v_codes%d_%d" % (first, b0), align_bytes=64)
+            v_tile = pool.tile([P, n * width * 4], U8, name="v_codes%d_%d" % (first, b0), align_bytes=64, **where)
             nc.sync.dma_start(
                 out=v_tile[:].bitcast(I32).rearrange("p (e c) -> p e c", e=n),
                 in_=wv_words.rearrange("e s p c d -> p (e s) (c d)").bitcast(I32)[:, first:last, b0 * P:b1 * P],
@@ -153,7 +156,7 @@ def tile_moe_qkb_kernel(
             )
 
         def multiply(acc, e, b0, b1):
-            u, place = divmod(e, EARLY)
+            u, place = divmod(e, QUAD)
             slots = slice(place * C, (place + 1) * C)
             cols = slice(e * K + b0 * P, e * K + b1 * P)
             nc.tensor.matmul_mx(
@@ -181,94 +184,122 @@ def tile_moe_qkb_kernel(
         def whole_expert(e):
             by_slot = psum.tile([P, K], F32, name="by_slot", tag="by_slot")
             multiply(by_slot[:], e, 0, BANDS)
-            rows = keep.tile([P, K], F32, name="gated%d" % e)
+            rows = landing.tile([P, K], F32, name="gated%d" % e, offset=GATED_HOME * RAW_BYTES + e * 4 * K)
             nc.scalar.activation(rows[:], by_slot[:], COPY, scale=gate_cols[:, e:e + 1])
             for b in range(BANDS):
                 gated[e, b] = rows[:, b * P:(b + 1) * P]
 
-        def band_of(b, first, last):
+        def stage_of(b):
+            return EARLY * STAGE_BYTES + b * LATE * PIECE_BYTES
+
+        def late_band(b):
             by_slot = psum.tile([P, K], F32, name="by_slot", tag="by_slot")
-            for e in range(first, last):
-                multiply(by_slot[:, (e - first) * P:(e - first + 1) * P], e, b, b + 1)
-            rows = ring.tile([P, 2 * P], F32, name="gated", tag="gated", bufs=3)
-            for e in range(first, last):
-                cols = slice((e - first) * P, (e - first + 1) * P)
+            for e in range(EARLY, E):
+                multiply(by_slot[:, (e - EARLY) * P:(e - EARLY + 1) * P], e, b, b + 1)
+            rows = shared.tile([P, LATE * P], F32, name="gated_late%d" % b, align_bytes=64, offset=stage_of(b + 1))
+            for e in range(EARLY, E):
+                cols = slice((e - EARLY) * P, (e - EARLY + 1) * P)
                 nc.scalar.activation(rows[:, cols], by_slot[:, cols], COPY, scale=gate_cols[:, e:e + 1])
                 gated[e, b] = rows[:, cols]
-            turn_back(b, first, last)
+            turn_back(b, 2 * QUAD, E)
 
         sums = {}
 
-        def combine_step(b, step, part, parts, pool, **where):
-            width = T // parts
-            sums[step, part] = pool.tile([P, width], F32, name="sums%d_%d_%d" % (b, step, part), align_bytes=64, **where)
-            picked = dx[b][:].indirect(pos_sb[step][:, part * width // 16:(part + 1) * width // 16])
+        def combine_step(b, step, half, pool, **where):
+            width = T // 2
+            sums[step, half] = pool.tile([P, width], F32, name="sums%d_%d_%d" % (b, step, half), align_bytes=64, **where)
+            picked = dx[b][:].indirect(pos_sb[step][:, half * width // 16:(half + 1) * width // 16])
             if step == 0:
-                nc.vector.tensor_copy(sums[step, part][:], picked)
+                nc.vector.tensor_copy(sums[step, half][:], picked)
             else:
-                nc.vector.tensor_tensor(sums[step, part][:], picked, sums[step - 1, part][:], ADD)
+                nc.vector.tensor_tensor(sums[step, half][:], picked, sums[step - 1, half][:], ADD)
             if step == 2:
-                nc.sync.dma_start(out=out[b * P:(b + 1) * P, part * width:(part + 1) * width], in_=sums[step, part][:])
+                nc.sync.dma_start(out=out[b * P:(b + 1) * P, half * width:(half + 1) * width], in_=sums[step, half][:])
 
         def load_d_words(i):
             src = (dq_words, dk_words, dv_words)[i]
             nc.sync.dma_start(out=d_words[i][:, 0:T], in_=src[0].rearrange("p t d -> p (t d)").bitcast(I32))
 
+        def load_whole(e):
+            load_q(e, 0, BANDS, e * RAW_BYTES)
+
+        def load_band(b):
+            load_v(EARLY, E, b, b + 1, landing, offset=b * RAW_BYTES + LATE * RAW_BYTES // BANDS)
+            for e in range(EARLY, E):
+                load_q(e, b, b + 1, b * RAW_BYTES + (e - EARLY) * RAW_BYTES // BANDS)
+
         nc.sync.dma_start(offs_sb[:], offs)
         load_d_words(0)
-        load_d_scales(0)
-        load_q(0, 0, BANDS, 0)
+        load_whole(0)
         load_d_words(1)
+        load_d_scales(0)
         load_d_words(2)
+        load_whole(1)
         load_d_scales(1)
-        load_q(1, 0, BANDS, 2 * STAGE_BYTES)
+        load_whole(2)
         load_d_scales(2)
-        planes_after = {2: (0, 1), 3: (2, 3, 4, 5), 4: (6, 7)}
-        kv_after = {4: (0, 1), 5: (2, 3, 4, 5)}
-        for e in range(2, EARLY):
-            load_q(e, 0, BANDS, e * 2 * STAGE_BYTES)
-            for j in planes_after.get(e, ()):
-                load_plane(j)
-            for x in kv_after.get(e, ()):
-                load_k(x, x + 1)
-                load_v(x, x + 1, 0, BANDS)
-        load_k(EARLY, E)
+        load_whole(3)
+        for j in range(0, 2):
+            load_plane(j)
+        load_whole(4)
+        for j in range(2, 5):
+            load_plane(j)
+        load_k(0, 2)
+        load_v(0, 2, 0, BANDS, keep)
+        for j in range(5, 8):
+            load_plane(j)
+        for e in range(5, EARLY - 1):
+            load_whole(e)
+            load_k(2 * e - 8, 2 * e - 6)
+            load_v(2 * e - 8, 2 * e - 6, 0, BANDS, keep)
+        load_whole(EARLY - 1)
+        load_k(EARLY - 1, E)
+        load_v(EARLY - 1, EARLY, 0, BANDS, keep)
         for i in range(3):
             nc.sync.dma_start(pos_sb[i][:], (pos1, pos2, pos3)[i])
-        piece = 0
-        for b in range(BANDS):
-            load_v(EARLY, E, b, b + 1)
-            for e in range(EARLY, E):
-                load_q(e, b, b + 1, piece * 2 * PIECE_BYTES)
-                piece = piece + 1
 
-        for i in range(3):
-            gather_words(i, 0, keep)
-            gather_scales(i, 0, keep)
+        for u in range(E // QUAD):
+            gather_words(0, u, keep)
+        gather_words(1, 0, keep)
+        gather_scales(0, 0, keep)
+        gather_words(2, 0, keep)
+        gather_scales(1, 0, keep)
+        gather_scales(2, 0, keep)
 
         for e in range(EARLY):
             grouped = shared.tile([P, K, 4], BF16, name="grouped%d" % e, align_bytes=64, offset=e * STAGE_BYTES)
-            quantize_q(e, e + 1, 0, grouped, cast_on_scalar)
-            if e % 2 == 1:
-                gather_words(e // 2, 1, shared, offset=e * STAGE_BYTES)
-                gather_scales(e // 2, 1, shared, offset=e * STAGE_BYTES + 4 * GATHER)
-            whole_expert(e)
-            if e == TRIO - 1:
+            quantize_q(e, e + 1, 0, grouped, cast_on_scalar if e < VECTOR_FROM else cast_on_vector)
+            if 1 <= e <= 6:
+                u, i = divmod(e - 1, 3)
+                if i > 0:
+                    gather_words(i, 1 + u, shared, offset=e * STAGE_BYTES)
+                gather_scales(i, 1 + u, shared, offset=e * STAGE_BYTES + 4 * GATHER)
+            if e >= QUAD:
+                whole_expert(e - QUAD)
+            if e == 2 * QUAD - 1:
                 for b in range(BANDS):
-                    turn_back(b, 0, TRIO)
-        duo = 0
+                    turn_back(b, 0, QUAD)
+        for e in range(EARLY - QUAD, EARLY):
+            whole_expert(e)
         for b in range(BANDS):
-            turn_back(b, TRIO, EARLY)
-            for first in range(EARLY, E, 2):
-                start = EARLY * STAGE_BYTES + duo * 2 * PIECE_BYTES
-                grouped = shared.tile([P, 2 * P, 4], BF16, name="duo%d" % duo, align_bytes=64, offset=start)
-                quantize_q(first, first + 2, b, grouped, cast_on_scalar)
-                if duo >= LAG:
-                    combine_step(*divmod(duo - LAG, 3), 0, 1, shared, offset=start)
-                duo = duo + 1
-                band_of(b, first, first + 2)
-        for m in range(3 * BANDS - LAG, 3 * BANDS - 3):
-            combine_step(*divmod(m, 3), 0, 1, keep)
+            load_band(b)
+
+        for b in range(BANDS):
+            turn_back(b, QUAD, 2 * QUAD)
+            for e in range(EARLY, E):
+                start = stage_of(b) + (e - EARLY) * PIECE_BYTES
+                grouped = shared.tile([P, P, 4], BF16, name="piece%d_%d" % (b, e), align_bytes=64, offset=start)
+                quantize_q(e, e + 1, b, grouped, cast_on_scalar)
+                if b > 0 and e == EARLY:
+                    combine_step(b - 1, 0, 0, shared, offset=start)
+                    combine_step(b - 1, 0, 1, ring, tag="sums", bufs=6)
+                if b > 0 and e == EARLY + 1:
+                    combine_step(b - 1, 1, 0, shared, offset=start)
+                if b > 0 and e == EARLY + 2:
+                    combine_step(b - 1, 1, 1, shared, offset=start)
+                    combine_step(b - 1, 2, 0, ring, tag="sums", bufs=6)
+                    combine_step(b - 1, 2, 1, ring, tag="sums", bufs=6)
+            late_band(b)
         for step in range(3):
-            for part in range(2):
-                combine_step(BANDS - 1, step, part, 2, keep)
+            for half in range(2):
+                combine_step(BANDS - 1, step, half, ring, tag="sums", bufs=6)

@@ -22,15 +22,14 @@ S = E * C
 K = 512
 BANDS = K // P
 QUAD = 4
-EARLY = 9
+QUADS = E // QUAD
 GATHER = QUAD * C
 WINDOW = T + T // 2
 RAW_BYTES = 4 * K * 4
-LATE = E - EARLY
-VECTOR_FROM = 7
-GATED_HOME = 4
+LANDINGS = 6
 STAGE_BYTES = 4 * K * 2
-PIECE_BYTES = 4 * P * 2
+REST = K - P
+BANK_BYTES = 2048
 V_ROW = 4
 FLOPS = 2 * 3 * 512 * K * S
 
@@ -45,7 +44,7 @@ def tile_moe_qkb_kernel(
         shared = ctx.enter_context(tc.tile_pool(name="shared", bufs=1))
         landing = ctx.enter_context(tc.tile_pool(name="landing", bufs=1))
         ring = ctx.enter_context(tc.tile_pool(name="ring", bufs=1))
-        psum = ctx.enter_context(tc.psum_pool(name="psum", bufs=4))
+        psum = ctx.enter_context(tc.psum_pool(name="psum", bufs=1))
 
         offs_sb = keep.tile([P, S // 16], U16, name="offs_sb")
         pos_sb = [keep.tile([P, T // 16], U16, name="pos_sb%d" % i) for i in range(3)]
@@ -60,11 +59,11 @@ def tile_moe_qkb_kernel(
         for i in range(3):
             nc.vector.memset(d_scales[i][:].bitcast(I32), 0)
         for i in range(3):
-            nc.gpsimd.memset(d_words[i][:, T:WINDOW], 0)
+            nc.vector.memset(d_words[i][:, T:WINDOW], 0)
         nc.vector.memset(kv_plane[:].bitcast(I32), 0)
+        make_identity(nc, identity[:])
         nc.gpsimd.memset(gate_rows[:], 0.0)
         nc.gpsimd.dma_start(out=gate_rows[0:E, :], in_=gate[0].rearrange("(e u) -> e u", u=C))
-        make_identity(nc, identity[:])
 
         def load_d_scales(i):
             for r in range(4):
@@ -73,7 +72,7 @@ def tile_moe_qkb_kernel(
                     in_=(dq_scales, dk_scales, dv_scales)[i].rearrange("s (q r) t -> r (s q) t", r=4)[r].bitcast(I32),
                 )
 
-        gate_bank = psum.tile([P, K], F32, name="gate_bank", tag="by_channel")
+        gate_bank = psum.tile([P, K], F32, name="gate_bank", offset=7 * BANK_BYTES)
         nc.tensor.transpose(gate_bank[:, 0:P], gate_rows[:], identity[:])
         nc.scalar.activation(gate_cols[:], gate_bank[:, 0:E], COPY)
 
@@ -87,57 +86,37 @@ def tile_moe_qkb_kernel(
         k_codes = {}
         v_codes = {}
 
-        def load_k(first, last):
-            n = last - first
-            k_tile = keep.tile([P, n * K * 2], U8, name="k_codes%d" % first, align_bytes=64)
-            nc.sync.dma_start(
-                out=k_tile[:].bitcast(I32).rearrange("p (e c) -> p e c", e=n),
-                in_=wk_words.rearrange("e s p c -> p (e s) c").bitcast(I32)[:, first:last, :],
-            )
-            for e in range(first, last):
-                k_codes[e] = k_tile[:, (e - first) * 2 * K:(e - first + 1) * 2 * K]
-
-        def load_v(first, last, b0, b1, pool, **where):
-            n = last - first
+        def load_kv(u, b0, b1, k_start, v_start):
+            first = QUAD * u
             width = (b1 - b0) * P
-            v_tile = pool.tile([P, n * width * 4], U8, name="v_codes%d_%d" % (first, b0), align_bytes=64, **where)
+            k_tile = landing.tile([P, QUAD * width * 2], U8, name="k_codes%d_%d" % (u, b0), align_bytes=64, offset=k_start)
+            v_tile = landing.tile([P, QUAD * width * 4], U8, name="v_codes%d_%d" % (u, b0), align_bytes=64, offset=v_start)
             nc.sync.dma_start(
-                out=v_tile[:].bitcast(I32).rearrange("p (e c) -> p e c", e=n),
-                in_=wv_words.rearrange("e s p c d -> p (e s) (c d)").bitcast(I32)[:, first:last, b0 * P:b1 * P],
+                out=k_tile[:].bitcast(I32).rearrange("p (e c) -> p e c", e=QUAD),
+                in_=wk_words.rearrange("e s p c -> p (e s) c").bitcast(I32)[:, first:first + QUAD, b0 * P // 2:b1 * P // 2],
             )
-            for e in range(first, last):
-                v_codes[e, b0] = v_tile[:, (e - first) * 4 * width:(e - first + 1) * 4 * width]
+            nc.sync.dma_start(
+                out=v_tile[:].bitcast(I32).rearrange("p (e c) -> p e c", e=QUAD),
+                in_=wv_words.rearrange("e s p c d -> p (e s) (c d)").bitcast(I32)[:, first:first + QUAD, b0 * P:b1 * P],
+            )
+            for place in range(QUAD):
+                k_codes[first + place, b0] = k_tile[:, place * 2 * width:(place + 1) * 2 * width]
+                v_codes[first + place, b0] = v_tile[:, place * 4 * width:(place + 1) * 4 * width]
 
         raw = {}
 
-        def load_q(e, b0, b1, start):
-            raw[e, b0] = landing.tile([P, 4, (b1 - b0) * P], F32, name="raw%d_%d" % (e, b0), offset=start)
-            nc.sync.dma_start(out=raw[e, b0][:], in_=wq[e].rearrange("(p j) c -> p j c", j=4)[:, :, b0 * P:b1 * P])
+        def load_q(e):
+            raw[e] = landing.tile([P, 4, K], F32, name="raw%d" % e, offset=(e % LANDINGS) * RAW_BYTES)
+            nc.sync.dma_start(out=raw[e][:], in_=wq[e].rearrange("(p j) c -> p j c", j=4))
 
-        def cast_on_scalar(grouped, rows):
+        def round_and_interleave(grouped, rows):
             nc.scalar.copy(grouped.rearrange("p (c i) j -> p c j i", i=4), rows.rearrange("p j (c i) -> p c j i", i=4))
 
-        def cast_on_vector(grouped, rows):
-            nc.vector.tensor_copy(grouped.rearrange("p (c i) j -> p c j i", i=4), rows.rearrange("p j (c i) -> p c j i", i=4))
+        def quantize(codes, plane, grouped):
+            nc.vector.quantize_mx(out=codes.bitcast(FP8X4), scales=plane, in_=grouped.rearrange("p c j -> p (c j)"))
 
         q_codes = {}
         q_plane = {}
-
-        def quantize_q(first, last, b0, grouped, copy):
-            width = grouped.shape[1]
-            each = width // (last - first)
-            for e in range(first, last):
-                copy(grouped[:, (e - first) * each:(e - first + 1) * each, :], raw[e, b0][:])
-            tag = "whole" if each == K else "band"
-            codes = ring.tile([P, width], U32, name="q_codes", tag="q_codes_" + tag, bufs=6, align_bytes=64)
-            plane = ring.tile([P, width], U8, name="q_plane", tag="q_plane_" + tag, bufs=6, align_bytes=64)
-            nc.vector.quantize_mx(
-                out=codes[:].bitcast(FP8X4), scales=plane[:], in_=grouped[:].rearrange("p c j -> p (c j)"),
-            )
-            for e in range(first, last):
-                q_codes[e, b0] = codes[:, (e - first) * each:(e - first + 1) * each]
-                q_plane[e, b0] = plane[:, (e - first) * each:(e - first + 1) * each]
-
         g_words = {}
         g_scales = {}
 
@@ -161,7 +140,7 @@ def tile_moe_qkb_kernel(
             cols = slice(e * K + b0 * P, e * K + b1 * P)
             nc.tensor.matmul_mx(
                 out=acc, lhsT=g_words[1, u][:, slots].bitcast(FP8X4), lhsT_scale=g_scales[1, u][:, slots],
-                rhs=k_codes[e][:, 2 * b0 * P:2 * b1 * P].bitcast(FP4X4),
+                rhs=k_codes[e, b0].bitcast(FP4X4),
                 rhs_scale=kv_plane[:, cols], start=True, stop=False,
             )
             nc.tensor.matmul_mx(
@@ -175,39 +154,36 @@ def tile_moe_qkb_kernel(
 
         gated = {}
 
-        def turn_back(b, first, last):
-            by_channel = psum.tile([P, K], F32, name="by_channel", tag="by_channel")
-            for e in range(first, last):
-                nc.tensor.transpose(by_channel[:, (e - first) * C:(e - first + 1) * C], gated[e, b], identity[:])
-            nc.scalar.copy(dx[b][:, first * C:last * C], by_channel[:, 0:(last - first) * C])
+        def turn_back(b, u, bank):
+            by_channel = psum.tile([P, K], F32, name="by_channel%d_%d" % (b, u), offset=bank * BANK_BYTES)
+            for place in range(QUAD):
+                nc.tensor.transpose(by_channel[:, place * C:(place + 1) * C], gated[QUAD * u + place, b], identity[:])
+            nc.scalar.copy(dx[b][:, u * GATHER:(u + 1) * GATHER], by_channel[:])
 
         def whole_expert(e):
-            by_slot = psum.tile([P, K], F32, name="by_slot", tag="by_slot")
+            by_slot = psum.tile([P, K], F32, name="whole%d" % e, offset=(3 + e % 2) * BANK_BYTES)
             multiply(by_slot[:], e, 0, BANDS)
-            rows = landing.tile([P, K], F32, name="gated%d" % e, offset=GATED_HOME * RAW_BYTES + e * 4 * K)
+            rows = keep.tile([P, K], F32, name="gated%d" % e)
             nc.scalar.activation(rows[:], by_slot[:], COPY, scale=gate_cols[:, e:e + 1])
             for b in range(BANDS):
                 gated[e, b] = rows[:, b * P:(b + 1) * P]
 
-        def stage_of(b):
-            return EARLY * STAGE_BYTES + b * LATE * PIECE_BYTES
-
-        def late_band(b):
-            by_slot = psum.tile([P, K], F32, name="by_slot", tag="by_slot")
-            for e in range(EARLY, E):
-                multiply(by_slot[:, (e - EARLY) * P:(e - EARLY + 1) * P], e, b, b + 1)
-            rows = shared.tile([P, LATE * P], F32, name="gated_late%d" % b, align_bytes=64, offset=stage_of(b + 1))
-            for e in range(EARLY, E):
-                cols = slice((e - EARLY) * P, (e - EARLY + 1) * P)
+        def band_of_quad(b, u, bank):
+            by_slot = psum.tile([P, K], F32, name="by_slot%d_%d" % (b, u), offset=bank * BANK_BYTES)
+            for place in range(QUAD):
+                multiply(by_slot[:, place * P:(place + 1) * P], QUAD * u + place, b, b + 1)
+            rows = ring.tile([P, K], F32, name="gated", tag="gated", bufs=3)
+            for place in range(QUAD):
+                e = QUAD * u + place
+                cols = slice(place * P, (place + 1) * P)
                 nc.scalar.activation(rows[:, cols], by_slot[:, cols], COPY, scale=gate_cols[:, e:e + 1])
                 gated[e, b] = rows[:, cols]
-            turn_back(b, 2 * QUAD, E)
 
         sums = {}
 
-        def combine_step(b, step, half, pool, **where):
+        def combine_step(b, step, half):
             width = T // 2
-            sums[step, half] = pool.tile([P, width], F32, name="sums%d_%d_%d" % (b, step, half), align_bytes=64, **where)
+            sums[step, half] = ring.tile([P, width], F32, name="sums", tag="sums", bufs=10)
             picked = dx[b][:].indirect(pos_sb[step][:, half * width // 16:(half + 1) * width // 16])
             if step == 0:
                 nc.vector.tensor_copy(sums[step, half][:], picked)
@@ -220,86 +196,92 @@ def tile_moe_qkb_kernel(
             src = (dq_words, dk_words, dv_words)[i]
             nc.sync.dma_start(out=d_words[i][:, 0:T], in_=src[0].rearrange("p t d -> p (t d)").bitcast(I32))
 
-        def load_whole(e):
-            load_q(e, 0, BANDS, e * RAW_BYTES)
-
-        def load_band(b):
-            load_v(EARLY, E, b, b + 1, landing, offset=b * RAW_BYTES + LATE * RAW_BYTES // BANDS)
-            for e in range(EARLY, E):
-                load_q(e, b, b + 1, b * RAW_BYTES + (e - EARLY) * RAW_BYTES // BANDS)
-
         nc.sync.dma_start(offs_sb[:], offs)
         load_d_words(0)
-        load_whole(0)
+        load_q(0)
         load_d_words(1)
         load_d_scales(0)
         load_d_words(2)
-        load_whole(1)
+        load_q(1)
         load_d_scales(1)
-        load_whole(2)
+        load_q(2)
         load_d_scales(2)
-        load_whole(3)
-        for j in range(0, 2):
-            load_plane(j)
-        load_whole(4)
-        for j in range(2, 5):
-            load_plane(j)
-        load_k(0, 2)
-        load_v(0, 2, 0, BANDS, keep)
-        for j in range(5, 8):
-            load_plane(j)
-        for e in range(5, EARLY - 1):
-            load_whole(e)
-            load_k(2 * e - 8, 2 * e - 6)
-            load_v(2 * e - 8, 2 * e - 6, 0, BANDS, keep)
-        load_whole(EARLY - 1)
-        load_k(EARLY - 1, E)
-        load_v(EARLY - 1, EARLY, 0, BANDS, keep)
+        for e in range(3, LANDINGS):
+            load_q(e)
+            for j in range(3 * e - 9, min(3 * e - 6, 8)):
+                load_plane(j)
         for i in range(3):
             nc.sync.dma_start(pos_sb[i][:], (pos1, pos2, pos3)[i])
 
-        for u in range(E // QUAD):
+        for u in range(2):
             gather_words(0, u, keep)
-        gather_words(1, 0, keep)
-        gather_scales(0, 0, keep)
-        gather_words(2, 0, keep)
-        gather_scales(1, 0, keep)
-        gather_scales(2, 0, keep)
+        for i in range(3):
+            if i > 0:
+                for u in range(2):
+                    gather_words(i, u, keep)
+            for u in range(2):
+                gather_scales(i, u, keep)
 
-        for e in range(EARLY):
+        for e in range(QUAD):
             grouped = shared.tile([P, K, 4], BF16, name="grouped%d" % e, align_bytes=64, offset=e * STAGE_BYTES)
-            quantize_q(e, e + 1, 0, grouped, cast_on_scalar if e < VECTOR_FROM else cast_on_vector)
-            if 1 <= e <= 6:
-                u, i = divmod(e - 1, 3)
-                if i > 0:
-                    gather_words(i, 1 + u, shared, offset=e * STAGE_BYTES)
-                gather_scales(i, 1 + u, shared, offset=e * STAGE_BYTES + 4 * GATHER)
-            if e >= QUAD:
-                whole_expert(e - QUAD)
-            if e == 2 * QUAD - 1:
-                for b in range(BANDS):
-                    turn_back(b, 0, QUAD)
-        for e in range(EARLY - QUAD, EARLY):
+            round_and_interleave(grouped[:], raw[e][:])
+            load_q(e + LANDINGS)
+            codes = keep.tile([P, K], U32, name="q_codes%d" % e, align_bytes=64)
+            plane = keep.tile([P, K], U8, name="q_plane%d" % e, align_bytes=64)
+            quantize(codes[:], plane[:], grouped[:])
+            q_codes[e, 0] = codes[:]
+            q_plane[e, 0] = plane[:]
+        for i in range(2):
+            gather_words(i, 2, shared, offset=2 * STAGE_BYTES + i * 4 * GATHER)
+        gather_words(2, 2, shared, offset=3 * STAGE_BYTES)
+        for i in range(3):
+            gather_scales(i, 2, shared, offset=3 * STAGE_BYTES + (4 + i) * GATHER)
+
+        rests = {}
+        for u in range(1, QUADS):
+            head = shared.tile([P, QUAD * P, 4], BF16, name="head%d" % u, align_bytes=64, offset=(3 + u) * STAGE_BYTES)
+            rests[u] = keep.tile([P, QUAD * REST, 4], BF16, name="rest%d" % u, align_bytes=64)
+            for place in range(QUAD):
+                e = QUAD * u + place
+                round_and_interleave(head[:, place * P:(place + 1) * P, :], raw[e][:, :, 0:P])
+                round_and_interleave(rests[u][:, place * REST:(place + 1) * REST, :], raw[e][:, :, P:K])
+                if e + LANDINGS < E:
+                    load_q(e + LANDINGS)
+            codes = keep.tile([P, QUAD * P], U32, name="head_codes%d" % u, align_bytes=64)
+            plane = keep.tile([P, QUAD * P], U8, name="head_plane%d" % u, align_bytes=64)
+            quantize(codes[:], plane[:], head[:])
+            for place in range(QUAD):
+                q_codes[QUAD * u + place, 0] = codes[:, place * P:(place + 1) * P]
+                q_plane[QUAD * u + place, 0] = plane[:, place * P:(place + 1) * P]
+
+        load_kv(0, 0, BANDS, RAW_BYTES, 0)
+        for b in range(BANDS):
+            for u in range(1, QUADS):
+                start = (2 + b) * RAW_BYTES + (u - 1) * 6 * GATHER
+                load_kv(u, b, b + 1, start, start + 2 * GATHER)
+
+        rest_planes = shared.tile(
+            [P, (QUADS - 1) * QUAD * REST], U8, name="rest_planes", align_bytes=64, offset=(2 + QUADS) * STAGE_BYTES,
+        )
+        for u in range(1, QUADS):
+            codes = keep.tile([P, QUAD * REST], U32, name="rest_codes%d" % u, align_bytes=64)
+            plane = rest_planes[:, (u - 1) * QUAD * REST:u * QUAD * REST]
+            for cols in (slice(0, 2 * K), slice(2 * K, 3 * K)):
+                quantize(codes[:, cols], plane[:, cols], rests[u][:, cols, :])
+            for place in range(QUAD):
+                for b in range(1, BANDS):
+                    cols = slice(place * REST + (b - 1) * P, place * REST + b * P)
+                    q_codes[QUAD * u + place, b] = codes[:, cols]
+                    q_plane[QUAD * u + place, b] = plane[:, cols]
+
+        for e in range(QUAD):
             whole_expert(e)
         for b in range(BANDS):
-            load_band(b)
-
-        for b in range(BANDS):
-            turn_back(b, QUAD, 2 * QUAD)
-            for e in range(EARLY, E):
-                start = stage_of(b) + (e - EARLY) * PIECE_BYTES
-                grouped = shared.tile([P, P, 4], BF16, name="piece%d_%d" % (b, e), align_bytes=64, offset=start)
-                quantize_q(e, e + 1, b, grouped, cast_on_scalar)
-                if b > 0 and e == EARLY:
-                    combine_step(b - 1, 0, 0, shared, offset=start)
-                    combine_step(b - 1, 0, 1, ring, tag="sums", bufs=6)
-                if b > 0 and e == EARLY + 1:
-                    combine_step(b - 1, 1, 0, shared, offset=start)
-                if b > 0 and e == EARLY + 2:
-                    combine_step(b - 1, 1, 1, shared, offset=start)
-                    combine_step(b - 1, 2, 0, ring, tag="sums", bufs=6)
-                    combine_step(b - 1, 2, 1, ring, tag="sums", bufs=6)
-            late_band(b)
-        for step in range(3):
-            for half in range(2):
-                combine_step(BANDS - 1, step, half, ring, tag="sums", bufs=6)
+            turn_back(b, 0, 5 + b % 2)
+            for u in range(1, QUADS):
+                band_of_quad(b, u, (4 * b + u - 1) % 3)
+            for u in range(1, QUADS):
+                turn_back(b, u, (4 * b + u + 1) % 3)
+            for step in range(3):
+                for half in range(2):
+                    combine_step(b, step, half)

@@ -27,6 +27,9 @@ GATHER = QUAD * C
 WINDOW = T + T // 2
 RAW_BYTES = 4 * K * 4
 LANDINGS = 6
+Q_HOME = (0, 1, 2, 3, 4, 5, 0, 1, 2, 5, 0, 1)
+BAND_HOME = (2, 5, 0, 1)
+VECTOR_FROM = 9
 STAGE_BYTES = 4 * K * 2
 REST = K - P
 BANK_BYTES = 2048
@@ -78,10 +81,13 @@ def tile_moe_qkb_kernel(
 
         def load_plane(j):
             which, r = divmod(j, 4)
-            nc.sync.dma_start(
+            nc.gpsimd.dma_start(
                 out=kv_plane[which * V_ROW + r:P:32, :].bitcast(I32).rearrange("q (e c) -> q e c", e=E),
                 in_=(wk_scales, wv_scales)[which].rearrange("e s (q r) c -> r q (e s) c", r=4)[r].bitcast(I32),
             )
+
+        for j in range(8):
+            load_plane(j)
 
         k_codes = {}
         v_codes = {}
@@ -106,11 +112,12 @@ def tile_moe_qkb_kernel(
         raw = {}
 
         def load_q(e):
-            raw[e] = landing.tile([P, 4, K], F32, name="raw%d" % e, offset=(e % LANDINGS) * RAW_BYTES)
+            raw[e] = landing.tile([P, 4, K], F32, name="raw%d" % e, offset=Q_HOME[e] * RAW_BYTES)
             nc.sync.dma_start(out=raw[e][:], in_=wq[e].rearrange("(p j) c -> p j c", j=4))
 
-        def round_and_interleave(grouped, rows):
-            nc.scalar.copy(grouped.rearrange("p (c i) j -> p c j i", i=4), rows.rearrange("p j (c i) -> p c j i", i=4))
+        def round_and_interleave(e, grouped, rows):
+            copy = nc.scalar.copy if e < VECTOR_FROM else nc.vector.tensor_copy
+            copy(grouped.rearrange("p (c i) j -> p c j i", i=4), rows.rearrange("p j (c i) -> p c j i", i=4))
 
         def quantize(codes, plane, grouped):
             nc.vector.quantize_mx(out=codes.bitcast(FP8X4), scales=plane, in_=grouped.rearrange("p c j -> p (c j)"))
@@ -208,8 +215,6 @@ def tile_moe_qkb_kernel(
         load_d_scales(2)
         for e in range(3, LANDINGS):
             load_q(e)
-            for j in range(3 * e - 9, min(3 * e - 6, 8)):
-                load_plane(j)
         for i in range(3):
             nc.sync.dma_start(pos_sb[i][:], (pos1, pos2, pos3)[i])
 
@@ -224,8 +229,9 @@ def tile_moe_qkb_kernel(
 
         for e in range(QUAD):
             grouped = shared.tile([P, K, 4], BF16, name="grouped%d" % e, align_bytes=64, offset=e * STAGE_BYTES)
-            round_and_interleave(grouped[:], raw[e][:])
-            load_q(e + LANDINGS)
+            round_and_interleave(e, grouped[:], raw[e][:])
+            if e < 3:
+                load_q(e + LANDINGS)
             codes = keep.tile([P, K], U32, name="q_codes%d" % e, align_bytes=64)
             plane = keep.tile([P, K], U8, name="q_plane%d" % e, align_bytes=64)
             quantize(codes[:], plane[:], grouped[:])
@@ -243,10 +249,12 @@ def tile_moe_qkb_kernel(
             rests[u] = keep.tile([P, QUAD * REST, 4], BF16, name="rest%d" % u, align_bytes=64)
             for place in range(QUAD):
                 e = QUAD * u + place
-                round_and_interleave(head[:, place * P:(place + 1) * P, :], raw[e][:, :, 0:P])
-                round_and_interleave(rests[u][:, place * REST:(place + 1) * REST, :], raw[e][:, :, P:K])
-                if e + LANDINGS < E:
-                    load_q(e + LANDINGS)
+                round_and_interleave(e, head[:, place * P:(place + 1) * P, :], raw[e][:, :, 0:P])
+                round_and_interleave(e, rests[u][:, place * REST:(place + 1) * REST, :], raw[e][:, :, P:K])
+                if e == 4:
+                    load_kv(0, 0, BANDS, 4 * RAW_BYTES, 3 * RAW_BYTES)
+                if 5 <= e <= 7:
+                    load_q(e + 4)
             codes = keep.tile([P, QUAD * P], U32, name="head_codes%d" % u, align_bytes=64)
             plane = keep.tile([P, QUAD * P], U8, name="head_plane%d" % u, align_bytes=64)
             quantize(codes[:], plane[:], head[:])
@@ -254,10 +262,9 @@ def tile_moe_qkb_kernel(
                 q_codes[QUAD * u + place, 0] = codes[:, place * P:(place + 1) * P]
                 q_plane[QUAD * u + place, 0] = plane[:, place * P:(place + 1) * P]
 
-        load_kv(0, 0, BANDS, RAW_BYTES, 0)
         for b in range(BANDS):
             for u in range(1, QUADS):
-                start = (2 + b) * RAW_BYTES + (u - 1) * 6 * GATHER
+                start = BAND_HOME[b] * RAW_BYTES + (u - 1) * 6 * GATHER
                 load_kv(u, b, b + 1, start, start + 2 * GATHER)
 
         rest_planes = shared.tile(
@@ -278,6 +285,7 @@ def tile_moe_qkb_kernel(
             whole_expert(e)
         for b in range(BANDS):
             turn_back(b, 0, 5 + b % 2)
+        for b in range(BANDS):
             for u in range(1, QUADS):
                 band_of_quad(b, u, (4 * b + u - 1) % 3)
             for u in range(1, QUADS):

@@ -21,19 +21,33 @@ C = 128
 S = E * C
 K = 512
 BANDS = K // P
+REST = K - P
+DQ, DK, DV = 0, 1, 2
+
 QUAD = 4
 QUADS = E // QUAD
-GATHER = QUAD * C
-WINDOW = T + T // 2
+SPAN = E // 2
+LISTED = SPAN * C
+WINDOW = 2 * T
+V_ROW = 4
+
+GROUPS = ((4, 8), (8, 11), (11, 12))
+VECTOR_FROM = 9
+QUANTIZE_WORDS = (1024, 512, 256, 128)
+
 RAW_BYTES = 4 * K * 4
 LANDINGS = 6
-Q_HOME = (0, 1, 2, 3, 4, 5, 0, 1, 2, 5, 0, 1)
-BAND_HOME = (2, 5, 0, 1)
-VECTOR_FROM = 9
 STAGE_BYTES = 4 * K * 2
-REST = K - P
+SMALL_RUN = 3
+SUM_BUFS = 10
+GATED_BUFS = 3
+
 BANK_BYTES = 2048
-V_ROW = 4
+GATE_BANK = 7
+WHOLE_BANK = 3
+SLOT_BANKS = (0, 3, 6)
+TURN_BANKS = (2, 1, 7)
+CYCLE = (SLOT_BANKS[2], TURN_BANKS[2], TURN_BANKS[1])
 FLOPS = 2 * 3 * 512 * K * S
 
 
@@ -44,7 +58,7 @@ def tile_moe_qkb_kernel(
     nc = tc.nc
     with ExitStack() as ctx:
         keep = ctx.enter_context(tc.tile_pool(name="keep", bufs=1))
-        shared = ctx.enter_context(tc.tile_pool(name="shared", bufs=1))
+        stage = ctx.enter_context(tc.tile_pool(name="stage", bufs=1))
         landing = ctx.enter_context(tc.tile_pool(name="landing", bufs=1))
         ring = ctx.enter_context(tc.tile_pool(name="ring", bufs=1))
         psum = ctx.enter_context(tc.psum_pool(name="psum", bufs=1))
@@ -61,12 +75,20 @@ def tile_moe_qkb_kernel(
 
         for i in range(3):
             nc.vector.memset(d_scales[i][:].bitcast(I32), 0)
+        nc.vector.memset(gate_rows[:], 0.0)
         for i in range(3):
             nc.vector.memset(d_words[i][:, T:WINDOW], 0)
         nc.vector.memset(kv_plane[:].bitcast(I32), 0)
         make_identity(nc, identity[:])
-        nc.gpsimd.memset(gate_rows[:], 0.0)
-        nc.gpsimd.dma_start(out=gate_rows[0:E, :], in_=gate[0].rearrange("(e u) -> e u", u=C))
+
+        nc.scalar.dma_start(out=gate_rows[0:E, :], in_=gate[0].rearrange("(e u) -> e u", u=C))
+        gate_bank = psum.tile([P, K], F32, name="gate_bank", offset=GATE_BANK * BANK_BYTES)
+        nc.tensor.transpose(gate_bank[:, 0:P], gate_rows[:], identity[:])
+        nc.scalar.activation(gate_cols[:], gate_bank[:, 0:E], COPY)
+
+        def load_d_words(i):
+            src = (dq_words, dk_words, dv_words)[i]
+            nc.sync.dma_start(out=d_words[i][:, 0:T], in_=src[0].rearrange("p t d -> p (t d)").bitcast(I32))
 
         def load_d_scales(i):
             for r in range(4):
@@ -75,19 +97,20 @@ def tile_moe_qkb_kernel(
                     in_=(dq_scales, dk_scales, dv_scales)[i].rearrange("s (q r) t -> r (s q) t", r=4)[r].bitcast(I32),
                 )
 
-        gate_bank = psum.tile([P, K], F32, name="gate_bank", offset=7 * BANK_BYTES)
-        nc.tensor.transpose(gate_bank[:, 0:P], gate_rows[:], identity[:])
-        nc.scalar.activation(gate_cols[:], gate_bank[:, 0:E], COPY)
-
-        def load_plane(j):
+        def load_kv_scales(j):
             which, r = divmod(j, 4)
-            nc.gpsimd.dma_start(
+            nc.sync.dma_start(
                 out=kv_plane[which * V_ROW + r:P:32, :].bitcast(I32).rearrange("q (e c) -> q e c", e=E),
                 in_=(wk_scales, wv_scales)[which].rearrange("e s (q r) c -> r q (e s) c", r=4)[r].bitcast(I32),
             )
 
-        for j in range(8):
-            load_plane(j)
+        raw = {}
+        place_of = {}
+
+        def load_q(e, start):
+            place_of[e] = start
+            raw[e] = landing.tile([P, 4, K], F32, name="raw%d" % e, offset=start)
+            nc.sync.dma_start(out=raw[e][:], in_=wq[e].rearrange("(p j) c -> p j c", j=4))
 
         k_codes = {}
         v_codes = {}
@@ -105,191 +128,193 @@ def tile_moe_qkb_kernel(
                 out=v_tile[:].bitcast(I32).rearrange("p (e c) -> p e c", e=QUAD),
                 in_=wv_words.rearrange("e s p c d -> p (e s) (c d)").bitcast(I32)[:, first:first + QUAD, b0 * P:b1 * P],
             )
-            for place in range(QUAD):
-                k_codes[first + place, b0] = k_tile[:, place * 2 * width:(place + 1) * 2 * width]
-                v_codes[first + place, b0] = v_tile[:, place * 4 * width:(place + 1) * 4 * width]
+            for x in range(QUAD):
+                k_codes[first + x, b0] = k_tile[:, x * 2 * width:(x + 1) * 2 * width]
+                v_codes[first + x, b0] = v_tile[:, x * 4 * width:(x + 1) * 4 * width]
 
-        raw = {}
-
-        def load_q(e):
-            raw[e] = landing.tile([P, 4, K], F32, name="raw%d" % e, offset=Q_HOME[e] * RAW_BYTES)
-            nc.sync.dma_start(out=raw[e][:], in_=wq[e].rearrange("(p j) c -> p j c", j=4))
+        def load_band(b, start):
+            for u in range(1, QUADS):
+                k_start = start + (u - 1) * QUAD * P * (2 + 4)
+                load_kv(u, b, b + 1, k_start, k_start + QUAD * P * 2)
 
         def round_and_interleave(e, grouped, rows):
             copy = nc.scalar.copy if e < VECTOR_FROM else nc.vector.tensor_copy
             copy(grouped.rearrange("p (c i) j -> p c j i", i=4), rows.rearrange("p j (c i) -> p c j i", i=4))
 
-        def quantize(codes, plane, grouped):
-            nc.vector.quantize_mx(out=codes.bitcast(FP8X4), scales=plane, in_=grouped.rearrange("p c j -> p (c j)"))
+        def quantize_columns(name, grouped):
+            width = grouped.shape[1]
+            codes = keep.tile([P, width], U32, name=name + "_codes", align_bytes=64)
+            plane = keep.tile([P, width], U8, name=name + "_plane", align_bytes=64)
+            done = 0
+            for piece in QUANTIZE_WORDS:
+                if width - done >= piece:
+                    cols = slice(done, done + piece)
+                    nc.vector.quantize_mx(
+                        out=codes[:, cols].bitcast(FP8X4), scales=plane[:, cols],
+                        in_=grouped[:, cols, :].rearrange("p c j -> p (c j)"),
+                    )
+                    done = done + piece
+            return codes, plane
 
         q_codes = {}
         q_plane = {}
+
         g_words = {}
         g_scales = {}
 
-        def gather_words(i, u, pool, **where):
-            g_words[i, u] = pool.tile([P, GATHER], U32, name="g_words%d_%d" % (i, u), align_bytes=64, **where)
+        def gather_words(i, h, pool, **where):
+            g_words[i, h] = pool.tile([P, LISTED], U32, name="g_words%d_%d" % (i, h), align_bytes=64, **where)
             nc.vector.tensor_copy(
-                g_words[i, u][:],
-                d_words[i][:].bitcast(U32).indirect(offs_sb[:, u * GATHER // 16:(u + 1) * GATHER // 16]),
+                g_words[i, h][:],
+                d_words[i][:].bitcast(U32).indirect(offs_sb[:, h * LISTED // 16:(h + 1) * LISTED // 16]),
             )
 
-        def gather_scales(i, u, pool, **where):
-            g_scales[i, u] = pool.tile([P, GATHER], U8, name="g_scales%d_%d" % (i, u), align_bytes=64, **where)
+        def gather_scales(i, h, pool, **where):
+            g_scales[i, h] = pool.tile([P, LISTED], U8, name="g_scales%d_%d" % (i, h), align_bytes=64, **where)
             nc.vector.tensor_copy(
-                g_scales[i, u][:],
-                d_scales[i][:].indirect(offs_sb[:, u * GATHER // 16:(u + 1) * GATHER // 16]),
+                g_scales[i, h][:],
+                d_scales[i][:].indirect(offs_sb[:, h * LISTED // 16:(h + 1) * LISTED // 16]),
             )
 
         def multiply(acc, e, b0, b1):
-            u, place = divmod(e, QUAD)
-            slots = slice(place * C, (place + 1) * C)
+            h, x = divmod(e, SPAN)
+            slots = slice(x * C, (x + 1) * C)
             cols = slice(e * K + b0 * P, e * K + b1 * P)
-            nc.tensor.matmul_mx(
-                out=acc, lhsT=g_words[1, u][:, slots].bitcast(FP8X4), lhsT_scale=g_scales[1, u][:, slots],
-                rhs=k_codes[e, b0].bitcast(FP4X4),
-                rhs_scale=kv_plane[:, cols], start=True, stop=False,
-            )
-            nc.tensor.matmul_mx(
-                out=acc, lhsT=g_words[2, u][:, slots].bitcast(FP8X4), lhsT_scale=g_scales[2, u][:, slots],
-                rhs=v_codes[e, b0].bitcast(FP8X4), rhs_scale=kv_plane[V_ROW:P, cols], start=False, stop=False,
-            )
-            nc.tensor.matmul_mx(
-                out=acc, lhsT=g_words[0, u][:, slots].bitcast(FP8X4), lhsT_scale=g_scales[0, u][:, slots],
-                rhs=q_codes[e, b0].bitcast(FP8X4), rhs_scale=q_plane[e, b0], start=False, stop=True,
-            )
+            moving = {
+                DK: (k_codes[e, b0].bitcast(FP4X4), kv_plane[:, cols]),
+                DV: (v_codes[e, b0].bitcast(FP8X4), kv_plane[V_ROW:P, cols]),
+                DQ: (q_codes[e, b0].bitcast(FP8X4), q_plane[e, b0]),
+            }
+            for i in (DK, DV, DQ):
+                nc.tensor.matmul_mx(
+                    out=acc, lhsT=g_words[i, h][:, slots].bitcast(FP8X4), lhsT_scale=g_scales[i, h][:, slots],
+                    rhs=moving[i][0], rhs_scale=moving[i][1], start=i == DK, stop=i == DQ,
+                )
 
         gated = {}
 
-        def turn_back(b, u, bank):
-            by_channel = psum.tile([P, K], F32, name="by_channel%d_%d" % (b, u), offset=bank * BANK_BYTES)
-            for place in range(QUAD):
-                nc.tensor.transpose(by_channel[:, place * C:(place + 1) * C], gated[QUAD * u + place, b], identity[:])
-            nc.scalar.copy(dx[b][:, u * GATHER:(u + 1) * GATHER], by_channel[:])
-
         def whole_expert(e):
-            by_slot = psum.tile([P, K], F32, name="whole%d" % e, offset=(3 + e % 2) * BANK_BYTES)
+            by_slot = psum.tile([P, K], F32, name="whole%d" % e, offset=(WHOLE_BANK + e) * BANK_BYTES)
             multiply(by_slot[:], e, 0, BANDS)
             rows = keep.tile([P, K], F32, name="gated%d" % e)
             nc.scalar.activation(rows[:], by_slot[:], COPY, scale=gate_cols[:, e:e + 1])
             for b in range(BANDS):
                 gated[e, b] = rows[:, b * P:(b + 1) * P]
 
-        def band_of_quad(b, u, bank):
-            by_slot = psum.tile([P, K], F32, name="by_slot%d_%d" % (b, u), offset=bank * BANK_BYTES)
-            for place in range(QUAD):
-                multiply(by_slot[:, place * P:(place + 1) * P], QUAD * u + place, b, b + 1)
-            rows = ring.tile([P, K], F32, name="gated", tag="gated", bufs=3)
-            for place in range(QUAD):
-                e = QUAD * u + place
-                cols = slice(place * P, (place + 1) * P)
+        def band_of(b, first, last, bank):
+            by_slot = psum.tile([P, K], F32, name="by_slot%d_%d" % (b, first), offset=bank * BANK_BYTES)
+            for e in range(first, last):
+                multiply(by_slot[:, (e - first) * P:(e - first + 1) * P], e, b, b + 1)
+            rows = ring.tile([P, K], F32, name="gated", tag="gated", bufs=GATED_BUFS)
+            for e in range(first, last):
+                cols = slice((e - first) * P, (e - first + 1) * P)
                 nc.scalar.activation(rows[:, cols], by_slot[:, cols], COPY, scale=gate_cols[:, e:e + 1])
                 gated[e, b] = rows[:, cols]
 
-        sums = {}
+        def turn_back(b, first, last, bank):
+            by_channel = psum.tile([P, K], F32, name="by_channel%d_%d" % (b, first), offset=bank * BANK_BYTES)
+            for e in range(first, last):
+                nc.tensor.transpose(by_channel[:, (e - first) * C:(e - first + 1) * C], gated[e, b], identity[:])
+            nc.scalar.copy(dx[b][:, first * C:last * C], by_channel[:, 0:(last - first) * C])
 
-        def combine_step(b, step, half):
+        def combine(b):
             width = T // 2
-            sums[step, half] = ring.tile([P, width], F32, name="sums", tag="sums", bufs=10)
-            picked = dx[b][:].indirect(pos_sb[step][:, half * width // 16:(half + 1) * width // 16])
-            if step == 0:
-                nc.vector.tensor_copy(sums[step, half][:], picked)
-            else:
-                nc.vector.tensor_tensor(sums[step, half][:], picked, sums[step - 1, half][:], ADD)
-            if step == 2:
-                nc.sync.dma_start(out=out[b * P:(b + 1) * P, half * width:(half + 1) * width], in_=sums[step, half][:])
-
-        def load_d_words(i):
-            src = (dq_words, dk_words, dv_words)[i]
-            nc.sync.dma_start(out=d_words[i][:, 0:T], in_=src[0].rearrange("p t d -> p (t d)").bitcast(I32))
+            sums = {}
+            for step in range(3):
+                for half in range(2):
+                    sums[step, half] = ring.tile([P, width], F32, name="sums", tag="sums", bufs=SUM_BUFS)
+                    picked = dx[b][:].indirect(pos_sb[step][:, half * width // 16:(half + 1) * width // 16])
+                    if step == 0:
+                        nc.vector.tensor_copy(sums[step, half][:], picked)
+                    else:
+                        nc.vector.tensor_tensor(sums[step, half][:], picked, sums[step - 1, half][:], ADD)
+                    if step == 2:
+                        nc.sync.dma_start(
+                            out=out[b * P:(b + 1) * P, half * width:(half + 1) * width], in_=sums[step, half][:],
+                        )
 
         nc.sync.dma_start(offs_sb[:], offs)
-        load_d_words(0)
-        load_q(0)
-        load_d_words(1)
-        load_d_scales(0)
-        load_d_words(2)
-        load_q(1)
-        load_d_scales(1)
-        load_q(2)
-        load_d_scales(2)
+        load_d_words(DQ)
+        load_q(0, 0)
+        load_d_words(DK)
+        load_d_scales(DQ)
+        load_q(1, RAW_BYTES)
+        load_d_words(DV)
+        load_d_scales(DK)
+        load_q(2, 2 * RAW_BYTES)
+        load_d_scales(DV)
         for e in range(3, LANDINGS):
-            load_q(e)
+            load_q(e, e * RAW_BYTES)
+            for j in range(SMALL_RUN * (e - 3), min(SMALL_RUN * (e - 2), 8)):
+                load_kv_scales(j)
         for i in range(3):
             nc.sync.dma_start(pos_sb[i][:], (pos1, pos2, pos3)[i])
 
-        for u in range(2):
-            gather_words(0, u, keep)
-        for i in range(3):
-            if i > 0:
-                for u in range(2):
-                    gather_words(i, u, keep)
-            for u in range(2):
-                gather_scales(i, u, keep)
+        for h in range(2):
+            gather_words(DQ, h, keep)
+        gather_scales(DQ, 0, keep)
+        for i in (DK, DV):
+            gather_words(i, 0, keep)
+            gather_scales(i, 0, keep)
 
         for e in range(QUAD):
-            grouped = shared.tile([P, K, 4], BF16, name="grouped%d" % e, align_bytes=64, offset=e * STAGE_BYTES)
+            grouped = stage.tile([P, K, 4], BF16, name="grouped%d" % e, align_bytes=64, offset=e * STAGE_BYTES)
             round_and_interleave(e, grouped[:], raw[e][:])
-            if e < 3:
-                load_q(e + LANDINGS)
-            codes = keep.tile([P, K], U32, name="q_codes%d" % e, align_bytes=64)
-            plane = keep.tile([P, K], U8, name="q_plane%d" % e, align_bytes=64)
-            quantize(codes[:], plane[:], grouped[:])
+            if e + LANDINGS < VECTOR_FROM:
+                load_q(e + LANDINGS, place_of[e])
+            codes, plane = quantize_columns("whole%d" % e, grouped)
             q_codes[e, 0] = codes[:]
             q_plane[e, 0] = plane[:]
-        for i in range(2):
-            gather_words(i, 2, shared, offset=2 * STAGE_BYTES + i * 4 * GATHER)
-        gather_words(2, 2, shared, offset=3 * STAGE_BYTES)
-        for i in range(3):
-            gather_scales(i, 2, shared, offset=3 * STAGE_BYTES + (4 + i) * GATHER)
 
-        rests = {}
-        for u in range(1, QUADS):
-            head = shared.tile([P, QUAD * P, 4], BF16, name="head%d" % u, align_bytes=64, offset=(3 + u) * STAGE_BYTES)
-            rests[u] = keep.tile([P, QUAD * REST, 4], BF16, name="rest%d" % u, align_bytes=64)
-            for place in range(QUAD):
-                e = QUAD * u + place
-                round_and_interleave(e, head[:, place * P:(place + 1) * P, :], raw[e][:, :, 0:P])
-                round_and_interleave(e, rests[u][:, place * REST:(place + 1) * REST, :], raw[e][:, :, P:K])
+        for i in (DQ, DK, DV):
+            if i != DQ:
+                gather_words(i, 1, stage, offset=(1 + i) * STAGE_BYTES)
+            gather_scales(i, 1, stage, offset=(1 + i) * STAGE_BYTES + 4 * LISTED)
+
+        for first, last in GROUPS:
+            n = last - first
+            pool, where = (stage, {"offset": QUAD * STAGE_BYTES}) if last == E else (keep, {})
+            head = pool.tile([P, n * P, 4], BF16, name="head%d" % first, align_bytes=64, **where)
+            rest = pool.tile([P, n * REST, 4], BF16, name="rest%d" % first, align_bytes=64, **where)
+            for e in range(first, last):
+                round_and_interleave(e, head[:, (e - first) * P:(e - first + 1) * P, :], raw[e][:, :, 0:P])
+                if e == last - 1:
+                    head_codes, head_plane = quantize_columns("head%d" % first, head)
+                round_and_interleave(e, rest[:, (e - first) * REST:(e - first + 1) * REST, :], raw[e][:, :, P:K])
                 if e == 4:
-                    load_kv(0, 0, BANDS, 4 * RAW_BYTES, 3 * RAW_BYTES)
-                if 5 <= e <= 7:
-                    load_q(e + 4)
-            codes = keep.tile([P, QUAD * P], U32, name="head_codes%d" % u, align_bytes=64)
-            plane = keep.tile([P, QUAD * P], U8, name="head_plane%d" % u, align_bytes=64)
-            quantize(codes[:], plane[:], head[:])
-            for place in range(QUAD):
-                q_codes[QUAD * u + place, 0] = codes[:, place * P:(place + 1) * P]
-                q_plane[QUAD * u + place, 0] = plane[:, place * P:(place + 1) * P]
-
-        for b in range(BANDS):
-            for u in range(1, QUADS):
-                start = BAND_HOME[b] * RAW_BYTES + (u - 1) * 6 * GATHER
-                load_kv(u, b, b + 1, start, start + 2 * GATHER)
-
-        rest_planes = shared.tile(
-            [P, (QUADS - 1) * QUAD * REST], U8, name="rest_planes", align_bytes=64, offset=(2 + QUADS) * STAGE_BYTES,
-        )
-        for u in range(1, QUADS):
-            codes = keep.tile([P, QUAD * REST], U32, name="rest_codes%d" % u, align_bytes=64)
-            plane = rest_planes[:, (u - 1) * QUAD * REST:u * QUAD * REST]
-            for cols in (slice(0, 2 * K), slice(2 * K, 3 * K)):
-                quantize(codes[:, cols], plane[:, cols], rests[u][:, cols, :])
-            for place in range(QUAD):
+                    load_kv(0, 0, BANDS, place_of[4], place_of[3])
+                elif e in (5, 6):
+                    load_q(e + 4, place_of[e])
+                elif e == 7:
+                    load_band(0, place_of[7])
+                elif e == 8:
+                    load_q(E - 1, place_of[8])
+            rest_codes, rest_plane = quantize_columns("rest%d" % first, rest)
+            for e in range(first, last):
+                cols = slice((e - first) * P, (e - first + 1) * P)
+                q_codes[e, 0] = head_codes[:, cols]
+                q_plane[e, 0] = head_plane[:, cols]
                 for b in range(1, BANDS):
-                    cols = slice(place * REST + (b - 1) * P, place * REST + b * P)
-                    q_codes[QUAD * u + place, b] = codes[:, cols]
-                    q_plane[QUAD * u + place, b] = plane[:, cols]
+                    cols = slice((e - first) * REST + (b - 1) * P, (e - first) * REST + b * P)
+                    q_codes[e, b] = rest_codes[:, cols]
+                    q_plane[e, b] = rest_plane[:, cols]
+        for b in range(1, BANDS):
+            load_band(b, place_of[E - BANDS + b])
 
         for e in range(QUAD):
             whole_expert(e)
         for b in range(BANDS):
-            turn_back(b, 0, 5 + b % 2)
-        for b in range(BANDS):
-            for u in range(1, QUADS):
-                band_of_quad(b, u, (4 * b + u - 1) % 3)
-            for u in range(1, QUADS):
-                turn_back(b, u, (4 * b + u + 1) % 3)
-            for step in range(3):
-                for half in range(2):
-                    combine_step(b, step, half)
+            turn_back(b, 0, QUAD, 1 + b % 2)
+
+        for (first, last), bank in zip(GROUPS, SLOT_BANKS):
+            band_of(0, first, last, bank)
+        for (first, last), bank in zip(GROUPS, TURN_BANKS):
+            turn_back(0, first, last, bank)
+        combine(0)
+        taken = 0
+        for b in range(1, BANDS):
+            for work in (band_of, turn_back):
+                for u in range(1, QUADS):
+                    work(b, QUAD * u, QUAD * (u + 1), CYCLE[taken % 3])
+                    taken = taken + 1
+            combine(b)

@@ -12,6 +12,7 @@ U8 = mybir.dt.uint8
 FP8X4 = mybir.dt.float8_e4m3fn_x4
 FP4X4 = mybir.dt.float4_e2m1fn_x4
 ADD = mybir.AluOpType.add
+MULT = mybir.AluOpType.mult
 COPY = mybir.ActivationFunctionType.Copy
 
 P = 128
@@ -21,33 +22,19 @@ C = 128
 S = E * C
 K = 512
 BANDS = K // P
-REST = K - P
 DQ, DK, DV = 0, 1, 2
 
-QUAD = 4
-QUADS = E // QUAD
 SPAN = E // 2
 LISTED = SPAN * C
 WINDOW = 2 * T
 V_ROW = 4
-
-GROUPS = ((4, 8), (8, 11), (11, 12))
-VECTOR_FROM = 9
-QUANTIZE_WORDS = (1024, 512, 256, 128)
-
+GROUPS = tuple((e, e + 2) for e in range(0, E, 2))
+KV_AFTER = (7, 11, 11, 11, 11, 11)
 RAW_BYTES = 4 * K * 4
-LANDINGS = 6
 STAGE_BYTES = 4 * K * 2
+LAG = 2
 SMALL_RUN = 3
-SUM_BUFS = 10
-GATED_BUFS = 3
-
 BANK_BYTES = 2048
-GATE_BANK = 7
-WHOLE_BANK = 3
-SLOT_BANKS = (0, 3, 6)
-TURN_BANKS = (2, 1, 7)
-CYCLE = (SLOT_BANKS[2], TURN_BANKS[2], TURN_BANKS[1])
 FLOPS = 2 * 3 * 512 * K * S
 
 
@@ -58,9 +45,7 @@ def tile_moe_qkb_kernel(
     nc = tc.nc
     with ExitStack() as ctx:
         keep = ctx.enter_context(tc.tile_pool(name="keep", bufs=1))
-        stage = ctx.enter_context(tc.tile_pool(name="stage", bufs=1))
         landing = ctx.enter_context(tc.tile_pool(name="landing", bufs=1))
-        ring = ctx.enter_context(tc.tile_pool(name="ring", bufs=1))
         psum = ctx.enter_context(tc.psum_pool(name="psum", bufs=1))
 
         offs_sb = keep.tile([P, S // 16], U16, name="offs_sb")
@@ -68,34 +53,31 @@ def tile_moe_qkb_kernel(
         d_words = [keep.tile([P, WINDOW], I32, name="d_words%d" % i, align_bytes=64) for i in range(3)]
         d_scales = [keep.tile([P, WINDOW], U8, name="d_scales%d" % i, align_bytes=64) for i in range(3)]
         kv_plane = keep.tile([P, E * K], U8, name="kv_plane", align_bytes=64)
-        gate_rows = keep.tile([P, C], F32, name="gate_rows")
-        gate_cols = keep.tile([P, E], F32, name="gate_cols")
+        gate_rows = keep.tile([P, 3, C], F32, name="gate_rows")
+        gate_cols = keep.tile([P, 3, 4], F32, name="gate_cols")
+        gate_wide = keep.tile([P, S], F32, name="gate_wide")
         identity = keep.tile([P, P], F32, name="identity")
         dx = [keep.tile([P, S], F32, name="dx%d" % b) for b in range(BANDS)]
 
+        nc.gpsimd.memset(gate_rows[:], 0.0)
+        make_identity(nc, identity[:])
         for i in range(3):
-            nc.vector.memset(d_scales[i][:].bitcast(I32), 0)
-        nc.vector.memset(gate_rows[:], 0.0)
+            nc.gpsimd.memset(d_scales[i][:].bitcast(I32), 0)
+        nc.gpsimd.memset(kv_plane[:].bitcast(I32), 0)
         for i in range(3):
             nc.vector.memset(d_words[i][:, T:WINDOW], 0)
-        nc.vector.memset(kv_plane[:].bitcast(I32), 0)
-        make_identity(nc, identity[:])
-
-        nc.scalar.dma_start(out=gate_rows[0:E, :], in_=gate[0].rearrange("(e u) -> e u", u=C))
-        gate_bank = psum.tile([P, K], F32, name="gate_bank", offset=GATE_BANK * BANK_BYTES)
-        nc.tensor.transpose(gate_bank[:, 0:P], gate_rows[:], identity[:])
-        nc.scalar.activation(gate_cols[:], gate_bank[:, 0:E], COPY)
+        nc.sync.dma_start(out=gate_rows[0:4], in_=gate[0].rearrange("(q x u) -> q x u", q=4, x=3))
 
         def load_d_words(i):
             src = (dq_words, dk_words, dv_words)[i]
             nc.sync.dma_start(out=d_words[i][:, 0:T], in_=src[0].rearrange("p t d -> p (t d)").bitcast(I32))
 
-        def load_d_scales(i):
-            for r in range(4):
-                nc.sync.dma_start(
-                    out=d_scales[i][r:P:32, 0:T].bitcast(I32),
-                    in_=(dq_scales, dk_scales, dv_scales)[i].rearrange("s (q r) t -> r (s q) t", r=4)[r].bitcast(I32),
-                )
+        def load_d_scales(j):
+            i, r = divmod(j, 4)
+            nc.sync.dma_start(
+                out=d_scales[i][r:P:32, 0:T].bitcast(I32),
+                in_=(dq_scales, dk_scales, dv_scales)[i].rearrange("s (q r) t -> r (s q) t", r=4)[r].bitcast(I32),
+            )
 
         def load_kv_scales(j):
             which, r = divmod(j, 4)
@@ -104,217 +86,135 @@ def tile_moe_qkb_kernel(
                 in_=(wk_scales, wv_scales)[which].rearrange("e s (q r) c -> r q (e s) c", r=4)[r].bitcast(I32),
             )
 
-        raw = {}
-        place_of = {}
+        def load_pos(i):
+            nc.sync.dma_start(pos_sb[i][:], (pos1, pos2, pos3)[i])
 
-        def load_q(e, start):
-            place_of[e] = start
-            raw[e] = landing.tile([P, 4, K], F32, name="raw%d" % e, offset=start)
+        raw = {}
+
+        def load_q(e):
+            raw[e] = landing.tile([P, 4, K], F32, name="raw%d" % e, align_bytes=64, offset=(e + LAG) * RAW_BYTES)
             nc.sync.dma_start(out=raw[e][:], in_=wq[e].rearrange("(p j) c -> p j c", j=4))
 
         k_codes = {}
         v_codes = {}
 
-        def load_kv(u, b0, b1, k_start, v_start):
-            first = QUAD * u
-            width = (b1 - b0) * P
-            k_tile = landing.tile([P, QUAD * width * 2], U8, name="k_codes%d_%d" % (u, b0), align_bytes=64, offset=k_start)
-            v_tile = landing.tile([P, QUAD * width * 4], U8, name="v_codes%d_%d" % (u, b0), align_bytes=64, offset=v_start)
+        def load_kv(first, last):
+            n = last - first
+            k_tile = keep.tile([P, n * K * 2], U8, name="k_codes%d" % first, align_bytes=64)
+            v_tile = keep.tile([P, n * K * 4], U8, name="v_codes%d" % first, align_bytes=64)
             nc.sync.dma_start(
-                out=k_tile[:].bitcast(I32).rearrange("p (e c) -> p e c", e=QUAD),
-                in_=wk_words.rearrange("e s p c -> p (e s) c").bitcast(I32)[:, first:first + QUAD, b0 * P // 2:b1 * P // 2],
+                out=k_tile[:].bitcast(I32).rearrange("p (e c) -> p e c", e=n),
+                in_=wk_words.rearrange("e s p c -> p (e s) c").bitcast(I32)[:, first:last, :],
             )
             nc.sync.dma_start(
-                out=v_tile[:].bitcast(I32).rearrange("p (e c) -> p e c", e=QUAD),
-                in_=wv_words.rearrange("e s p c d -> p (e s) (c d)").bitcast(I32)[:, first:first + QUAD, b0 * P:b1 * P],
+                out=v_tile[:].bitcast(I32).rearrange("p (e c) -> p e c", e=n),
+                in_=wv_words.rearrange("e s p c d -> p (e s) (c d)").bitcast(I32)[:, first:last, :],
             )
-            for x in range(QUAD):
-                k_codes[first + x, b0] = k_tile[:, x * 2 * width:(x + 1) * 2 * width]
-                v_codes[first + x, b0] = v_tile[:, x * 4 * width:(x + 1) * 4 * width]
+            for e in range(first, last):
+                k_codes[e] = k_tile[:, (e - first) * 2 * K:(e - first + 1) * 2 * K]
+                v_codes[e] = v_tile[:, (e - first) * 4 * K:(e - first + 1) * 4 * K]
 
-        def load_band(b, start):
-            for u in range(1, QUADS):
-                k_start = start + (u - 1) * QUAD * P * (2 + 4)
-                load_kv(u, b, b + 1, k_start, k_start + QUAD * P * 2)
+        small = [(load_d_scales, j) for j in range(12)] + [(load_kv_scales, j) for j in range(8)] + [(load_pos, i) for i in range(3)]
+        nc.sync.dma_start(offs_sb[:], offs)
+        load_d_words(DQ)
+        load_q(0)
+        load_d_words(DK)
+        load_d_words(DV)
+        for e in range(1, E):
+            load_q(e)
+            for load, j in small[SMALL_RUN * (e - 1):SMALL_RUN * e]:
+                load(j)
+            for group, after in zip(GROUPS, KV_AFTER):
+                if after == e:
+                    load_kv(*group)
 
-        def round_and_interleave(e, grouped, rows):
-            copy = nc.scalar.copy if e < VECTOR_FROM else nc.vector.tensor_copy
-            copy(grouped.rearrange("p (c i) j -> p c j i", i=4), rows.rearrange("p j (c i) -> p c j i", i=4))
+        gate_bank = psum.tile([P, K], F32, name="gate_bank", offset=7 * BANK_BYTES)
+        for x in range(3):
+            nc.tensor.transpose(gate_bank[:, x * P:(x + 1) * P], gate_rows[:, x, :], identity[:])
+        nc.scalar.activation(gate_cols[:], gate_bank[:].rearrange("p (x q) -> p x q", q=P)[:, 0:3, 0:4], COPY)
+        for u in range(E // 4):
+            spread = psum.tile([P, K], F32, name="spread%d" % u, offset=(4 + u) * BANK_BYTES)
+            for x in range(4):
+                e = 4 * u + x
+                nc.tensor.transpose(spread[:, x * C:(x + 1) * C], gate_cols[:, e % 3, e // 3:e // 3 + 1].to_broadcast([P, P]), identity[:])
+            nc.scalar.copy(gate_wide[:, u * K:(u + 1) * K], spread[:])
 
-        def quantize_columns(name, grouped):
-            width = grouped.shape[1]
-            codes = keep.tile([P, width], U32, name=name + "_codes", align_bytes=64)
-            plane = keep.tile([P, width], U8, name=name + "_plane", align_bytes=64)
-            done = 0
-            for piece in QUANTIZE_WORDS:
-                if width - done >= piece:
-                    cols = slice(done, done + piece)
-                    nc.vector.quantize_mx(
-                        out=codes[:, cols].bitcast(FP8X4), scales=plane[:, cols],
-                        in_=grouped[:, cols, :].rearrange("p c j -> p (c j)"),
-                    )
-                    done = done + piece
-            return codes, plane
+        g_words = {}
+        g_scales = {}
+        for h in range(2):
+            part = offs_sb[:, h * LISTED // 16:(h + 1) * LISTED // 16]
+            for i in (DQ, DK, DV):
+                g_words[i, h] = keep.tile([P, LISTED], U32, name="g_words%d_%d" % (i, h), align_bytes=64)
+                nc.vector.tensor_copy(g_words[i, h][:], d_words[i][:].bitcast(U32).indirect(part))
+            for i in (DQ, DK, DV):
+                g_scales[i, h] = keep.tile([P, LISTED], U8, name="g_scales%d_%d" % (i, h), align_bytes=64)
+                nc.vector.tensor_copy(g_scales[i, h][:], d_scales[i][:].indirect(part))
 
         q_codes = {}
         q_plane = {}
 
-        g_words = {}
-        g_scales = {}
-
-        def gather_words(i, h, pool, **where):
-            g_words[i, h] = pool.tile([P, LISTED], U32, name="g_words%d_%d" % (i, h), align_bytes=64, **where)
-            nc.vector.tensor_copy(
-                g_words[i, h][:],
-                d_words[i][:].bitcast(U32).indirect(offs_sb[:, h * LISTED // 16:(h + 1) * LISTED // 16]),
+        def quantize_q(e):
+            place = e * RAW_BYTES
+            grouped = landing.tile([P, K, 4], BF16, name="grouped%d" % e, align_bytes=64, offset=place)
+            codes = landing.tile([P, K], U32, name="q_codes%d" % e, align_bytes=64, offset=place + STAGE_BYTES)
+            plane = landing.tile([P, K], U8, name="q_plane%d" % e, align_bytes=64, offset=place + STAGE_BYTES + 4 * K)
+            share = K
+            nc.scalar.copy(
+                grouped[:, 0:share, :].rearrange("p (c i) j -> p c j i", i=4),
+                raw[e][:, :, 0:share].rearrange("p j (c i) -> p c j i", i=4),
             )
-
-        def gather_scales(i, h, pool, **where):
-            g_scales[i, h] = pool.tile([P, LISTED], U8, name="g_scales%d_%d" % (i, h), align_bytes=64, **where)
-            nc.vector.tensor_copy(
-                g_scales[i, h][:],
-                d_scales[i][:].indirect(offs_sb[:, h * LISTED // 16:(h + 1) * LISTED // 16]),
-            )
-
-        def multiply(acc, e, b0, b1):
-            h, x = divmod(e, SPAN)
-            slots = slice(x * C, (x + 1) * C)
-            cols = slice(e * K + b0 * P, e * K + b1 * P)
-            moving = {
-                DK: (k_codes[e, b0].bitcast(FP4X4), kv_plane[:, cols]),
-                DV: (v_codes[e, b0].bitcast(FP8X4), kv_plane[V_ROW:P, cols]),
-                DQ: (q_codes[e, b0].bitcast(FP8X4), q_plane[e, b0]),
-            }
-            for i in (DK, DV, DQ):
-                nc.tensor.matmul_mx(
-                    out=acc, lhsT=g_words[i, h][:, slots].bitcast(FP8X4), lhsT_scale=g_scales[i, h][:, slots],
-                    rhs=moving[i][0], rhs_scale=moving[i][1], start=i == DK, stop=i == DQ,
+            if share < K:
+                nc.vector.tensor_copy(
+                    grouped[:, share:K, :].rearrange("p (c i) j -> p c j i", i=4),
+                    raw[e][:, :, share:K].rearrange("p j (c i) -> p c j i", i=4),
                 )
+            nc.vector.quantize_mx(
+                out=codes[:].bitcast(FP8X4), scales=plane[:], in_=grouped[:].rearrange("p c j -> p (c j)"),
+            )
+            q_codes[e] = codes
+            q_plane[e] = plane
 
-        gated = {}
+        def stationary(i, e, b):
+            cols = slice(e * K + b * P, e * K + (b + 1) * P)
+            if i == DQ:
+                return q_codes[e][:, b * P:(b + 1) * P].bitcast(FP8X4), q_plane[e][:, b * P:(b + 1) * P]
+            if i == DK:
+                return k_codes[e][:, b * 2 * P:(b + 1) * 2 * P].bitcast(FP4X4), kv_plane[:, cols]
+            return v_codes[e][:, b * 4 * P:(b + 1) * 4 * P].bitcast(FP8X4), kv_plane[V_ROW:P, cols]
 
-        def whole_expert(e):
-            by_slot = psum.tile([P, K], F32, name="whole%d" % e, offset=(WHOLE_BANK + e) * BANK_BYTES)
-            multiply(by_slot[:], e, 0, BANDS)
-            rows = keep.tile([P, K], F32, name="gated%d" % e)
-            nc.scalar.activation(rows[:], by_slot[:], COPY, scale=gate_cols[:, e:e + 1])
-            for b in range(BANDS):
-                gated[e, b] = rows[:, b * P:(b + 1) * P]
+        for e in range(E):
+            quantize_q(e)
+        for g, (first, last) in enumerate(GROUPS):
+            width = (last - first) * C
+            for half in range(2):
+                bank = psum.tile([P, K], F32, name="sums%d_%d" % (g, half), offset=((2 * g + half) % 8) * BANK_BYTES)
+                order = [(i, b, e) for i in (DQ, DK, DV) for b in (2 * half, 2 * half + 1) for e in range(first, last)]
+                for i, b, e in order:
+                    h, x = divmod(e, SPAN)
+                    slots = slice(x * C, (x + 1) * C)
+                    codes, plane = stationary(i, e, b)
+                    at = (b % 2) * width + (e - first) * C
+                    nc.tensor.matmul_mx(
+                        out=bank[:, at:at + C], lhsT=codes, lhsT_scale=plane,
+                        rhs=g_words[i, h][:, slots].bitcast(FP8X4), rhs_scale=g_scales[i, h][:, slots],
+                        start=(i, b, e) == order[0], stop=(i, b, e) == order[-1],
+                    )
+                cols = slice(first * C, last * C)
+                for b in (2 * half, 2 * half + 1):
+                    at = (b % 2) * width
+                    nc.vector.tensor_tensor(dx[b][:, cols], bank[:, at:at + width], gate_wide[:, cols], MULT)
 
-        def band_of(b, first, last, bank):
-            by_slot = psum.tile([P, K], F32, name="by_slot%d_%d" % (b, first), offset=bank * BANK_BYTES)
-            for e in range(first, last):
-                multiply(by_slot[:, (e - first) * P:(e - first + 1) * P], e, b, b + 1)
-            rows = ring.tile([P, K], F32, name="gated", tag="gated", bufs=GATED_BUFS)
-            for e in range(first, last):
-                cols = slice((e - first) * P, (e - first + 1) * P)
-                nc.scalar.activation(rows[:, cols], by_slot[:, cols], COPY, scale=gate_cols[:, e:e + 1])
-                gated[e, b] = rows[:, cols]
-
-        def turn_back(b, first, last, bank):
-            by_channel = psum.tile([P, K], F32, name="by_channel%d_%d" % (b, first), offset=bank * BANK_BYTES)
-            for e in range(first, last):
-                nc.tensor.transpose(by_channel[:, (e - first) * C:(e - first + 1) * C], gated[e, b], identity[:])
-            nc.scalar.copy(dx[b][:, first * C:last * C], by_channel[:, 0:(last - first) * C])
-
-        def combine(b):
-            width = T // 2
-            sums = {}
-            for step in range(3):
-                for half in range(2):
-                    sums[step, half] = ring.tile([P, width], F32, name="sums", tag="sums", bufs=SUM_BUFS)
-                    picked = dx[b][:].indirect(pos_sb[step][:, half * width // 16:(half + 1) * width // 16])
-                    if step == 0:
-                        nc.vector.tensor_copy(sums[step, half][:], picked)
-                    else:
-                        nc.vector.tensor_tensor(sums[step, half][:], picked, sums[step - 1, half][:], ADD)
-                    if step == 2:
-                        nc.sync.dma_start(
-                            out=out[b * P:(b + 1) * P, half * width:(half + 1) * width], in_=sums[step, half][:],
-                        )
-
-        nc.sync.dma_start(offs_sb[:], offs)
-        load_d_words(DQ)
-        load_q(0, 0)
-        load_d_words(DK)
-        load_d_scales(DQ)
-        load_q(1, RAW_BYTES)
-        load_d_words(DV)
-        load_d_scales(DK)
-        load_q(2, 2 * RAW_BYTES)
-        load_d_scales(DV)
-        for e in range(3, LANDINGS):
-            load_q(e, e * RAW_BYTES)
-            for j in range(SMALL_RUN * (e - 3), min(SMALL_RUN * (e - 2), 8)):
-                load_kv_scales(j)
-        for i in range(3):
-            nc.sync.dma_start(pos_sb[i][:], (pos1, pos2, pos3)[i])
-
-        for h in range(2):
-            gather_words(DQ, h, keep)
-        gather_scales(DQ, 0, keep)
-        for i in (DK, DV):
-            gather_words(i, 0, keep)
-            gather_scales(i, 0, keep)
-
-        for e in range(QUAD):
-            grouped = stage.tile([P, K, 4], BF16, name="grouped%d" % e, align_bytes=64, offset=e * STAGE_BYTES)
-            round_and_interleave(e, grouped[:], raw[e][:])
-            if e + LANDINGS < VECTOR_FROM:
-                load_q(e + LANDINGS, place_of[e])
-            codes, plane = quantize_columns("whole%d" % e, grouped)
-            q_codes[e, 0] = codes[:]
-            q_plane[e, 0] = plane[:]
-
-        for i in (DQ, DK, DV):
-            if i != DQ:
-                gather_words(i, 1, stage, offset=(1 + i) * STAGE_BYTES)
-            gather_scales(i, 1, stage, offset=(1 + i) * STAGE_BYTES + 4 * LISTED)
-
-        for first, last in GROUPS:
-            n = last - first
-            pool, where = (stage, {"offset": QUAD * STAGE_BYTES}) if last == E else (keep, {})
-            head = pool.tile([P, n * P, 4], BF16, name="head%d" % first, align_bytes=64, **where)
-            rest = pool.tile([P, n * REST, 4], BF16, name="rest%d" % first, align_bytes=64, **where)
-            for e in range(first, last):
-                round_and_interleave(e, head[:, (e - first) * P:(e - first + 1) * P, :], raw[e][:, :, 0:P])
-                if e == last - 1:
-                    head_codes, head_plane = quantize_columns("head%d" % first, head)
-                round_and_interleave(e, rest[:, (e - first) * REST:(e - first + 1) * REST, :], raw[e][:, :, P:K])
-                if e == 4:
-                    load_kv(0, 0, BANDS, place_of[4], place_of[3])
-                elif e in (5, 6):
-                    load_q(e + 4, place_of[e])
-                elif e == 7:
-                    load_band(0, place_of[7])
-                elif e == 8:
-                    load_q(E - 1, place_of[8])
-            rest_codes, rest_plane = quantize_columns("rest%d" % first, rest)
-            for e in range(first, last):
-                cols = slice((e - first) * P, (e - first + 1) * P)
-                q_codes[e, 0] = head_codes[:, cols]
-                q_plane[e, 0] = head_plane[:, cols]
-                for b in range(1, BANDS):
-                    cols = slice((e - first) * REST + (b - 1) * P, (e - first) * REST + b * P)
-                    q_codes[e, b] = rest_codes[:, cols]
-                    q_plane[e, b] = rest_plane[:, cols]
-        for b in range(1, BANDS):
-            load_band(b, place_of[E - BANDS + b])
-
-        for e in range(QUAD):
-            whole_expert(e)
         for b in range(BANDS):
-            turn_back(b, 0, QUAD, 1 + b % 2)
-
-        for (first, last), bank in zip(GROUPS, SLOT_BANKS):
-            band_of(0, first, last, bank)
-        for (first, last), bank in zip(GROUPS, TURN_BANKS):
-            turn_back(0, first, last, bank)
-        combine(0)
-        taken = 0
-        for b in range(1, BANDS):
-            for work in (band_of, turn_back):
-                for u in range(1, QUADS):
-                    work(b, QUAD * u, QUAD * (u + 1), CYCLE[taken % 3])
-                    taken = taken + 1
-            combine(b)
+            parts = [
+                landing.tile([P, T], F32, name="part%d_%d" % (b, j), offset=((3 * b + j) // 2) * RAW_BYTES + ((3 * b + j) % 2) * 4 * T)
+                for j in range(3)
+            ]
+            nc.scalar.activation(parts[0][:], dx[b][:].indirect(pos_sb[0][:]), COPY)
+            if b == 0:
+                nc.vector.tensor_tensor(parts[1][:], dx[b][:].indirect(pos_sb[1][:]), parts[0][:], ADD)
+                nc.vector.tensor_tensor(parts[2][:], dx[b][:].indirect(pos_sb[2][:]), parts[1][:], ADD)
+            else:
+                nc.scalar.activation(parts[1][:], dx[b][:].indirect(pos_sb[1][:]), COPY)
+                nc.vector.tensor_tensor(parts[2][:], dx[b][:].indirect(pos_sb[2][:]), parts[0][:], ADD)
+                nc.vector.tensor_tensor(parts[2][:], parts[2][:], parts[1][:], ADD)
+            nc.sync.dma_start(out=out[b * P:(b + 1) * P, :], in_=parts[2][:])

@@ -28,8 +28,10 @@ SPAN = E // 2
 LISTED = SPAN * C
 WINDOW = 2 * T
 V_ROW = 4
-GROUPS = tuple((e, e + 2) for e in range(0, E, 2))
-KV_AFTER = (7, 11, 11, 11, 11, 11)
+QUAD = 4
+QUADS = E // QUAD
+HALF = K // 2
+EARLY_AFTER = (6, 9, 11)
 RAW_BYTES = 4 * K * 4
 STAGE_BYTES = 4 * K * 2
 LAG = 2
@@ -46,6 +48,7 @@ def tile_moe_qkb_kernel(
     with ExitStack() as ctx:
         keep = ctx.enter_context(tc.tile_pool(name="keep", bufs=1))
         landing = ctx.enter_context(tc.tile_pool(name="landing", bufs=1))
+        turn = ctx.enter_context(tc.tile_pool(name="turn", bufs=1))
         psum = ctx.enter_context(tc.psum_pool(name="psum", bufs=1))
 
         offs_sb = keep.tile([P, S // 16], U16, name="offs_sb")
@@ -55,7 +58,7 @@ def tile_moe_qkb_kernel(
         kv_plane = keep.tile([P, E * K], U8, name="kv_plane", align_bytes=64)
         gate_rows = keep.tile([P, 3, C], F32, name="gate_rows")
         gate_cols = keep.tile([P, 3, 4], F32, name="gate_cols")
-        gate_wide = keep.tile([P, S], F32, name="gate_wide")
+        gate_wide = [turn.tile([P, QUAD * C], F32, name="gate_wide%d" % u, offset=u * 4 * T) for u in range(QUADS)]
         identity = keep.tile([P, P], F32, name="identity")
         dx = [keep.tile([P, S], F32, name="dx%d" % b) for b in range(BANDS)]
 
@@ -98,21 +101,23 @@ def tile_moe_qkb_kernel(
         k_codes = {}
         v_codes = {}
 
-        def load_kv(first, last):
-            n = last - first
-            k_tile = keep.tile([P, n * K * 2], U8, name="k_codes%d" % first, align_bytes=64)
-            v_tile = keep.tile([P, n * K * 4], U8, name="v_codes%d" % first, align_bytes=64)
+        def load_kv(u, half):
+            first = QUAD * u
+            k_tile = keep.tile([P, QUAD * HALF * 2], U8, name="k_codes%d_%d" % (u, half), align_bytes=64)
+            v_tile = keep.tile([P, QUAD * HALF * 4], U8, name="v_codes%d_%d" % (u, half), align_bytes=64)
             nc.sync.dma_start(
-                out=k_tile[:].bitcast(I32).rearrange("p (e c) -> p e c", e=n),
-                in_=wk_words.rearrange("e s p c -> p (e s) c").bitcast(I32)[:, first:last, :],
+                out=k_tile[:].bitcast(I32).rearrange("p (e c) -> p e c", e=QUAD),
+                in_=wk_words.rearrange("e s p c -> p (e s) c").bitcast(I32)[:, first:first + QUAD, half * HALF // 2:(half + 1) * HALF // 2],
             )
             nc.sync.dma_start(
-                out=v_tile[:].bitcast(I32).rearrange("p (e c) -> p e c", e=n),
-                in_=wv_words.rearrange("e s p c d -> p (e s) (c d)").bitcast(I32)[:, first:last, :],
+                out=v_tile[:].bitcast(I32).rearrange("p (e c) -> p e c", e=QUAD),
+                in_=wv_words.rearrange("e s p c d -> p (e s) (c d)").bitcast(I32)[:, first:first + QUAD, half * HALF:(half + 1) * HALF],
             )
-            for e in range(first, last):
-                k_codes[e] = k_tile[:, (e - first) * 2 * K:(e - first + 1) * 2 * K]
-                v_codes[e] = v_tile[:, (e - first) * 4 * K:(e - first + 1) * 4 * K]
+            for x in range(QUAD):
+                for y in range(2):
+                    at = x * HALF + y * P
+                    k_codes[first + x, 2 * half + y] = k_tile[:, 2 * at:2 * (at + P)]
+                    v_codes[first + x, 2 * half + y] = v_tile[:, 4 * at:4 * (at + P)]
 
         small = [(load_d_scales, j) for j in range(12)] + [(load_kv_scales, j) for j in range(8)] + [(load_pos, i) for i in range(3)]
         nc.sync.dma_start(offs_sb[:], offs)
@@ -124,9 +129,11 @@ def tile_moe_qkb_kernel(
             load_q(e)
             for load, j in small[SMALL_RUN * (e - 1):SMALL_RUN * e]:
                 load(j)
-            for group, after in zip(GROUPS, KV_AFTER):
-                if after == e:
-                    load_kv(*group)
+            for u in range(QUADS):
+                if EARLY_AFTER[u] == e:
+                    load_kv(u, 0)
+        for u in range(QUADS):
+            load_kv(u, 1)
 
         gate_bank = psum.tile([P, K], F32, name="gate_bank", offset=7 * BANK_BYTES)
         for x in range(3):
@@ -137,7 +144,7 @@ def tile_moe_qkb_kernel(
             for x in range(4):
                 e = 4 * u + x
                 nc.tensor.transpose(spread[:, x * C:(x + 1) * C], gate_cols[:, e % 3, e // 3:e // 3 + 1].to_broadcast([P, P]), identity[:])
-            nc.scalar.copy(gate_wide[:, u * K:(u + 1) * K], spread[:])
+            nc.scalar.copy(gate_wide[u][:], spread[:])
 
         g_words = {}
         g_scales = {}
@@ -158,19 +165,17 @@ def tile_moe_qkb_kernel(
             grouped = landing.tile([P, K, 4], BF16, name="grouped%d" % e, align_bytes=64, offset=place)
             codes = landing.tile([P, K], U32, name="q_codes%d" % e, align_bytes=64, offset=place + STAGE_BYTES)
             plane = landing.tile([P, K], U8, name="q_plane%d" % e, align_bytes=64, offset=place + STAGE_BYTES + 4 * K)
-            share = K
-            nc.scalar.copy(
-                grouped[:, 0:share, :].rearrange("p (c i) j -> p c j i", i=4),
-                raw[e][:, :, 0:share].rearrange("p j (c i) -> p c j i", i=4),
-            )
-            if share < K:
-                nc.vector.tensor_copy(
-                    grouped[:, share:K, :].rearrange("p (c i) j -> p c j i", i=4),
-                    raw[e][:, :, share:K].rearrange("p j (c i) -> p c j i", i=4),
+            width = HALF if e == E - 1 else K
+            for start in range(0, K, width):
+                cols = slice(start, start + width)
+                nc.scalar.copy(
+                    grouped[:, cols, :].rearrange("p (c i) j -> p c j i", i=4),
+                    raw[e][:, :, cols].rearrange("p j (c i) -> p c j i", i=4),
                 )
-            nc.vector.quantize_mx(
-                out=codes[:].bitcast(FP8X4), scales=plane[:], in_=grouped[:].rearrange("p c j -> p (c j)"),
-            )
+                nc.vector.quantize_mx(
+                    out=codes[:, cols].bitcast(FP8X4), scales=plane[:, cols],
+                    in_=grouped[:, cols, :].rearrange("p c j -> p (c j)"),
+                )
             q_codes[e] = codes
             q_plane[e] = plane
 
@@ -179,42 +184,74 @@ def tile_moe_qkb_kernel(
             if i == DQ:
                 return q_codes[e][:, b * P:(b + 1) * P].bitcast(FP8X4), q_plane[e][:, b * P:(b + 1) * P]
             if i == DK:
-                return k_codes[e][:, b * 2 * P:(b + 1) * 2 * P].bitcast(FP4X4), kv_plane[:, cols]
-            return v_codes[e][:, b * 4 * P:(b + 1) * 4 * P].bitcast(FP8X4), kv_plane[V_ROW:P, cols]
+                return k_codes[e, b].bitcast(FP4X4), kv_plane[:, cols]
+            return v_codes[e, b].bitcast(FP8X4), kv_plane[V_ROW:P, cols]
 
         for e in range(E):
             quantize_q(e)
-        for g, (first, last) in enumerate(GROUPS):
-            width = (last - first) * C
-            for half in range(2):
-                bank = psum.tile([P, K], F32, name="sums%d_%d" % (g, half), offset=((2 * g + half) % 8) * BANK_BYTES)
-                order = [(i, b, e) for i in (DQ, DK, DV) for b in (2 * half, 2 * half + 1) for e in range(first, last)]
-                for i, b, e in order:
-                    h, x = divmod(e, SPAN)
-                    slots = slice(x * C, (x + 1) * C)
-                    codes, plane = stationary(i, e, b)
-                    at = (b % 2) * width + (e - first) * C
-                    nc.tensor.matmul_mx(
-                        out=bank[:, at:at + C], lhsT=codes, lhsT_scale=plane,
-                        rhs=g_words[i, h][:, slots].bitcast(FP8X4), rhs_scale=g_scales[i, h][:, slots],
-                        start=(i, b, e) == order[0], stop=(i, b, e) == order[-1],
-                    )
-                cols = slice(first * C, last * C)
-                for b in (2 * half, 2 * half + 1):
-                    at = (b % 2) * width
-                    nc.vector.tensor_tensor(dx[b][:, cols], bank[:, at:at + width], gate_wide[:, cols], MULT)
 
-        for b in range(BANDS):
-            parts = [
-                landing.tile([P, T], F32, name="part%d_%d" % (b, j), offset=((3 * b + j) // 2) * RAW_BYTES + ((3 * b + j) % 2) * 4 * T)
-                for j in range(3)
-            ]
-            nc.scalar.activation(parts[0][:], dx[b][:].indirect(pos_sb[0][:]), COPY)
-            if b == 0:
-                nc.vector.tensor_tensor(parts[1][:], dx[b][:].indirect(pos_sb[1][:]), parts[0][:], ADD)
-                nc.vector.tensor_tensor(parts[2][:], dx[b][:].indirect(pos_sb[2][:]), parts[1][:], ADD)
-            else:
-                nc.scalar.activation(parts[1][:], dx[b][:].indirect(pos_sb[1][:]), COPY)
-                nc.vector.tensor_tensor(parts[2][:], dx[b][:].indirect(pos_sb[2][:]), parts[0][:], ADD)
-                nc.vector.tensor_tensor(parts[2][:], parts[2][:], parts[1][:], ADD)
-            nc.sync.dma_start(out=out[b * P:(b + 1) * P, :], in_=parts[2][:])
+        def multiply(bank, parts, sorts):
+            order = [(i, n) for i in sorts for n in range(len(parts))]
+            for i, n in order:
+                b, e = parts[n]
+                h, x = divmod(e, SPAN)
+                slots = slice(x * C, (x + 1) * C)
+                codes, plane = stationary(i, e, b)
+                nc.tensor.matmul_mx(
+                    out=bank[:, n * C:(n + 1) * C], lhsT=codes, lhsT_scale=plane,
+                    rhs=g_words[i, h][:, slots].bitcast(FP8X4), rhs_scale=g_scales[i, h][:, slots],
+                    start=(i, n) == order[0], stop=(i, n) == order[-1],
+                )
+
+        for pair in range(E // 2):
+            bank = psum.tile([P, K], F32, name="early%d" % pair, offset=(pair % 2) * BANK_BYTES)
+            multiply(bank, [(b, e) for b in range(2) for e in (2 * pair, 2 * pair + 1)], (DK, DV, DQ) if pair < 4 else (DQ, DK, DV))
+            for b in range(2):
+                nc.vector.tensor_tensor(
+                    dx[b][:, pair * 2 * C:(pair + 1) * 2 * C], bank[:, b * 2 * C:(b + 1) * 2 * C],
+                    gate_wide[pair // 2][:, (pair % 2) * 2 * C:(pair % 2 + 1) * 2 * C], MULT,
+                )
+        for u in range(QUADS):
+            for b in (2, 3):
+                bank = psum.tile([P, K], F32, name="late%d_%d" % (u, b), offset=(2 * u + b) * BANK_BYTES)
+                multiply(bank, [(b, e) for e in range(QUAD * u, QUAD * (u + 1))], (DQ, DK, DV))
+                nc.vector.tensor_tensor(dx[b][:, u * QUAD * C:(u + 1) * QUAD * C], bank[:], gate_wide[u][:], MULT)
+
+        taken = []
+
+        def part(place=None):
+            if place is None:
+                place = len(taken)
+            taken.append(place)
+            return landing.tile(
+                [P, T], F32, name="part%d" % len(taken), offset=(place // 2) * RAW_BYTES + (place % 2) * 4 * T,
+            )
+
+        def on_gate(u):
+            return turn.tile([P, T], F32, name="on_gate%d" % u, offset=u * 4 * T)
+
+        def pick(b, i):
+            picked = part()
+            nc.scalar.activation(picked[:], dx[b][:].indirect(pos_sb[i][:]), COPY)
+            return picked
+
+        def store(b, rows):
+            nc.sync.dma_start(out=out[b * P:(b + 1) * P, :], in_=rows[:])
+
+        first, second = pick(0, 0), pick(0, 1)
+        two = on_gate(0)
+        nc.vector.tensor_tensor(two[:], dx[0][:].indirect(pos_sb[2][:]), first[:], ADD)
+        three = on_gate(2)
+        nc.vector.tensor_tensor(three[:], two[:], second[:], ADD)
+        store(0, three)
+        first, second, third = pick(1, 0), pick(1, 1), pick(1, 2)
+        two = part(1)
+        nc.vector.tensor_tensor(two[:], first[:], second[:], ADD)
+        nc.vector.tensor_tensor(two[:], two[:], third[:], ADD)
+        store(1, two)
+        for b in (2, 3):
+            first, second = pick(b, 0), pick(b, 1)
+            two = part()
+            nc.vector.tensor_tensor(two[:], dx[b][:].indirect(pos_sb[2][:]), first[:], ADD)
+            nc.vector.tensor_tensor(two[:], two[:], second[:], ADD)
+            store(b, two)

@@ -31,7 +31,8 @@ V_ROW = 4
 QUAD = 4
 QUADS = E // QUAD
 HALF = K // 2
-EARLY_AFTER = (6, 9, 11)
+V_CUTS = (((0, 4), (4, 8), (8, 12)), ((0, 12),), ((0, 12),), ((0, 8), (8, 12)))
+V_BAND = E * P * 4
 RAW_BYTES = 4 * K * 4
 STAGE_BYTES = 4 * K * 2
 LAG = 2
@@ -58,7 +59,7 @@ def tile_moe_qkb_kernel(
         kv_plane = keep.tile([P, E * K], U8, name="kv_plane", align_bytes=64)
         gate_rows = keep.tile([P, 3, C], F32, name="gate_rows")
         gate_cols = keep.tile([P, 3, 4], F32, name="gate_cols")
-        gate_wide = [turn.tile([P, QUAD * C], F32, name="gate_wide%d" % u, offset=u * 4 * T) for u in range(QUADS)]
+        gate_wide = [keep.tile([P, QUAD * C], F32, name="gate_wide%d" % u) for u in range(QUADS)]
         identity = keep.tile([P, P], F32, name="identity")
         dx = [keep.tile([P, S], F32, name="dx%d" % b) for b in range(BANDS)]
 
@@ -101,23 +102,28 @@ def tile_moe_qkb_kernel(
         k_codes = {}
         v_codes = {}
 
-        def load_kv(u, half):
-            first = QUAD * u
-            k_tile = keep.tile([P, QUAD * HALF * 2], U8, name="k_codes%d_%d" % (u, half), align_bytes=64)
-            v_tile = keep.tile([P, QUAD * HALF * 4], U8, name="v_codes%d_%d" % (u, half), align_bytes=64)
+        def load_k(half):
+            k_tile = keep.tile([P, E * HALF * 2], U8, name="k_codes%d" % half, align_bytes=64)
             nc.sync.dma_start(
-                out=k_tile[:].bitcast(I32).rearrange("p (e c) -> p e c", e=QUAD),
-                in_=wk_words.rearrange("e s p c -> p (e s) c").bitcast(I32)[:, first:first + QUAD, half * HALF // 2:(half + 1) * HALF // 2],
+                out=k_tile[:].bitcast(I32).rearrange("p (e c) -> p e c", e=E),
+                in_=wk_words.rearrange("e s p c -> p (e s) c").bitcast(I32)[:, :, half * HALF // 2:(half + 1) * HALF // 2],
             )
-            nc.sync.dma_start(
-                out=v_tile[:].bitcast(I32).rearrange("p (e c) -> p e c", e=QUAD),
-                in_=wv_words.rearrange("e s p c d -> p (e s) (c d)").bitcast(I32)[:, first:first + QUAD, half * HALF:(half + 1) * HALF],
-            )
-            for x in range(QUAD):
+            for e in range(E):
                 for y in range(2):
-                    at = x * HALF + y * P
-                    k_codes[first + x, 2 * half + y] = k_tile[:, 2 * at:2 * (at + P)]
-                    v_codes[first + x, 2 * half + y] = v_tile[:, 4 * at:4 * (at + P)]
+                    at = e * HALF + y * P
+                    k_codes[e, 2 * half + y] = k_tile[:, 2 * at:2 * (at + P)]
+
+        def load_v(b, first, last):
+            n = last - first
+            v_tile = turn.tile(
+                [P, n * P * 4], U8, name="v_codes%d_%d" % (b, first), align_bytes=64, offset=b * V_BAND + first * P * 4,
+            )
+            nc.sync.dma_start(
+                out=v_tile[:].bitcast(I32).rearrange("p (e c) -> p e c", e=n),
+                in_=wv_words.rearrange("e s p c d -> p (e s) (c d)").bitcast(I32)[:, first:last, b * P:(b + 1) * P],
+            )
+            for e in range(first, last):
+                v_codes[e, b] = v_tile[:, (e - first) * 4 * P:(e - first + 1) * 4 * P]
 
         small = [(load_d_scales, j) for j in range(12)] + [(load_kv_scales, j) for j in range(8)] + [(load_pos, i) for i in range(3)]
         nc.sync.dma_start(offs_sb[:], offs)
@@ -126,14 +132,16 @@ def tile_moe_qkb_kernel(
         load_d_words(DK)
         load_d_words(DV)
         for e in range(1, E):
+            if e == E - 1:
+                load_k(0)
             load_q(e)
             for load, j in small[SMALL_RUN * (e - 1):SMALL_RUN * e]:
                 load(j)
-            for u in range(QUADS):
-                if EARLY_AFTER[u] == e:
-                    load_kv(u, 0)
-        for u in range(QUADS):
-            load_kv(u, 1)
+        for b in range(BANDS):
+            if b == 2:
+                load_k(1)
+            for first, last in V_CUTS[b]:
+                load_v(b, first, last)
 
         gate_bank = psum.tile([P, K], F32, name="gate_bank", offset=7 * BANK_BYTES)
         for x in range(3):
@@ -165,9 +173,7 @@ def tile_moe_qkb_kernel(
             grouped = landing.tile([P, K, 4], BF16, name="grouped%d" % e, align_bytes=64, offset=place)
             codes = landing.tile([P, K], U32, name="q_codes%d" % e, align_bytes=64, offset=place + STAGE_BYTES)
             plane = landing.tile([P, K], U8, name="q_plane%d" % e, align_bytes=64, offset=place + STAGE_BYTES + 4 * K)
-            width = HALF if e == E - 1 else K
-            for start in range(0, K, width):
-                cols = slice(start, start + width)
+            for cols in (slice(0, P), slice(P, K)) if e == E - 1 else (slice(0, K),):
                 nc.scalar.copy(
                     grouped[:, cols, :].rearrange("p (c i) j -> p c j i", i=4),
                     raw[e][:, :, cols].rearrange("p j (c i) -> p c j i", i=4),
@@ -203,55 +209,48 @@ def tile_moe_qkb_kernel(
                     start=(i, n) == order[0], stop=(i, n) == order[-1],
                 )
 
-        for pair in range(E // 2):
-            bank = psum.tile([P, K], F32, name="early%d" % pair, offset=(pair % 2) * BANK_BYTES)
-            multiply(bank, [(b, e) for b in range(2) for e in (2 * pair, 2 * pair + 1)], (DK, DV, DQ) if pair < 4 else (DQ, DK, DV))
-            for b in range(2):
-                nc.vector.tensor_tensor(
-                    dx[b][:, pair * 2 * C:(pair + 1) * 2 * C], bank[:, b * 2 * C:(b + 1) * 2 * C],
-                    gate_wide[pair // 2][:, (pair % 2) * 2 * C:(pair % 2 + 1) * 2 * C], MULT,
-                )
-        for u in range(QUADS):
-            for b in (2, 3):
-                bank = psum.tile([P, K], F32, name="late%d_%d" % (u, b), offset=(2 * u + b) * BANK_BYTES)
+        for b in range(BANDS):
+            for u in range(QUADS):
+                bank = psum.tile([P, K], F32, name="sums%d_%d" % (b, u), offset=((QUADS * b + u) % 8) * BANK_BYTES)
                 multiply(bank, [(b, e) for e in range(QUAD * u, QUAD * (u + 1))], (DQ, DK, DV))
                 nc.vector.tensor_tensor(dx[b][:, u * QUAD * C:(u + 1) * QUAD * C], bank[:], gate_wide[u][:], MULT)
 
         taken = []
 
-        def part(place=None):
-            if place is None:
-                place = len(taken)
+        def spare():
+            place = len(taken)
             taken.append(place)
             return landing.tile(
-                [P, T], F32, name="part%d" % len(taken), offset=(place // 2) * RAW_BYTES + (place % 2) * 4 * T,
+                [P, T], F32, name="spare%d" % place, offset=(place // 2) * RAW_BYTES + (place % 2) * 4 * T,
             )
 
-        def on_gate(u):
-            return turn.tile([P, T], F32, name="on_gate%d" % u, offset=u * 4 * T)
+        def behind(b, u):
+            taken.append(None)
+            return turn.tile([P, T], F32, name="behind%d" % len(taken), offset=b * V_BAND + u * 4 * T)
 
         def pick(b, i):
-            picked = part()
+            picked = spare()
             nc.scalar.activation(picked[:], dx[b][:].indirect(pos_sb[i][:]), COPY)
             return picked
 
         def store(b, rows):
             nc.sync.dma_start(out=out[b * P:(b + 1) * P, :], in_=rows[:])
 
-        first, second = pick(0, 0), pick(0, 1)
-        two = on_gate(0)
-        nc.vector.tensor_tensor(two[:], dx[0][:].indirect(pos_sb[2][:]), first[:], ADD)
-        three = on_gate(2)
-        nc.vector.tensor_tensor(three[:], two[:], second[:], ADD)
-        store(0, three)
-        first, second, third = pick(1, 0), pick(1, 1), pick(1, 2)
-        two = part(1)
-        nc.vector.tensor_tensor(two[:], first[:], second[:], ADD)
-        nc.vector.tensor_tensor(two[:], two[:], third[:], ADD)
-        store(1, two)
+        for b in (0, 1):
+            first, second = pick(b, 0), pick(b, 1)
+            if b == 0:
+                third = pick(b, 2)
+                first, third = third, first
+                first, second = second, first
+            else:
+                third = spare()
+                nc.vector.tensor_copy(third[:], dx[b][:].indirect(pos_sb[2][:]))
+            nc.gpsimd.tensor_tensor(third[:], third[:], first[:], ADD)
+            nc.gpsimd.tensor_tensor(third[:], third[:], second[:], ADD)
+            store(b, third)
         for b in (2, 3):
             first, second = pick(b, 0), pick(b, 1)
-            two = part()
+            two = behind(3, 2) if b == 2 else spare()
             nc.vector.tensor_tensor(two[:], dx[b][:].indirect(pos_sb[2][:]), first[:], ADD)
             nc.vector.tensor_tensor(two[:], two[:], second[:], ADD)
             store(b, two)

@@ -22,22 +22,33 @@ C = 128
 S = E * C
 K = 512
 BANDS = K // P
+HALF = K // 2
+QUAD = 4
+QUADS = E // QUAD
+LAST = E - 1
 DQ, DK, DV = 0, 1, 2
 
 SPAN = E // 2
 LISTED = SPAN * C
 WINDOW = 2 * T
 V_ROW = 4
-QUAD = 4
-QUADS = E // QUAD
-HALF = K // 2
-V_CUTS = (((0, 4), (4, 8), (8, 12)), ((0, 12),), ((0, 12),), ((0, 8), (8, 12)))
-V_BAND = E * P * 4
+GATE_ROWS = 4
+GATE_RUN = E // GATE_ROWS
+
+BY_QUAD = tuple((first, first + QUAD) for first in range(0, E, QUAD))
+V_CUTS = (BY_QUAD, ((0, E),), BY_QUAD, ((0, E - QUAD), (E - QUAD, E)))
+Q_GROUPS = tuple((first, first + 2) for first in range(0, E - 2, 2)) + ((E - 2, E - 1),)
+SMALL_RUN = 3
+
 RAW_BYTES = 4 * K * 4
 STAGE_BYTES = 4 * K * 2
 LAG = 2
-SMALL_RUN = 3
+V_BAND = E * P * 4
+PICK_BYTES = 4 * T
 BANK_BYTES = 2048
+BANKS = 8
+GATE_BANK = 7
+SPREAD_BANK = 4
 FLOPS = 2 * 3 * 512 * K * S
 
 
@@ -49,7 +60,7 @@ def tile_moe_qkb_kernel(
     with ExitStack() as ctx:
         keep = ctx.enter_context(tc.tile_pool(name="keep", bufs=1))
         landing = ctx.enter_context(tc.tile_pool(name="landing", bufs=1))
-        turn = ctx.enter_context(tc.tile_pool(name="turn", bufs=1))
+        v_pool = ctx.enter_context(tc.tile_pool(name="v_pool", bufs=1))
         psum = ctx.enter_context(tc.psum_pool(name="psum", bufs=1))
 
         offs_sb = keep.tile([P, S // 16], U16, name="offs_sb")
@@ -57,8 +68,8 @@ def tile_moe_qkb_kernel(
         d_words = [keep.tile([P, WINDOW], I32, name="d_words%d" % i, align_bytes=64) for i in range(3)]
         d_scales = [keep.tile([P, WINDOW], U8, name="d_scales%d" % i, align_bytes=64) for i in range(3)]
         kv_plane = keep.tile([P, E * K], U8, name="kv_plane", align_bytes=64)
-        gate_rows = keep.tile([P, 3, C], F32, name="gate_rows")
-        gate_cols = keep.tile([P, 3, 4], F32, name="gate_cols")
+        gate_rows = keep.tile([P, GATE_RUN, C], F32, name="gate_rows")
+        gate_cols = keep.tile([P, GATE_RUN, GATE_ROWS], F32, name="gate_cols")
         gate_wide = [keep.tile([P, QUAD * C], F32, name="gate_wide%d" % u) for u in range(QUADS)]
         identity = keep.tile([P, P], F32, name="identity")
         dx = [keep.tile([P, S], F32, name="dx%d" % b) for b in range(BANDS)]
@@ -67,10 +78,9 @@ def tile_moe_qkb_kernel(
         make_identity(nc, identity[:])
         for i in range(3):
             nc.gpsimd.memset(d_scales[i][:].bitcast(I32), 0)
-        nc.gpsimd.memset(kv_plane[:].bitcast(I32), 0)
+        nc.vector.memset(kv_plane[:].bitcast(I32), 0)
         for i in range(3):
             nc.vector.memset(d_words[i][:, T:WINDOW], 0)
-        nc.sync.dma_start(out=gate_rows[0:4], in_=gate[0].rearrange("(q x u) -> q x u", q=4, x=3))
 
         def load_d_words(i):
             src = (dq_words, dk_words, dv_words)[i]
@@ -85,7 +95,7 @@ def tile_moe_qkb_kernel(
 
         def load_kv_scales(j):
             which, r = divmod(j, 4)
-            nc.sync.dma_start(
+            nc.gpsimd.dma_start(
                 out=kv_plane[which * V_ROW + r:P:32, :].bitcast(I32).rearrange("q (e c) -> q e c", e=E),
                 in_=(wk_scales, wv_scales)[which].rearrange("e s (q r) c -> r q (e s) c", r=4)[r].bitcast(I32),
             )
@@ -115,7 +125,7 @@ def tile_moe_qkb_kernel(
 
         def load_v(b, first, last):
             n = last - first
-            v_tile = turn.tile(
+            v_tile = v_pool.tile(
                 [P, n * P * 4], U8, name="v_codes%d_%d" % (b, first), align_bytes=64, offset=b * V_BAND + first * P * 4,
             )
             nc.sync.dma_start(
@@ -125,16 +135,20 @@ def tile_moe_qkb_kernel(
             for e in range(first, last):
                 v_codes[e, b] = v_tile[:, (e - first) * 4 * P:(e - first + 1) * 4 * P]
 
-        small = [(load_d_scales, j) for j in range(12)] + [(load_kv_scales, j) for j in range(8)] + [(load_pos, i) for i in range(3)]
+        nc.sync.dma_start(out=gate_rows[0:GATE_ROWS], in_=gate[0].rearrange("(q x u) -> q x u", q=GATE_ROWS, x=GATE_RUN))
+        for j in range(8):
+            load_kv_scales(j)
+        small = [(load_d_scales, j) for j in range(12)] + [(load_pos, i) for i in range(3)]
         nc.sync.dma_start(offs_sb[:], offs)
         load_d_words(DQ)
         load_q(0)
         load_d_words(DK)
-        load_d_words(DV)
         for e in range(1, E):
-            if e == E - 1:
+            if e == LAST:
                 load_k(0)
             load_q(e)
+            if e == 1:
+                load_d_words(DV)
             for load, j in small[SMALL_RUN * (e - 1):SMALL_RUN * e]:
                 load(j)
         for b in range(BANDS):
@@ -143,114 +157,134 @@ def tile_moe_qkb_kernel(
             for first, last in V_CUTS[b]:
                 load_v(b, first, last)
 
-        gate_bank = psum.tile([P, K], F32, name="gate_bank", offset=7 * BANK_BYTES)
-        for x in range(3):
+        gate_bank = psum.tile([P, K], F32, name="gate_bank", offset=GATE_BANK * BANK_BYTES)
+        for x in range(GATE_RUN):
             nc.tensor.transpose(gate_bank[:, x * P:(x + 1) * P], gate_rows[:, x, :], identity[:])
-        nc.scalar.activation(gate_cols[:], gate_bank[:].rearrange("p (x q) -> p x q", q=P)[:, 0:3, 0:4], COPY)
-        for u in range(E // 4):
-            spread = psum.tile([P, K], F32, name="spread%d" % u, offset=(4 + u) * BANK_BYTES)
-            for x in range(4):
-                e = 4 * u + x
-                nc.tensor.transpose(spread[:, x * C:(x + 1) * C], gate_cols[:, e % 3, e // 3:e // 3 + 1].to_broadcast([P, P]), identity[:])
+        nc.scalar.activation(
+            gate_cols[:], gate_bank[:].rearrange("p (x q) -> p x q", q=P)[:, 0:GATE_RUN, 0:GATE_ROWS], COPY,
+        )
+        for u in range(QUADS):
+            spread = psum.tile([P, K], F32, name="spread%d" % u, offset=(SPREAD_BANK + u) * BANK_BYTES)
+            for x in range(QUAD):
+                row, run = divmod(QUAD * u + x, GATE_RUN)
+                column = gate_cols[:, run, row:row + 1].to_broadcast([P, P])
+                nc.tensor.transpose(spread[:, x * C:(x + 1) * C], column, identity[:])
             nc.scalar.copy(gate_wide[u][:], spread[:])
 
         g_words = {}
         g_scales = {}
-        for h in range(2):
-            part = offs_sb[:, h * LISTED // 16:(h + 1) * LISTED // 16]
+        for h in range(E // SPAN):
+            listed = offs_sb[:, h * LISTED // 16:(h + 1) * LISTED // 16]
             for i in (DQ, DK, DV):
                 g_words[i, h] = keep.tile([P, LISTED], U32, name="g_words%d_%d" % (i, h), align_bytes=64)
-                nc.vector.tensor_copy(g_words[i, h][:], d_words[i][:].bitcast(U32).indirect(part))
+                nc.vector.tensor_copy(g_words[i, h][:], d_words[i][:].bitcast(U32).indirect(listed))
             for i in (DQ, DK, DV):
                 g_scales[i, h] = keep.tile([P, LISTED], U8, name="g_scales%d_%d" % (i, h), align_bytes=64)
-                nc.vector.tensor_copy(g_scales[i, h][:], d_scales[i][:].indirect(part))
+                nc.vector.tensor_copy(g_scales[i, h][:], d_scales[i][:].indirect(listed))
 
         q_codes = {}
         q_plane = {}
 
-        def quantize_q(e):
-            place = e * RAW_BYTES
-            grouped = landing.tile([P, K, 4], BF16, name="grouped%d" % e, align_bytes=64, offset=place)
-            codes = landing.tile([P, K], U32, name="q_codes%d" % e, align_bytes=64, offset=place + STAGE_BYTES)
-            plane = landing.tile([P, K], U8, name="q_plane%d" % e, align_bytes=64, offset=place + STAGE_BYTES + 4 * K)
-            for cols in (slice(0, P), slice(P, K)) if e == E - 1 else (slice(0, K),):
-                nc.scalar.copy(
-                    grouped[:, cols, :].rearrange("p (c i) j -> p c j i", i=4),
-                    raw[e][:, :, cols].rearrange("p j (c i) -> p c j i", i=4),
-                )
-                nc.vector.quantize_mx(
-                    out=codes[:, cols].bitcast(FP8X4), scales=plane[:, cols],
-                    in_=grouped[:, cols, :].rearrange("p c j -> p (c j)"),
-                )
-            q_codes[e] = codes
-            q_plane[e] = plane
+        def round_q(copy, grouped, rows):
+            copy(grouped.rearrange("p (c i) j -> p c j i", i=4), rows.rearrange("p j (c i) -> p c j i", i=4))
+
+        def quantize_q(grouped, pieces, pool, place):
+            width = P * len(pieces)
+            name = "%d_%d" % pieces[0]
+            codes = pool.tile([P, width], U32, name="q_codes" + name, align_bytes=64, offset=place)
+            plane = pool.tile([P, width], U8, name="q_plane" + name, align_bytes=64, offset=place + 4 * width)
+            nc.vector.quantize_mx(
+                out=codes[:].bitcast(FP8X4), scales=plane[:], in_=grouped.rearrange("p c j -> p (c j)"),
+            )
+            for n, piece in enumerate(pieces):
+                q_codes[piece] = codes[:, n * P:(n + 1) * P]
+                q_plane[piece] = plane[:, n * P:(n + 1) * P]
+
+        for first, last in Q_GROUPS:
+            grouped = landing.tile(
+                [P, (last - first) * K, 4], BF16, name="grouped%d" % first, align_bytes=64, offset=first * RAW_BYTES,
+            )
+            for e in range(first, last):
+                if e == LAST - 1:
+                    round_q(nc.scalar.copy, grouped[:, 0:HALF, :], raw[e][:, :, 0:HALF])
+                    round_q(nc.vector.tensor_copy, grouped[:, HALF:K, :], raw[e][:, :, HALF:K])
+                else:
+                    round_q(nc.scalar.copy, grouped[:, (e - first) * K:(e - first + 1) * K, :], raw[e][:])
+            pieces = [(e, b) for e in range(first, last) for b in range(BANDS)]
+            quantize_q(grouped[:], pieces, landing, first * RAW_BYTES + (last - first) * STAGE_BYTES)
+        last_grouped = landing.tile([P, K, 4], BF16, name="grouped_last", align_bytes=64, offset=LAST * RAW_BYTES)
+        round_q(nc.scalar.copy, last_grouped[:, 0:P, :], raw[LAST][:, :, 0:P])
+        quantize_q(last_grouped[:, 0:P, :], [(LAST, 0)], landing, LAST * RAW_BYTES + STAGE_BYTES)
+        round_q(nc.scalar.copy, last_grouped[:, P:K, :], raw[LAST][:, :, P:K])
 
         def stationary(i, e, b):
             cols = slice(e * K + b * P, e * K + (b + 1) * P)
             if i == DQ:
-                return q_codes[e][:, b * P:(b + 1) * P].bitcast(FP8X4), q_plane[e][:, b * P:(b + 1) * P]
+                return q_codes[e, b].bitcast(FP8X4), q_plane[e, b]
             if i == DK:
                 return k_codes[e, b].bitcast(FP4X4), kv_plane[:, cols]
             return v_codes[e, b].bitcast(FP8X4), kv_plane[V_ROW:P, cols]
 
-        for e in range(E):
-            quantize_q(e)
-
-        def multiply(bank, parts, sorts):
-            order = [(i, n) for i in sorts for n in range(len(parts))]
-            for i, n in order:
-                b, e = parts[n]
+        def multiply(bank, b, u):
+            experts = range(QUAD * u, QUAD * (u + 1))
+            late = [(DQ, LAST)] if LAST in experts and b < 2 else []
+            order = [(DQ, e) for e in experts if (DQ, e) not in late] + [(DK, e) for e in experts]
+            order = order + late + [(DV, e) for e in experts]
+            for i, e in order:
                 h, x = divmod(e, SPAN)
                 slots = slice(x * C, (x + 1) * C)
                 codes, plane = stationary(i, e, b)
                 nc.tensor.matmul_mx(
-                    out=bank[:, n * C:(n + 1) * C], lhsT=codes, lhsT_scale=plane,
+                    out=bank[:, (e % QUAD) * C:(e % QUAD + 1) * C], lhsT=codes, lhsT_scale=plane,
                     rhs=g_words[i, h][:, slots].bitcast(FP8X4), rhs_scale=g_scales[i, h][:, slots],
-                    start=(i, n) == order[0], stop=(i, n) == order[-1],
+                    start=(i, e) == order[0], stop=(i, e) == order[-1],
                 )
 
         for b in range(BANDS):
+            if b == 1:
+                rest = [(LAST, n) for n in range(1, BANDS)]
+                quantize_q(last_grouped[:, P:K, :], rest, v_pool, V_BAND - (4 + 1) * P * len(rest))
             for u in range(QUADS):
-                bank = psum.tile([P, K], F32, name="sums%d_%d" % (b, u), offset=((QUADS * b + u) % 8) * BANK_BYTES)
-                multiply(bank, [(b, e) for e in range(QUAD * u, QUAD * (u + 1))], (DQ, DK, DV))
+                number = (QUADS * max(b - 1, 0) + u) % BANKS
+                bank = psum.tile([P, K], F32, name="sums%d_%d" % (b, u), offset=number * BANK_BYTES)
+                multiply(bank, b, u)
                 nc.vector.tensor_tensor(dx[b][:, u * QUAD * C:(u + 1) * QUAD * C], bank[:], gate_wide[u][:], MULT)
 
-        taken = []
+        def token_tile(b, n):
+            place, at = divmod(3 * b + n, RAW_BYTES // PICK_BYTES)
+            return landing.tile([P, T], F32, name="tokens%d_%d" % (b, n), offset=2 * place * RAW_BYTES + at * PICK_BYTES)
 
-        def spare():
-            place = len(taken)
-            taken.append(place)
-            return landing.tile(
-                [P, T], F32, name="spare%d" % place, offset=(place // 2) * RAW_BYTES + (place % 2) * 4 * T,
-            )
-
-        def behind(b, u):
-            taken.append(None)
-            return turn.tile([P, T], F32, name="behind%d" % len(taken), offset=b * V_BAND + u * 4 * T)
-
-        def pick(b, i):
-            picked = spare()
-            nc.scalar.activation(picked[:], dx[b][:].indirect(pos_sb[i][:]), COPY)
-            return picked
-
-        def store(b, rows):
-            nc.sync.dma_start(out=out[b * P:(b + 1) * P, :], in_=rows[:])
+        def picked(b, i, first=0, last=T):
+            return dx[b][:].indirect(pos_sb[i][:, first // 16:last // 16])
 
         for b in (0, 1):
-            first, second = pick(b, 0), pick(b, 1)
-            if b == 0:
-                third = pick(b, 2)
-                first, third = third, first
-                first, second = second, first
-            else:
-                third = spare()
-                nc.vector.tensor_copy(third[:], dx[b][:].indirect(pos_sb[2][:]))
-            nc.gpsimd.tensor_tensor(third[:], third[:], first[:], ADD)
-            nc.gpsimd.tensor_tensor(third[:], third[:], second[:], ADD)
-            store(b, third)
+            picks = [token_tile(b, i) for i in range(3)]
+            for i in range(3):
+                if (b, i) == (1, 2):
+                    nc.vector.tensor_copy(picks[i][:], picked(b, i))
+                else:
+                    nc.scalar.activation(picks[i][:], picked(b, i), COPY)
+            total, sooner, later = picks if b == 0 else (picks[2], picks[0], picks[1])
+            nc.gpsimd.tensor_tensor(total[:], total[:], sooner[:], ADD)
+            nc.gpsimd.tensor_tensor(total[:], total[:], later[:], ADD)
+            nc.sync.dma_start(out=out[b * P:(b + 1) * P, :], in_=total[:])
+
+        halves = ((0, T // 2), (T // 2, T))
         for b in (2, 3):
-            first, second = pick(b, 0), pick(b, 1)
-            two = behind(3, 2) if b == 2 else spare()
-            nc.vector.tensor_tensor(two[:], dx[b][:].indirect(pos_sb[2][:]), first[:], ADD)
-            nc.vector.tensor_tensor(two[:], two[:], second[:], ADD)
-            store(b, two)
+            final = b == BANDS - 1
+            picks = [token_tile(b, i) for i in range(2)]
+            for i in range(2):
+                for first, last in halves if final else ((0, T),):
+                    nc.scalar.activation(picks[i][:, first:last], picked(b, i, first, last), COPY)
+            if final:
+                total = token_tile(b, 2)
+            else:
+                total = v_pool.tile([P, T], F32, name="tokens2_sum", offset=BANDS * V_BAND - PICK_BYTES)
+            for first, last in halves:
+                nc.vector.tensor_tensor(total[:, first:last], picked(b, 2, first, last), picks[0][:, first:last], ADD)
+            for first, last in halves:
+                nc.vector.tensor_tensor(total[:, first:last], total[:, first:last], picks[1][:, first:last], ADD)
+                if final:
+                    nc.sync.dma_start(out=out[b * P:(b + 1) * P, first:last], in_=total[:, first:last])
+            if not final:
+                nc.sync.dma_start(out=out[b * P:(b + 1) * P, :], in_=total[:])

@@ -38,7 +38,8 @@ GATE_RUN = E // GATE_ROWS
 BY_QUAD = tuple((first, first + QUAD) for first in range(0, E, QUAD))
 V_CUTS = (BY_QUAD, ((0, E),), BY_QUAD, ((0, E - QUAD), (E - QUAD, E)))
 Q_GROUPS = tuple((first, first + 2) for first in range(0, E - 2, 2)) + ((E - 2, E - 1),)
-SMALL_RUN = 3
+SMALL_RUN = 2
+POS_BEHIND = {0: (0,), 1: (1, 2)}
 
 RAW_BYTES = 4 * K * 4
 STAGE_BYTES = 4 * K * 2
@@ -138,7 +139,6 @@ def tile_moe_qkb_kernel(
         nc.sync.dma_start(out=gate_rows[0:GATE_ROWS], in_=gate[0].rearrange("(q x u) -> q x u", q=GATE_ROWS, x=GATE_RUN))
         for j in range(8):
             load_kv_scales(j)
-        small = [(load_d_scales, j) for j in range(12)] + [(load_pos, i) for i in range(3)]
         nc.sync.dma_start(offs_sb[:], offs)
         load_d_words(DQ)
         load_q(0)
@@ -149,13 +149,15 @@ def tile_moe_qkb_kernel(
             load_q(e)
             if e == 1:
                 load_d_words(DV)
-            for load, j in small[SMALL_RUN * (e - 1):SMALL_RUN * e]:
-                load(j)
+            for j in range(SMALL_RUN * (e - 1), min(SMALL_RUN * e, 12)):
+                load_d_scales(j)
         for b in range(BANDS):
             if b == 2:
                 load_k(1)
             for first, last in V_CUTS[b]:
                 load_v(b, first, last)
+            for i in POS_BEHIND.get(b, ()):
+                load_pos(i)
 
         gate_bank = psum.tile([P, K], F32, name="gate_bank", offset=GATE_BANK * BANK_BYTES)
         for x in range(GATE_RUN):

@@ -32,8 +32,8 @@ SPAN = E // 2
 LISTED = SPAN * C
 WINDOW = 2 * T
 V_ROW = 4
-GATE_ROWS = 4
-GATE_RUN = E // GATE_ROWS
+GATE_RUN = S // P
+LINE = 4
 
 BY_QUAD = tuple((first, first + QUAD) for first in range(0, E, QUAD))
 V_CUTS = (BY_QUAD, ((0, E),), BY_QUAD, ((0, E - QUAD), (E - QUAD, E)))
@@ -48,8 +48,7 @@ V_BAND = E * P * 4
 PICK_BYTES = 4 * T
 BANK_BYTES = 2048
 BANKS = 8
-GATE_BANK = 7
-SPREAD_BANK = 4
+SPREAD_BANK = 5
 FLOPS = 2 * 3 * 512 * K * S
 
 
@@ -69,13 +68,11 @@ def tile_moe_qkb_kernel(
         d_words = [keep.tile([P, WINDOW], I32, name="d_words%d" % i, align_bytes=64) for i in range(3)]
         d_scales = [keep.tile([P, WINDOW], U8, name="d_scales%d" % i, align_bytes=64) for i in range(3)]
         kv_plane = keep.tile([P, E * K], U8, name="kv_plane", align_bytes=64)
-        gate_rows = keep.tile([P, GATE_RUN, C], F32, name="gate_rows")
-        gate_cols = keep.tile([P, GATE_RUN, GATE_ROWS], F32, name="gate_cols")
-        gate_wide = [keep.tile([P, QUAD * C], F32, name="gate_wide%d" % u) for u in range(QUADS)]
+        gate_cols = keep.tile([P, GATE_RUN], F32, name="gate_cols")
+        gate_wide = keep.tile([P, S], F32, name="gate_wide")
         identity = keep.tile([P, P], F32, name="identity")
         dx = [keep.tile([P, S], F32, name="dx%d" % b) for b in range(BANDS)]
 
-        nc.gpsimd.memset(gate_rows[:], 0.0)
         make_identity(nc, identity[:])
         for i in range(3):
             nc.gpsimd.memset(d_scales[i][:].bitcast(I32), 0)
@@ -136,11 +133,11 @@ def tile_moe_qkb_kernel(
             for e in range(first, last):
                 v_codes[e, b] = v_tile[:, (e - first) * 4 * P:(e - first + 1) * 4 * P]
 
-        nc.sync.dma_start(out=gate_rows[0:GATE_ROWS], in_=gate[0].rearrange("(q x u) -> q x u", q=GATE_ROWS, x=GATE_RUN))
         for j in range(8):
             load_kv_scales(j)
-        nc.sync.dma_start(offs_sb[:], offs)
         load_d_words(DQ)
+        nc.sync.dma_start(offs_sb[:], offs)
+        nc.sync.dma_start(out=gate_cols[:], in_=gate[0].rearrange("(p x) -> p x", x=GATE_RUN))
         load_q(0)
         load_d_words(DK)
         for e in range(1, E):
@@ -159,19 +156,15 @@ def tile_moe_qkb_kernel(
             for i in POS_BEHIND.get(b, ()):
                 load_pos(i)
 
-        gate_bank = psum.tile([P, K], F32, name="gate_bank", offset=GATE_BANK * BANK_BYTES)
-        for x in range(GATE_RUN):
-            nc.tensor.transpose(gate_bank[:, x * P:(x + 1) * P], gate_rows[:, x, :], identity[:])
-        nc.scalar.activation(
-            gate_cols[:], gate_bank[:].rearrange("p (x q) -> p x q", q=P)[:, 0:GATE_RUN, 0:GATE_ROWS], COPY,
-        )
-        for u in range(QUADS):
-            spread = psum.tile([P, K], F32, name="spread%d" % u, offset=(SPREAD_BANK + u) * BANK_BYTES)
-            for x in range(QUAD):
-                row, run = divmod(QUAD * u + x, GATE_RUN)
-                column = gate_cols[:, run, row:row + 1].to_broadcast([P, P])
-                nc.tensor.transpose(spread[:, x * C:(x + 1) * C], column, identity[:])
-            nc.scalar.copy(gate_wide[u][:], spread[:])
+        for y in range(GATE_RUN // LINE):
+            spread = psum.tile([P, LINE, P], F32, name="spread%d" % y, offset=(SPREAD_BANK + y) * BANK_BYTES)
+            for x in range(LINE):
+                at = LINE * y + x
+                nc.tensor.transpose(spread[:, x, :], gate_cols[:, at:at + 1].to_broadcast([P, P]), identity[:])
+            nc.scalar.copy(
+                gate_wide[:].rearrange("q (p x) -> q p x", x=GATE_RUN)[:, :, LINE * y:LINE * (y + 1)],
+                spread[:].rearrange("q x p -> q p x"),
+            )
 
         g_words = {}
         g_scales = {}
@@ -250,7 +243,8 @@ def tile_moe_qkb_kernel(
                 number = (QUADS * max(b - 1, 0) + u) % BANKS
                 bank = psum.tile([P, K], F32, name="sums%d_%d" % (b, u), offset=number * BANK_BYTES)
                 multiply(bank, b, u)
-                nc.vector.tensor_tensor(dx[b][:, u * QUAD * C:(u + 1) * QUAD * C], bank[:], gate_wide[u][:], MULT)
+                cols = slice(u * QUAD * C, (u + 1) * QUAD * C)
+                nc.vector.tensor_tensor(dx[b][:, cols], bank[:], gate_wide[:, cols], MULT)
 
         def token_tile(b, n):
             place, at = divmod(3 * b + n, RAW_BYTES // PICK_BYTES)

@@ -73,12 +73,13 @@ def tile_moe_qkb_kernel(
         identity = keep.tile([P, P], F32, name="identity")
         dx = [keep.tile([P, S], F32, name="dx%d" % b) for b in range(BANDS)]
 
+        nc.vector.memset(d_words[DQ][:, T:WINDOW], 0)
         make_identity(nc, identity[:])
         for i in range(3):
             nc.gpsimd.memset(d_scales[i][:].bitcast(I32), 0)
-        nc.vector.memset(kv_plane[:].bitcast(I32), 0)
-        for i in range(3):
-            nc.vector.memset(d_words[i][:, T:WINDOW], 0)
+        for i in (DK, DV):
+            nc.gpsimd.memset(d_words[i][:, T:WINDOW], 0)
+        nc.gpsimd.memset(kv_plane[:].bitcast(I32), 0)
 
         def load_d_words(i):
             src = (dq_words, dk_words, dv_words)[i]
@@ -210,7 +211,10 @@ def tile_moe_qkb_kernel(
         last_grouped = landing.tile([P, K, 4], BF16, name="grouped_last", align_bytes=64, offset=LAST * RAW_BYTES)
         round_q(nc.scalar.copy, last_grouped[:, 0:P, :], raw[LAST][:, :, 0:P])
         quantize_q(last_grouped[:, 0:P, :], [(LAST, 0)], landing, LAST * RAW_BYTES + STAGE_BYTES)
-        round_q(nc.scalar.copy, last_grouped[:, P:K, :], raw[LAST][:, :, P:K])
+        round_q(nc.scalar.copy, last_grouped[:, P:HALF, :], raw[LAST][:, :, P:HALF])
+        round_q(nc.vector.tensor_copy, last_grouped[:, HALF:K, :], raw[LAST][:, :, HALF:K])
+        late = [(LAST, n) for n in range(2, BANDS)]
+        quantize_q(last_grouped[:, HALF:K, :], late, landing, LAST * RAW_BYTES + STAGE_BYTES + 5 * P)
 
         def stationary(i, e, b):
             cols = slice(e * K + b * P, e * K + (b + 1) * P)
@@ -237,8 +241,8 @@ def tile_moe_qkb_kernel(
 
         for b in range(BANDS):
             if b == 1:
-                rest = [(LAST, n) for n in range(1, BANDS)]
-                quantize_q(last_grouped[:, P:K, :], rest, v_pool, V_BAND - (4 + 1) * P * len(rest))
+                rest = [(LAST, 1)]
+                quantize_q(last_grouped[:, P:HALF, :], rest, v_pool, V_BAND - (4 + 1) * P * len(rest))
             for u in range(QUADS):
                 number = (QUADS * max(b - 1, 0) + u) % BANKS
                 bank = psum.tile([P, K], F32, name="sums%d_%d" % (b, u), offset=number * BANK_BYTES)
@@ -266,21 +270,26 @@ def tile_moe_qkb_kernel(
             nc.sync.dma_start(out=out[b * P:(b + 1) * P, :], in_=total[:])
 
         halves = ((0, T // 2), (T // 2, T))
-        for b in (2, 3):
-            final = b == BANDS - 1
-            picks = [token_tile(b, i) for i in range(2)]
-            for i in range(2):
-                for first, last in halves if final else ((0, T),):
-                    nc.scalar.activation(picks[i][:, first:last], picked(b, i, first, last), COPY)
-            if final:
-                total = token_tile(b, 2)
-            else:
-                total = v_pool.tile([P, T], F32, name="tokens2_sum", offset=BANDS * V_BAND - PICK_BYTES)
-            for first, last in halves:
-                nc.vector.tensor_tensor(total[:, first:last], picked(b, 2, first, last), picks[0][:, first:last], ADD)
-            for first, last in halves:
-                nc.vector.tensor_tensor(total[:, first:last], total[:, first:last], picks[1][:, first:last], ADD)
-                if final:
-                    nc.sync.dma_start(out=out[b * P:(b + 1) * P, first:last], in_=total[:, first:last])
-            if not final:
-                nc.sync.dma_start(out=out[b * P:(b + 1) * P, :], in_=total[:])
+        picks = [token_tile(2, i) for i in range(2)]
+        for i in range(2):
+            nc.scalar.activation(picks[i][:], picked(2, i), COPY)
+        total = v_pool.tile([P, T], F32, name="tokens2_sum", offset=BANDS * V_BAND - PICK_BYTES)
+        for first, last in halves:
+            nc.vector.tensor_tensor(total[:, first:last], picked(2, 2, first, last), picks[0][:, first:last], ADD)
+        for first, last in halves:
+            nc.vector.tensor_tensor(total[:, first:last], total[:, first:last], picks[1][:, first:last], ADD)
+        nc.sync.dma_start(out=out[2 * P:3 * P, :], in_=total[:])
+
+        cut = T - T // 4
+        picks = [token_tile(3, i) for i in range(3)]
+        for first, last in reversed(halves):
+            nc.scalar.activation(picks[0][:, first:last], picked(3, 0, first, last), COPY)
+        for first, last in ((0, T // 2), (T // 2, cut)):
+            nc.scalar.activation(picks[1][:, first:last], picked(3, 1, first, last), COPY)
+        for first, last in reversed(halves):
+            nc.vector.tensor_tensor(picks[2][:, first:last], picked(3, 2, first, last), picks[0][:, first:last], ADD)
+        nc.vector.tensor_tensor(picks[1][:, cut:T], picked(3, 1, cut, T), picks[2][:, cut:T], ADD)
+        nc.vector.tensor_tensor(picks[1][:, 0:T // 2], picks[1][:, 0:T // 2], picks[2][:, 0:T // 2], ADD)
+        nc.sync.dma_start(out=out[3 * P:4 * P, 0:T // 2], in_=picks[1][:, 0:T // 2])
+        nc.vector.tensor_tensor(picks[1][:, T // 2:cut], picks[1][:, T // 2:cut], picks[2][:, T // 2:cut], ADD)
+        nc.sync.dma_start(out=out[3 * P:4 * P, T // 2:T], in_=picks[1][:, T // 2:T])

@@ -73,13 +73,12 @@ def tile_moe_qkb_kernel(
         identity = keep.tile([P, P], F32, name="identity")
         dx = [keep.tile([P, S], F32, name="dx%d" % b) for b in range(BANDS)]
 
-        nc.vector.memset(d_words[DQ][:, T:WINDOW], 0)
         make_identity(nc, identity[:])
         for i in range(3):
             nc.gpsimd.memset(d_scales[i][:].bitcast(I32), 0)
-        for i in (DK, DV):
-            nc.gpsimd.memset(d_words[i][:, T:WINDOW], 0)
-        nc.gpsimd.memset(kv_plane[:].bitcast(I32), 0)
+        nc.vector.memset(kv_plane[:].bitcast(I32), 0)
+        for i in range(3):
+            nc.vector.memset(d_words[i][:, T:WINDOW], 0)
 
         def load_d_words(i):
             src = (dq_words, dk_words, dv_words)[i]

@@ -208,10 +208,10 @@ def tile_moe_qkb_kernel(
             pieces = [(e, b) for e in range(first, last) for b in range(BANDS)]
             quantize_q(grouped[:], pieces, landing, first * RAW_BYTES + (last - first) * STAGE_BYTES)
         last_grouped = landing.tile([P, K, 4], BF16, name="grouped_last", align_bytes=64, offset=LAST * RAW_BYTES)
+        round_q(nc.vector.tensor_copy, last_grouped[:, HALF:K, :], raw[LAST][:, :, HALF:K])
         round_q(nc.scalar.copy, last_grouped[:, 0:P, :], raw[LAST][:, :, 0:P])
         quantize_q(last_grouped[:, 0:P, :], [(LAST, 0)], landing, LAST * RAW_BYTES + STAGE_BYTES)
         round_q(nc.scalar.copy, last_grouped[:, P:HALF, :], raw[LAST][:, :, P:HALF])
-        round_q(nc.vector.tensor_copy, last_grouped[:, HALF:K, :], raw[LAST][:, :, HALF:K])
         late = [(LAST, n) for n in range(2, BANDS)]
         quantize_q(last_grouped[:, HALF:K, :], late, landing, LAST * RAW_BYTES + STAGE_BYTES + 5 * P)
 
@@ -225,7 +225,7 @@ def tile_moe_qkb_kernel(
 
         def multiply(bank, b, u):
             experts = range(QUAD * u, QUAD * (u + 1))
-            late = [(DQ, LAST)] if LAST in experts and b < 2 else []
+            late = [(DQ, LAST)] if LAST in experts else []
             order = [(DQ, e) for e in experts if (DQ, e) not in late] + [(DK, e) for e in experts]
             order = order + late + [(DV, e) for e in experts]
             for i, e in order:

from contextlib import ExitStack

import concourse.mybir as mybir
from concourse.masks import make_identity

F32 = mybir.dt.float32
BF16 = mybir.dt.bfloat16
I32 = mybir.dt.int32
U32 = mybir.dt.uint32
U16 = mybir.dt.uint16
U8 = mybir.dt.uint8
FP8X4 = mybir.dt.float8_e4m3fn_x4
FP4X4 = mybir.dt.float4_e2m1fn_x4
ADD = mybir.AluOpType.add
MULT = mybir.AluOpType.mult
COPY = mybir.ActivationFunctionType.Copy

P = 128
T = 512
E = 12
C = 128
S = E * C
K = 512
BANDS = K // P
HALF = K // 2
QUAD = 4
QUADS = E // QUAD
LAST = E - 1
DQ, DK, DV = 0, 1, 2

SPAN = E // 2
LISTED = SPAN * C
WINDOW = 2 * T
V_ROW = 4
GATE_RUN = S // P
LINE = 4

BY_QUAD = tuple((first, first + QUAD) for first in range(0, E, QUAD))
V_CUTS = (BY_QUAD, ((0, E),), BY_QUAD, ((0, E - QUAD), (E - QUAD, E)))
Q_GROUPS = tuple((first, first + 2) for first in range(0, E - 2, 2)) + ((E - 2, E - 1),)
SMALL_RUN = 2
POS_BEHIND = {0: (0,), 1: (1, 2)}

RAW_BYTES = 4 * K * 4
STAGE_BYTES = 4 * K * 2
LAG = 2
V_BAND = E * P * 4
PICK_BYTES = 4 * T
BANK_BYTES = 2048
BANKS = 8
SPREAD_BANK = 5
FLOPS = 2 * 3 * 512 * K * S


def tile_moe_qkb_kernel(
    tc, dq_words, dq_scales, dk_words, dk_scales, dv_words, dv_scales, wq, wk_words, wk_scales,
    wv_words, wv_scales, gate, offs, pos1, pos2, pos3, out,
):
    nc = tc.nc
    with ExitStack() as ctx:
        keep = ctx.enter_context(tc.tile_pool(name="keep", bufs=1))
        landing = ctx.enter_context(tc.tile_pool(name="landing", bufs=1))
        v_pool = ctx.enter_context(tc.tile_pool(name="v_pool", bufs=1))
        psum = ctx.enter_context(tc.psum_pool(name="psum", bufs=1))

        offs_sb = keep.tile([P, S // 16], U16, name="offs_sb")
        pos_sb = [keep.tile([P, T // 16], U16, name="pos_sb%d" % i) for i in range(3)]
        d_words = [keep.tile([P, WINDOW], I32, name="d_words%d" % i, align_bytes=64) for i in range(3)]
        d_scales = [keep.tile([P, WINDOW], U8, name="d_scales%d" % i, align_bytes=64) for i in range(3)]
        kv_plane = keep.tile([P, E * K], U8, name="kv_plane", align_bytes=64)
        gate_cols = keep.tile([P, GATE_RUN], F32, name="gate_cols")
        gate_wide = keep.tile([P, S], F32, name="gate_wide")
        identity = keep.tile([P, P], F32, name="identity")
        dx = [keep.tile([P, S], F32, name="dx%d" % b) for b in range(BANDS)]

        make_identity(nc, identity[:])
        for i in range(3):
            nc.gpsimd.memset(d_scales[i][:].bitcast(I32), 0)
        nc.vector.memset(kv_plane[:].bitcast(I32), 0)
        for i in range(3):
            nc.vector.memset(d_words[i][:, T:WINDOW], 0)

        def load_d_words(i):
            src = (dq_words, dk_words, dv_words)[i]
            nc.sync.dma_start(out=d_words[i][:, 0:T], in_=src[0].rearrange("p t d -> p (t d)").bitcast(I32))

        def load_d_scales(j):
            i, r = divmod(j, 4)
            nc.sync.dma_start(
                out=d_scales[i][r:P:32, 0:T].bitcast(I32),
                in_=(dq_scales, dk_scales, dv_scales)[i].rearrange("s (q r) t -> r (s q) t", r=4)[r].bitcast(I32),
            )

        def load_kv_scales(j):
            which, r = divmod(j, 4)
            nc.gpsimd.dma_start(
                out=kv_plane[which * V_ROW + r:P:32, :].bitcast(I32).rearrange("q (e c) -> q e c", e=E),
                in_=(wk_scales, wv_scales)[which].rearrange("e s (q r) c -> r q (e s) c", r=4)[r].bitcast(I32),
            )

        def load_pos(i):
            nc.sync.dma_start(pos_sb[i][:], (pos1, pos2, pos3)[i])

        raw = {}

        def load_q(e):
            raw[e] = landing.tile([P, 4, K], F32, name="raw%d" % e, align_bytes=64, offset=(e + LAG) * RAW_BYTES)
            nc.sync.dma_start(out=raw[e][:], in_=wq[e].rearrange("(p j) c -> p j c", j=4))

        k_codes = {}
        v_codes = {}

        def load_k(half):
            k_tile = keep.tile([P, E * HALF * 2], U8, name="k_codes%d" % half, align_bytes=64)
            nc.sync.dma_start(
                out=k_tile[:].bitcast(I32).rearrange("p (e c) -> p e c", e=E),
                in_=wk_words.rearrange("e s p c -> p (e s) c").bitcast(I32)[:, :, half * HALF // 2:(half + 1) * HALF // 2],
            )
            for e in range(E):
                for y in range(2):
                    at = e * HALF + y * P
                    k_codes[e, 2 * half + y] = k_tile[:, 2 * at:2 * (at + P)]

        def load_v(b, first, last):
            n = last - first
            v_tile = v_pool.tile(
                [P, n * P * 4], U8, name="v_codes%d_%d" % (b, first), align_bytes=64, offset=b * V_BAND + first * P * 4,
            )
            nc.sync.dma_start(
                out=v_tile[:].bitcast(I32).rearrange("p (e c) -> p e c", e=n),
                in_=wv_words.rearrange("e s p c d -> p (e s) (c d)").bitcast(I32)[:, first:last, b * P:(b + 1) * P],
            )
            for e in range(first, last):
                v_codes[e, b] = v_tile[:, (e - first) * 4 * P:(e - first + 1) * 4 * P]

        for j in range(8):
            load_kv_scales(j)
        load_d_words(DQ)
        nc.sync.dma_start(offs_sb[:], offs)
        nc.sync.dma_start(out=gate_cols[:], in_=gate[0].rearrange("(p x) -> p x", x=GATE_RUN))
        load_q(0)
        load_d_words(DK)
        for e in range(1, E):
            if e == LAST:
                load_k(0)
            load_q(e)
            if e == 1:
                load_d_words(DV)
            for j in range(SMALL_RUN * (e - 1), min(SMALL_RUN * e, 12)):
                load_d_scales(j)
        for b in range(BANDS):
            if b == 2:
                load_k(1)
            for first, last in V_CUTS[b]:
                load_v(b, first, last)
            for i in POS_BEHIND.get(b, ()):
                load_pos(i)

        for y in range(GATE_RUN // LINE):
            spread = psum.tile([P, LINE, P], F32, name="spread%d" % y, offset=(SPREAD_BANK + y) * BANK_BYTES)
            for x in range(LINE):
                at = LINE * y + x
                nc.tensor.transpose(spread[:, x, :], gate_cols[:, at:at + 1].to_broadcast([P, P]), identity[:])
            nc.scalar.copy(
                gate_wide[:].rearrange("q (p x) -> q p x", x=GATE_RUN)[:, :, LINE * y:LINE * (y + 1)],
                spread[:].rearrange("q x p -> q p x"),
            )

        g_words = {}
        g_scales = {}
        for h in range(E // SPAN):
            listed = offs_sb[:, h * LISTED // 16:(h + 1) * LISTED // 16]
            for i in (DQ, DK, DV):
                g_words[i, h] = keep.tile([P, LISTED], U32, name="g_words%d_%d" % (i, h), align_bytes=64)
                nc.vector.tensor_copy(g_words[i, h][:], d_words[i][:].bitcast(U32).indirect(listed))
            for i in (DQ, DK, DV):
                g_scales[i, h] = keep.tile([P, LISTED], U8, name="g_scales%d_%d" % (i, h), align_bytes=64)
                nc.vector.tensor_copy(g_scales[i, h][:], d_scales[i][:].indirect(listed))

        q_codes = {}
        q_plane = {}

        def round_q(copy, grouped, rows):
            copy(grouped.rearrange("p (c i) j -> p c j i", i=4), rows.rearrange("p j (c i) -> p c j i", i=4))

        def quantize_q(grouped, pieces, pool, place):
            width = P * len(pieces)
            name = "%d_%d" % pieces[0]
            codes = pool.tile([P, width], U32, name="q_codes" + name, align_bytes=64, offset=place)
            plane = pool.tile([P, width], U8, name="q_plane" + name, align_bytes=64, offset=place + 4 * width)
            nc.vector.quantize_mx(
                out=codes[:].bitcast(FP8X4), scales=plane[:], in_=grouped.rearrange("p c j -> p (c j)"),
            )
            for n, piece in enumerate(pieces):
                q_codes[piece] = codes[:, n * P:(n + 1) * P]
                q_plane[piece] = plane[:, n * P:(n + 1) * P]

        for first, last in Q_GROUPS:
            grouped = landing.tile(
                [P, (last - first) * K, 4], BF16, name="grouped%d" % first, align_bytes=64, offset=first * RAW_BYTES,
            )
            for e in range(first, last):
                if e == LAST - 1:
                    round_q(nc.scalar.copy, grouped[:, 0:HALF, :], raw[e][:, :, 0:HALF])
                    round_q(nc.vector.tensor_copy, grouped[:, HALF:K, :], raw[e][:, :, HALF:K])
                else:
                    round_q(nc.scalar.copy, grouped[:, (e - first) * K:(e - first + 1) * K, :], raw[e][:])
            pieces = [(e, b) for e in range(first, last) for b in range(BANDS)]
            quantize_q(grouped[:], pieces, landing, first * RAW_BYTES + (last - first) * STAGE_BYTES)
        last_grouped = landing.tile([P, K, 4], BF16, name="grouped_last", align_bytes=64, offset=LAST * RAW_BYTES)
        round_q(nc.vector.tensor_copy, last_grouped[:, HALF:K, :], raw[LAST][:, :, HALF:K])
        round_q(nc.scalar.copy, last_grouped[:, 0:P, :], raw[LAST][:, :, 0:P])
        quantize_q(last_grouped[:, 0:P, :], [(LAST, 0)], landing, LAST * RAW_BYTES + STAGE_BYTES)
        round_q(nc.scalar.copy, last_grouped[:, P:HALF, :], raw[LAST][:, :, P:HALF])
        late = [(LAST, n) for n in range(2, BANDS)]
        quantize_q(last_grouped[:, HALF:K, :], late, landing, LAST * RAW_BYTES + STAGE_BYTES + 5 * P)

        def stationary(i, e, b):
            cols = slice(e * K + b * P, e * K + (b + 1) * P)
            if i == DQ:
                return q_codes[e, b].bitcast(FP8X4), q_plane[e, b]
            if i == DK:
                return k_codes[e, b].bitcast(FP4X4), kv_plane[:, cols]
            return v_codes[e, b].bitcast(FP8X4), kv_plane[V_ROW:P, cols]

        def multiply(bank, b, u):
            experts = range(QUAD * u, QUAD * (u + 1))
            late = [(DQ, LAST)] if LAST in experts else []
            order = [(DQ, e) for e in experts if (DQ, e) not in late] + [(DK, e) for e in experts]
            order = order + late + [(DV, e) for e in experts]
            for i, e in order:
                h, x = divmod(e, SPAN)
                slots = slice(x * C, (x + 1) * C)
                codes, plane = stationary(i, e, b)
                nc.tensor.matmul_mx(
                    out=bank[:, (e % QUAD) * C:(e % QUAD + 1) * C], lhsT=codes, lhsT_scale=plane,
                    rhs=g_words[i, h][:, slots].bitcast(FP8X4), rhs_scale=g_scales[i, h][:, slots],
                    start=(i, e) == order[0], stop=(i, e) == order[-1],
                )

        for b in range(BANDS):
            if b == 1:
                rest = [(LAST, 1)]
                quantize_q(last_grouped[:, P:HALF, :], rest, v_pool, V_BAND - (4 + 1) * P * len(rest))
            for u in range(QUADS):
                number = (QUADS * max(b - 1, 0) + u) % BANKS
                bank = psum.tile([P, K], F32, name="sums%d_%d" % (b, u), offset=number * BANK_BYTES)
                multiply(bank, b, u)
                cols = slice(u * QUAD * C, (u + 1) * QUAD * C)
                nc.vector.tensor_tensor(dx[b][:, cols], bank[:], gate_wide[:, cols], MULT)

        def token_tile(b, n):
            place, at = divmod(3 * b + n, RAW_BYTES // PICK_BYTES)
            return landing.tile([P, T], F32, name="tokens%d_%d" % (b, n), offset=2 * place * RAW_BYTES + at * PICK_BYTES)

        def picked(b, i, first=0, last=T):
            return dx[b][:].indirect(pos_sb[i][:, first // 16:last // 16])

        for b in (0, 1):
            picks = [token_tile(b, i) for i in range(3)]
            for i in range(3):
                if (b, i) == (1, 2):
                    nc.vector.tensor_copy(picks[i][:], picked(b, i))
                else:
                    nc.scalar.activation(picks[i][:], picked(b, i), COPY)
            total, sooner, later = picks if b == 0 else (picks[2], picks[0], picks[1])
            nc.gpsimd.tensor_tensor(total[:], total[:], sooner[:], ADD)
            nc.gpsimd.tensor_tensor(total[:], total[:], later[:], ADD)
            nc.sync.dma_start(out=out[b * P:(b + 1) * P, :], in_=total[:])

        halves = ((0, T // 2), (T // 2, T))
        picks = [token_tile(2, i) for i in range(2)]
        for i in range(2):
            nc.scalar.activation(picks[i][:], picked(2, i), COPY)
        total = v_pool.tile([P, T], F32, name="tokens2_sum", offset=BANDS * V_BAND - PICK_BYTES)
        for first, last in halves:
            nc.vector.tensor_tensor(total[:, first:last], picked(2, 2, first, last), picks[0][:, first:last], ADD)
        for first, last in halves:
            nc.vector.tensor_tensor(total[:, first:last], total[:, first:last], picks[1][:, first:last], ADD)
        nc.sync.dma_start(out=out[2 * P:3 * P, :], in_=total[:])

        cut = T - T // 4
        picks = [token_tile(3, i) for i in range(3)]
        for first, last in reversed(halves):
            nc.scalar.activation(picks[0][:, first:last], picked(3, 0, first, last), COPY)
        for first, last in ((0, T // 2), (T // 2, cut)):
            nc.scalar.activation(picks[1][:, first:last], picked(3, 1, first, last), COPY)
        for first, last in reversed(halves):
            nc.vector.tensor_tensor(picks[2][:, first:last], picked(3, 2, first, last), picks[0][:, first:last], ADD)
        nc.vector.tensor_tensor(picks[1][:, cut:T], picked(3, 1, cut, T), picks[2][:, cut:T], ADD)
        nc.vector.tensor_tensor(picks[1][:, 0:T // 2], picks[1][:, 0:T // 2], picks[2][:, 0:T // 2], ADD)
        nc.sync.dma_start(out=out[3 * P:4 * P, 0:T // 2], in_=picks[1][:, 0:T // 2])
        nc.vector.tensor_tensor(picks[1][:, T // 2:cut], picks[1][:, T // 2:cut], picks[2][:, T // 2:cut], ADD)
        nc.sync.dma_start(out=out[3 * P:4 * P, T // 2:T], in_=picks[1][:, T // 2:T])
